import numpy as np
import ml_dtypes


def mxq(x, axis, fmt="e4m3"):
    dtype, down = {"e4m3": (ml_dtypes.float8_e4m3fn, 7), "e5m2": (ml_dtypes.float8_e5m2, 14)}[fmt]
    v = np.moveaxis(np.asarray(x, np.float32).astype(ml_dtypes.bfloat16).astype(np.float64), axis, -1)
    blocks = v.reshape(v.shape[:-1] + (-1, 32))
    amax = np.abs(blocks).max(-1, keepdims=True)
    byte = np.maximum(np.where(amax > 0, np.frexp(amax)[1] - 1 + 127, 0) - down, 1)
    scale = np.exp2(byte - 127.0)
    codes = (blocks / scale).astype(np.float32).astype(dtype).astype(np.float64)
    return np.moveaxis((codes * scale).reshape(v.shape), -1, axis)


WIDE = False


def mx_kscale(k):
    if not WIDE:
        return np.ones(k)
    levels = np.array([10, -10, 5, -5, 0])
    if k % 512:
        return np.exp2(np.random.permutation(np.resize(levels, k // 32))).repeat(32)
    a = np.empty((k // 512, 16))
    for p in range(k // 512):
        a[p, :8] = np.random.permutation(np.resize(levels, 8))
        for g in range(8):
            far = levels[np.abs(levels - a[p, g]) >= 10]
            a[p, g + 8] = far[np.random.randint(len(far))]
    return np.exp2(a.ravel()).repeat(32)


def f64(x):
    return np.asarray(x).astype(np.float64)


def striped(idx):
    return np.tile(np.asarray(idx).reshape(-1, 16).T, (8, 1)).astype(np.uint16)


def unstriped(offs):
    return offs[:16].T.reshape(-1).astype(np.int64)


B, N, T, D, DV, NQ = 1, 512, 1024, 512, 256, 128
NEW = 128


def setup_inputs():
    n = np.random.standard_normal
    idx = np.random.permutation(T)[:B * N]
    s = mx_kscale(D)[:, None]
    u = np.ones(T)
    u[idx] = mx_kscale(B * N)
    r = np.random.uniform(0.5, 2.0, T)
    rk = np.random.uniform(0.5, 2.0, T)
    k = n((D, T)) / s / rk
    v = n((DV, T)) / (u * r)
    new = np.random.permutation(idx.reshape(B, N)[:, -NEW // B:].reshape(-1))
    return {
        "qT": (n((B, D, NQ)) * s * (0.60 / np.sqrt(D))).astype(np.float32),
        "kT": np.where(np.isin(np.arange(T), new)[None, :], n((D, T)), k).astype(np.float32),
        "vT": np.where(np.isin(np.arange(T), new)[None, :], n((DV, T)), v).astype(np.float32),
        "new_kT": k[:, new].astype(np.float32),
        "new_vT": v[:, new].astype(np.float32),
        "ks": np.tile(rk, (128, 1)).astype(np.float32),
        "vs": np.tile(u * r, (128, 1)).astype(np.float32),
        "offs": striped(idx),
        "slots": striped(new),
    }


def reference(qT, kT, vT, new_kT, new_vT, ks, vs, offs, slots):
    idx = unstriped(offs)
    k = f64(kT)
    k[:, unstriped(slots)] = f64(new_kT)
    v = f64(vT)
    v[:, unstriped(slots)] = f64(new_vT)
    pick = lambda x: x[:, idx].reshape(x.shape[0], B, N).transpose(1, 0, 2)
    q = f64(qT)
    score = mxq(q, 1, "e4m3").transpose(0, 2, 1) @ mxq(pick(k), 1, "e4m3")
    score = score * pick(f64(ks))[:, :1, :]
    m = score.max(-1, keepdims=True)
    p = np.exp(score - m)
    total = p.sum(-1, keepdims=True)
    w = p * pick(f64(vs))[:, :1, :]
    y = mxq(w, 2, "e4m3") @ mxq(pick(v).transpose(0, 2, 1), 1, "e4m3")
    y = y / total
    return y

@@ -1,0 +1,201 @@
+from contextlib import ExitStack
+
+import concourse.mybir as mybir
+from concourse.masks import make_identity
+
+F32 = mybir.dt.float32
+BF16 = mybir.dt.bfloat16
+U32 = mybir.dt.uint32
+U16 = mybir.dt.uint16
+U8 = mybir.dt.uint8
+FP8X4 = mybir.dt.float8_e4m3fn_x4
+ACT = mybir.ActivationFunctionType
+ALU = mybir.AluOpType
+AX = mybir.AxisListType
+
+P = 128
+PACK = 4
+T = 1024
+N = 512
+NQ = 128
+DV = 256
+NEW = 128
+HALF = N // 2
+FLOPS = 2 * NQ * N * 512 + 2 * NQ * N * DV
+
+
+def tile_attend_x_ks_append128_topk_kernel(tc, qT, kT, vT, new_kT, new_vT, ks, vs, offs, slots, out):
+    nc = tc.nc
+    with ExitStack() as ctx:
+        keep = ctx.enter_context(tc.tile_pool(name="keep", bufs=1))
+        psum = ctx.enter_context(tc.psum_pool(name="psum", bufs=1))
+
+        kview = kT.rearrange("(p t) n -> p t n", t=PACK)
+        newkview = new_kT.rearrange("(p t) n -> p t n", t=PACK)
+        newk23 = keep.tile([P, 2, NEW], F32, name="newk23")
+        newk01 = keep.tile([P, 2, NEW], F32, name="newk01")
+        newv = keep.tile([P, 2, NEW], F32, name="newv")
+        place = keep.tile([P, NEW // 16], U16, name="place")
+        idx = keep.tile([P, N // 16], U16, name="idx")
+        kp = []
+        vp = []
+        for t in range(PACK):
+            kp.append(keep.tile([P, T], F32, name="kpool%d" % t))
+        for b in range(2):
+            vp.append(keep.tile([P, T], F32, name="vpool%d" % b))
+        q_sb = keep.tile([P, PACK, NQ], F32, name="q_sb")
+        ks_sb = keep.tile([P, T], F32, name="ks_sb")
+        vs_sb = keep.tile([P, T], F32, name="vs_sb")
+        nc.sync.dma_start(newk23[:], newkview[:, 2:4, :])
+        nc.sync.dma_start(kp[2][:], kview[:, 2, :])
+        nc.sync.dma_start(place[:], slots)
+        nc.sync.dma_start(idx[:], offs)
+        nc.sync.dma_start(kp[3][:], kview[:, 3, :])
+        nc.sync.dma_start(q_sb[:], qT[0].rearrange("(p t) q -> p t q", t=PACK))
+        nc.sync.dma_start(newv[:], new_vT.rearrange("(b p) n -> p b n", b=2))
+        nc.sync.dma_start(vp[0][:], vT[0:P, :])
+        nc.sync.dma_start(ks_sb[:], ks)
+        nc.sync.dma_start(vp[1][:], vT[P : 2 * P, :])
+        nc.sync.dma_start(newk01[:], newkview[:, 0:2, :])
+        nc.sync.dma_start(kp[0][:], kview[:, 0, :])
+        nc.sync.dma_start(kp[1][:], kview[:, 1, :])
+        nc.sync.dma_start(vs_sb[:], vs)
+
+        ident = keep.tile([P, P], BF16, name="ident")
+        make_identity(nc, ident[:])
+        identf = keep.tile([P, P], F32, name="identf")
+        make_identity(nc, identf[:])
+        dummy = keep.tile([P, 1], F32, name="dummy")
+        nc.vector.memset(dummy[:], 0.0)
+        nc.scalar.activation(dummy[:], dummy[:], ACT.Exp)
+
+        kgrp = keep.tile([P, N, PACK], BF16, name="kgrp", tag="grp", align_bytes=64)
+        kcodes = keep.tile([P, N], U32, name="kcodes", align_bytes=64)
+        kscale = keep.tile([P, N], U8, name="kscale", align_bytes=64)
+        vgrp = keep.tile([P, DV, PACK], BF16, name="vgrp", align_bytes=64)
+        vscale = keep.tile([P, DV], U8, name="vscale", align_bytes=64)
+        qgrp = keep.tile([P, NQ, PACK], BF16, name="qgrp", align_bytes=64)
+        qcodes = keep.tile([P, NQ], U32, name="qcodes", align_bytes=64)
+        qscale = keep.tile([P, NQ], U8, name="qscale", align_bytes=64)
+        ksg = keep.tile([P, N], F32, name="ksg")
+
+        newk = [newk01[:, 0, :], newk01[:, 1, :], newk23[:, 0, :], newk23[:, 1, :]]
+
+        def write_key(t):
+            nc.vector.tensor_copy(kp[t][:].indirect(place[:]), newk[t])
+
+        def scalar_key(t):
+            kb = keep.tile([P, T], BF16, name="kb%d" % t)
+            nc.scalar.copy(kb[:], kp[t][:])
+            nc.scalar.activation(kgrp[:, :, t], kb[:].indirect(idx[:]), ACT.Copy)
+
+        write_key(2)
+        scalar_key(2)
+        write_key(3)
+        scalar_key(3)
+        nc.vector.tensor_copy(qgrp[:], q_sb[:].rearrange("p t q -> p q t"))
+        nc.vector.quantize_mx(out=qcodes[:].bitcast(FP8X4), scales=qscale[:], in_=qgrp[:].rearrange("p q t -> p (q t)"))
+        vb = []
+        vg = []
+        for b in range(2):
+            vb.append(keep.tile([P, T], BF16, name="vb%d" % b))
+            vg.append(keep.tile([P, N], BF16, name="vg%d" % b, align_bytes=64))
+
+        def write_value(b):
+            nc.vector.tensor_copy(vp[b][:].indirect(place[:]), newv[:, b, :])
+
+        def scalar_value(b):
+            nc.scalar.copy(vb[b][:], vp[b][:])
+            nc.scalar.activation(vg[b][:].rearrange("p (t s) -> p s t", t=PACK), vb[b][:].indirect(idx[:]), ACT.Copy)
+
+        write_value(0)
+        nc.vector.tensor_copy(ksg[:], ks_sb[:].indirect(idx[:]))
+        write_value(1)
+        write_key(0)
+        write_key(1)
+        nc.vector.tensor_copy(kgrp[:, :, 0], kp[0][:].indirect(idx[:]))
+        for h in range(2):
+            cols = slice(h * HALF, (h + 1) * HALF)
+            nc.vector.tensor_copy(kgrp[:, cols, 1], kp[1][:].indirect(idx[:, h * HALF // 16 : (h + 1) * HALF // 16]))
+        for b in range(2):
+            scalar_value(b)
+        a = keep.tile([P, PACK, P], F32, name="a")
+        low = keep.tile([P, 1], F32, name="low")
+        bias = keep.tile([P, 1], F32, name="bias")
+        sc = []
+        for h in range(2):
+            cols = slice(h * HALF, (h + 1) * HALF)
+            sc.append(psum.tile([P, HALF], F32, name="sc%d" % h, tag="scores%d" % h))
+            nc.vector.quantize_mx(out=kcodes[:, cols].bitcast(FP8X4), scales=kscale[:, cols], in_=kgrp[:, cols, :].rearrange("p n t -> p (n t)"))
+            nc.tensor.matmul_mx(
+                out=sc[h][:],
+                lhsT=qcodes[:].bitcast(FP8X4),
+                lhsT_scale=qscale[:],
+                rhs=kcodes[:, cols].bitcast(FP8X4),
+                rhs_scale=kscale[:, cols],
+                start=True,
+                stop=True,
+            )
+        vsg = keep.tile([P, N], F32, name="vsg", tag="grp", align_bytes=64)
+        vst = keep.tile([P, PACK], F32, name="vst")
+        nc.vector.tensor_copy(vsg[:], vs_sb[:].indirect(idx[:]))
+        vsps = psum.tile([P, PACK, P], F32, name="vsps")
+        for t in range(PACK):
+            nc.tensor.transpose(vsps[:, t, :], vsg[:].rearrange("p (s t) -> p t s", t=PACK)[:, t, :], identf[:])
+        nc.scalar.copy(vst[:], vsps[:, :, 0])
+        junk = keep.tile([P, PACK, HALF // PACK], F32, name="junk", align_bytes=64)
+        for h in range(2):
+            cols = slice(h * HALF, (h + 1) * HALF)
+            part = a[:, :, h * 64 : (h + 1) * 64]
+            nc.vector.scalar_tensor_tensor(
+                part.rearrange("q t s -> q s t"),
+                sc[h][:].rearrange("q (s t) -> q s t", t=PACK),
+                -1.0,
+                ksg[:, cols].rearrange("q (s t) -> q s t", t=PACK),
+                ALU.mult,
+                ALU.mult,
+            )
+            if h == 0:
+                nc.vector.tensor_reduce(low[:], part, AX.XY, ALU.min)
+            else:
+                nc.vector.tensor_scalar(junk[:], part, 1.0, low[:], ALU.mult, ALU.min, accum_out=bias[:])
+
+        p = keep.tile([P, PACK, P], F32, name="p")
+        total2 = keep.tile([P, 2], F32, name="total2")
+        pps = psum.tile([P, PACK, NQ], F32, name="pps")
+        for h in range(2):
+            ts = slice(2 * h, 2 * h + 2)
+            nc.scalar.activation(p[:, ts, :], a[:, ts, :], ACT.Exp, bias=bias[:], scale=-1.0, accum_out=total2[:, h : h + 1])
+
+        vps = psum.tile([P, 2, PACK, P], BF16, name="vps", tag="scores1")
+        for b in range(2):
+            for t in range(PACK):
+                nc.tensor.transpose(vps[:, b, t, :], vg[b][:, t * P : (t + 1) * P], ident[:])
+        nc.vector.tensor_copy(vgrp[:].rearrange("s (b e) t -> s b e t", b=2), vps[:].rearrange("s b t e -> s b e t"))
+        vcodes = keep.tile([P, DV], U32, name="vcodes", align_bytes=64)
+        nc.vector.quantize_mx(out=vcodes[:].bitcast(FP8X4), scales=vscale[:], in_=vgrp[:].rearrange("p e t -> p (e t)"))
+        for t in range(PACK):
+            nc.tensor.transpose(pps[:, t, :], p[:, t, :], identf[:])
+
+        wgrp = keep.tile([P, NQ, PACK], BF16, name="wgrp", align_bytes=64)
+        nc.vector.tensor_tensor(wgrp[:], pps[:].rearrange("s t q -> s q t"), vst[:].unsqueeze(1).to_broadcast([P, NQ, PACK]), ALU.mult)
+        wcodes = keep.tile([P, NQ], U32, name="wcodes", align_bytes=64)
+        wscale = keep.tile([P, NQ], U8, name="wscale", align_bytes=64)
+        nc.vector.quantize_mx(out=wcodes[:].bitcast(FP8X4), scales=wscale[:], in_=wgrp[:].rearrange("p q t -> p (q t)"))
+        total = keep.tile([P, 1], F32, name="total")
+        nc.vector.tensor_tensor(total[:], total2[:, 0:1], total2[:, 1:2], ALU.add)
+        recip = keep.tile([P, 1], F32, name="recip")
+        nc.vector.reciprocal(recip[:], total[:])
+        ps_out = psum.tile([P, DV], F32, name="ps_out")
+        nc.tensor.matmul_mx(
+            out=ps_out[:],
+            lhsT=wcodes[:].bitcast(FP8X4),
+            lhsT_scale=wscale[:],
+            rhs=vcodes[:].bitcast(FP8X4),
+            rhs_scale=vscale[:],
+            start=True,
+            stop=True,
+        )
+        o_sb = keep.tile([P, DV], F32, name="o_sb")
+        nc.vector.tensor_scalar(o_sb[:], ps_out[:], recip[:], None, ALU.mult)
+        nc.sync.dma_start(out[0], o_sb[:])

@@ -20,7 +20,6 @@ N = 512
 NQ = 128
 DV = 256
 NEW = 128
-HALF = N // 2
 FLOPS = 2 * NQ * N * 512 + 2 * NQ * N * DV
 
 
@@ -32,160 +31,125 @@ def tile_attend_x_ks_append128_topk_kernel(tc, qT, kT, vT, new_kT, new_vT, ks, v
 
         kview = kT.rearrange("(p t) n -> p t n", t=PACK)
         newkview = new_kT.rearrange("(p t) n -> p t n", t=PACK)
-        newk23 = keep.tile([P, 2, NEW], F32, name="newk23")
-        newk01 = keep.tile([P, 2, NEW], F32, name="newk01")
+        newk23 = keep.tile([P, 2, NEW], F32, name="newk23", tag="newk23", align_bytes=64)
+        newk01 = keep.tile([P, 2, NEW], F32, name="newk01", tag="grp", align_bytes=64)
         newv = keep.tile([P, 2, NEW], F32, name="newv")
         place = keep.tile([P, NEW // 16], U16, name="place")
         idx = keep.tile([P, N // 16], U16, name="idx")
-        kp = []
-        vp = []
-        for t in range(PACK):
-            kp.append(keep.tile([P, T], F32, name="kpool%d" % t))
-        for b in range(2):
-            vp.append(keep.tile([P, T], F32, name="vpool%d" % b))
+        kp = [keep.tile([P, T], F32, name="kpool%d" % t, tag="kpool%d" % t) for t in range(PACK)]
+        vp = [keep.tile([P, T], F32, name="vpool%d" % b) for b in range(2)]
         q_sb = keep.tile([P, PACK, NQ], F32, name="q_sb")
         ks_sb = keep.tile([P, T], F32, name="ks_sb")
         vs_sb = keep.tile([P, T], F32, name="vs_sb")
+        nc.vector.memset(vs_sb[0 : P - 1, :], 0.0)
+        nc.sync.dma_start(vs_sb[P - 1 : P, :], vs[0:1, :])
+        nc.sync.dma_start(idx[:], offs)
+        nc.sync.dma_start(kp[0][:], kview[:, 0, :])
+        nc.sync.dma_start(place[:], slots)
+        nc.sync.dma_start(newk01[:], newkview[:, 0:2, :])
+        nc.sync.dma_start(kp[1][:], kview[:, 1, :])
         nc.sync.dma_start(newk23[:], newkview[:, 2:4, :])
         nc.sync.dma_start(kp[2][:], kview[:, 2, :])
-        nc.sync.dma_start(place[:], slots)
-        nc.sync.dma_start(idx[:], offs)
-        nc.sync.dma_start(kp[3][:], kview[:, 3, :])
         nc.sync.dma_start(q_sb[:], qT[0].rearrange("(p t) q -> p t q", t=PACK))
         nc.sync.dma_start(newv[:], new_vT.rearrange("(b p) n -> p b n", b=2))
         nc.sync.dma_start(vp[0][:], vT[0:P, :])
-        nc.sync.dma_start(ks_sb[:], ks)
+        nc.sync.dma_start(kp[3][:], kview[:, 3, :])
         nc.sync.dma_start(vp[1][:], vT[P : 2 * P, :])
-        nc.sync.dma_start(newk01[:], newkview[:, 0:2, :])
-        nc.sync.dma_start(kp[0][:], kview[:, 0, :])
-        nc.sync.dma_start(kp[1][:], kview[:, 1, :])
-        nc.sync.dma_start(vs_sb[:], vs)
+        nc.sync.dma_start(ks_sb[:], ks)
 
-        ident = keep.tile([P, P], BF16, name="ident")
-        make_identity(nc, ident[:])
         identf = keep.tile([P, P], F32, name="identf")
         make_identity(nc, identf[:])
         dummy = keep.tile([P, 1], F32, name="dummy")
         nc.vector.memset(dummy[:], 0.0)
         nc.scalar.activation(dummy[:], dummy[:], ACT.Exp)
 
-        kgrp = keep.tile([P, N, PACK], BF16, name="kgrp", tag="grp", align_bytes=64)
-        kcodes = keep.tile([P, N], U32, name="kcodes", align_bytes=64)
-        kscale = keep.tile([P, N], U8, name="kscale", align_bytes=64)
-        vgrp = keep.tile([P, DV, PACK], BF16, name="vgrp", align_bytes=64)
-        vscale = keep.tile([P, DV], U8, name="vscale", align_bytes=64)
-        qgrp = keep.tile([P, NQ, PACK], BF16, name="qgrp", align_bytes=64)
-        qcodes = keep.tile([P, NQ], U32, name="qcodes", align_bytes=64)
-        qscale = keep.tile([P, NQ], U8, name="qscale", align_bytes=64)
-        ksg = keep.tile([P, N], F32, name="ksg")
-
-        newk = [newk01[:, 0, :], newk01[:, 1, :], newk23[:, 0, :], newk23[:, 1, :]]
-
-        def write_key(t):
-            nc.vector.tensor_copy(kp[t][:].indirect(place[:]), newk[t])
-
-        def scalar_key(t):
-            kb = keep.tile([P, T], BF16, name="kb%d" % t)
-            nc.scalar.copy(kb[:], kp[t][:])
-            nc.scalar.activation(kgrp[:, :, t], kb[:].indirect(idx[:]), ACT.Copy)
-
-        write_key(2)
-        scalar_key(2)
-        write_key(3)
-        scalar_key(3)
-        nc.vector.tensor_copy(qgrp[:], q_sb[:].rearrange("p t q -> p q t"))
-        nc.vector.quantize_mx(out=qcodes[:].bitcast(FP8X4), scales=qscale[:], in_=qgrp[:].rearrange("p q t -> p (q t)"))
-        vb = []
-        vg = []
-        for b in range(2):
-            vb.append(keep.tile([P, T], BF16, name="vb%d" % b))
-            vg.append(keep.tile([P, N], BF16, name="vg%d" % b, align_bytes=64))
-
-        def write_value(b):
-            nc.vector.tensor_copy(vp[b][:].indirect(place[:]), newv[:, b, :])
-
-        def scalar_value(b):
-            nc.scalar.copy(vb[b][:], vp[b][:])
-            nc.scalar.activation(vg[b][:].rearrange("p (t s) -> p s t", t=PACK), vb[b][:].indirect(idx[:]), ACT.Copy)
-
-        write_value(0)
-        nc.vector.tensor_copy(ksg[:], ks_sb[:].indirect(idx[:]))
-        write_value(1)
-        write_key(0)
-        write_key(1)
-        nc.vector.tensor_copy(kgrp[:, :, 0], kp[0][:].indirect(idx[:]))
-        for h in range(2):
-            cols = slice(h * HALF, (h + 1) * HALF)
-            nc.vector.tensor_copy(kgrp[:, cols, 1], kp[1][:].indirect(idx[:, h * HALF // 16 : (h + 1) * HALF // 16]))
-        for b in range(2):
-            scalar_value(b)
-        a = keep.tile([P, PACK, P], F32, name="a")
-        low = keep.tile([P, 1], F32, name="low")
-        bias = keep.tile([P, 1], F32, name="bias")
-        sc = []
-        for h in range(2):
-            cols = slice(h * HALF, (h + 1) * HALF)
-            sc.append(psum.tile([P, HALF], F32, name="sc%d" % h, tag="scores%d" % h))
-            nc.vector.quantize_mx(out=kcodes[:, cols].bitcast(FP8X4), scales=kscale[:, cols], in_=kgrp[:, cols, :].rearrange("p n t -> p (n t)"))
-            nc.tensor.matmul_mx(
-                out=sc[h][:],
-                lhsT=qcodes[:].bitcast(FP8X4),
-                lhsT_scale=qscale[:],
-                rhs=kcodes[:, cols].bitcast(FP8X4),
-                rhs_scale=kscale[:, cols],
-                start=True,
-                stop=True,
-            )
-        vsg = keep.tile([P, N], F32, name="vsg", tag="grp", align_bytes=64)
-        vst = keep.tile([P, PACK], F32, name="vst")
+        vsg = keep.tile([P, N], F32, name="vsg")
         nc.vector.tensor_copy(vsg[:], vs_sb[:].indirect(idx[:]))
         vsps = psum.tile([P, PACK, P], F32, name="vsps")
         for t in range(PACK):
-            nc.tensor.transpose(vsps[:, t, :], vsg[:].rearrange("p (s t) -> p t s", t=PACK)[:, t, :], identf[:])
-        nc.scalar.copy(vst[:], vsps[:, :, 0])
-        junk = keep.tile([P, PACK, HALF // PACK], F32, name="junk", align_bytes=64)
-        for h in range(2):
-            cols = slice(h * HALF, (h + 1) * HALF)
-            part = a[:, :, h * 64 : (h + 1) * 64]
-            nc.vector.scalar_tensor_tensor(
-                part.rearrange("q t s -> q s t"),
-                sc[h][:].rearrange("q (s t) -> q s t", t=PACK),
-                -1.0,
-                ksg[:, cols].rearrange("q (s t) -> q s t", t=PACK),
-                ALU.mult,
-                ALU.mult,
-            )
-            if h == 0:
-                nc.vector.tensor_reduce(low[:], part, AX.XY, ALU.min)
-            else:
-                nc.vector.tensor_scalar(junk[:], part, 1.0, low[:], ALU.mult, ALU.min, accum_out=bias[:])
+            nc.tensor.transpose(vsps[:, t, :], vsg[:, t:N:PACK], identf[:])
 
-        p = keep.tile([P, PACK, P], F32, name="p")
-        total2 = keep.tile([P, 2], F32, name="total2")
-        pps = psum.tile([P, PACK, NQ], F32, name="pps")
-        for h in range(2):
-            ts = slice(2 * h, 2 * h + 2)
-            nc.scalar.activation(p[:, ts, :], a[:, ts, :], ACT.Exp, bias=bias[:], scale=-1.0, accum_out=total2[:, h : h + 1])
+        kcodes = keep.tile([P, N], U32, name="kcodes", align_bytes=64)
+        kscale = keep.tile([P, N], U8, name="kscale", align_bytes=64)
+        qscale = keep.tile([P, NQ], U8, name="qscale", align_bytes=64)
+        kb = [keep.tile([P, T], BF16, name="kb%d" % t, tag="stage%d" % t, align_bytes=64) for t in range(2)]
+        vg = [keep.tile([P, N], BF16, name="vg%d" % b) for b in range(2)]
+        vps = psum.tile([P, 2, 2, P], F32, name="vps")
 
-        vps = psum.tile([P, 2, PACK, P], BF16, name="vps", tag="scores1")
-        for b in range(2):
-            for t in range(PACK):
-                nc.tensor.transpose(vps[:, b, t, :], vg[b][:, t * P : (t + 1) * P], ident[:])
-        nc.vector.tensor_copy(vgrp[:].rearrange("s (b e) t -> s b e t", b=2), vps[:].rearrange("s b t e -> s b e t"))
+        def cast_values(b):
+            vb = keep.tile([P, T], BF16, name="vb%d" % b, tag="stage0", align_bytes=64)
+            nc.vector.tensor_copy(vp[b][:].indirect(place[:]), newv[:, b, :])
+            nc.scalar.copy(vb[:], vp[b][:])
+            return vb
+
+        def gather_values(b, vb):
+            nc.scalar.activation(vg[b][:], vb[:].indirect(idx[:]), ACT.Copy)
+            words = vg[b][:].bitcast(F32)
+            for u in range(2):
+                nc.tensor.transpose(vps[:, b, u, :], words[:, u : N // 2 : 2], identf[:])
+
+        for t in range(2):
+            nc.vector.tensor_copy(kp[t][:].indirect(place[:]), newk01[:, t, :])
+            nc.scalar.copy(kb[t][:], kp[t][:])
+        kgrp = keep.tile([P, N, PACK], BF16, name="kgrp", tag="grp", align_bytes=64)
+        for t in range(2):
+            nc.scalar.activation(kgrp[:, :, t], kb[t][:].indirect(idx[:]), ACT.Copy)
+        vst = keep.tile([P, PACK], F32, name="vst", tag="kpool1")
+        nc.scalar.copy(vst[:], vsps[:, :, P - 1])
+        nc.vector.tensor_copy(kp[2][:].indirect(place[:]), newk23[:, 0, :])
+        nc.vector.tensor_copy(kgrp[:, :, 2], kp[2][:].indirect(idx[:]))
+        vb0 = cast_values(0)
+        qgrp = keep.tile([P, NQ, PACK], BF16, name="qgrp", tag="stage1", align_bytes=64)
+        nc.scalar.copy(qgrp[:], q_sb[:].rearrange("p t q -> p q t"))
+        gather_values(0, vb0)
+        nc.vector.tensor_copy(kp[3][:].indirect(place[:]), newk23[:, 1, :])
+        nc.vector.tensor_copy(kgrp[:, :, 3], kp[3][:].indirect(idx[:]))
+        qcodes = keep.tile([P, NQ], U32, name="qcodes", tag="newk23", align_bytes=64)
+        nc.vector.quantize_mx(out=qcodes[:].bitcast(FP8X4), scales=qscale[:], in_=qgrp[:].rearrange("p q t -> p (q t)"))
+        nc.vector.quantize_mx(out=kcodes[:].bitcast(FP8X4), scales=kscale[:], in_=kgrp[:].rearrange("p n t -> p (n t)"))
+        scores = psum.tile([P, N], F32, name="scores")
+        nc.tensor.matmul_mx(
+            out=scores[:],
+            lhsT=qcodes[:].bitcast(FP8X4),
+            lhsT_scale=qscale[:],
+            rhs=kcodes[:].bitcast(FP8X4),
+            rhs_scale=kscale[:],
+            start=True,
+            stop=True,
+        )
+        gather_values(1, cast_values(1))
+        ksg = keep.tile([P, N], F32, name="ksg", tag="grp", align_bytes=64)
+        nc.vector.tensor_copy(ksg[:], ks_sb[:].indirect(idx[:]))
+
+        a = keep.tile([P, PACK, P], F32, name="a")
+        bias = keep.tile([P, 1], F32, name="bias")
+        nc.vector.tensor_tensor(
+            a[:].rearrange("q t s -> q s t"),
+            scores[:].rearrange("q (s t) -> q s t", t=PACK),
+            ksg[:].rearrange("q (s t) -> q s t", t=PACK),
+            ALU.mult,
+        )
+        nc.vector.tensor_reduce(bias[:], a[:], AX.XY, ALU.max, negate=True)
+        p = keep.tile([P, PACK, P], F32, name="p", tag="stage0", align_bytes=64)
+        total = keep.tile([P, 1], F32, name="total")
+        nc.scalar.activation(p[:], a[:], ACT.Exp, bias=bias[:], scale=1.0, accum_out=total[:])
+
+        vgrp = keep.tile([P, DV * PACK], BF16, name="vgrp", tag="grp", align_bytes=64)
+        nc.vector.tensor_copy(vgrp[:].bitcast(F32).rearrange("s (b e u) -> s b e u", b=2, u=2), vps[:].rearrange("s b u e -> s b e u"))
         vcodes = keep.tile([P, DV], U32, name="vcodes", align_bytes=64)
-        nc.vector.quantize_mx(out=vcodes[:].bitcast(FP8X4), scales=vscale[:], in_=vgrp[:].rearrange("p e t -> p (e t)"))
+        vscale = keep.tile([P, DV], U8, name="vscale", align_bytes=64)
+        nc.vector.quantize_mx(out=vcodes[:].bitcast(FP8X4), scales=vscale[:], in_=vgrp[:])
+        recip = keep.tile([P, 1], F32, name="recip")
+        nc.vector.reciprocal(recip[:], total[:])
+
+        pps = psum.tile([P, PACK, NQ], F32, name="pps")
         for t in range(PACK):
             nc.tensor.transpose(pps[:, t, :], p[:, t, :], identf[:])
-
         wgrp = keep.tile([P, NQ, PACK], BF16, name="wgrp", align_bytes=64)
         nc.vector.tensor_tensor(wgrp[:], pps[:].rearrange("s t q -> s q t"), vst[:].unsqueeze(1).to_broadcast([P, NQ, PACK]), ALU.mult)
         wcodes = keep.tile([P, NQ], U32, name="wcodes", align_bytes=64)
         wscale = keep.tile([P, NQ], U8, name="wscale", align_bytes=64)
         nc.vector.quantize_mx(out=wcodes[:].bitcast(FP8X4), scales=wscale[:], in_=wgrp[:].rearrange("p q t -> p (q t)"))
-        total = keep.tile([P, 1], F32, name="total")
-        nc.vector.tensor_tensor(total[:], total2[:, 0:1], total2[:, 1:2], ALU.add)
-        recip = keep.tile([P, 1], F32, name="recip")
-        nc.vector.reciprocal(recip[:], total[:])
         ps_out = psum.tile([P, DV], F32, name="ps_out")
         nc.tensor.matmul_mx(
             out=ps_out[:],

@@ -31,9 +31,9 @@ def tile_attend_x_ks_append128_topk_kernel(tc, qT, kT, vT, new_kT, new_vT, ks, v
 
         kview = kT.rearrange("(p t) n -> p t n", t=PACK)
         newkview = new_kT.rearrange("(p t) n -> p t n", t=PACK)
-        newk23 = keep.tile([P, 2, NEW], F32, name="newk23", tag="newk23", align_bytes=64)
+        newk23 = keep.tile([P, 2, NEW], F32, name="newk23")
         newk01 = keep.tile([P, 2, NEW], F32, name="newk01", tag="grp", align_bytes=64)
-        newv = keep.tile([P, 2, NEW], F32, name="newv")
+        newv = keep.tile([P, 2, NEW], F32, name="newv", tag="newv")
         place = keep.tile([P, NEW // 16], U16, name="place")
         idx = keep.tile([P, N // 16], U16, name="idx")
         kp = [keep.tile([P, T], F32, name="kpool%d" % t, tag="kpool%d" % t) for t in range(PACK)]
@@ -53,8 +53,8 @@ def tile_attend_x_ks_append128_topk_kernel(tc, qT, kT, vT, new_kT, new_vT, ks, v
         nc.sync.dma_start(q_sb[:], qT[0].rearrange("(p t) q -> p t q", t=PACK))
         nc.sync.dma_start(newv[:], new_vT.rearrange("(b p) n -> p b n", b=2))
         nc.sync.dma_start(vp[0][:], vT[0:P, :])
-        nc.sync.dma_start(kp[3][:], kview[:, 3, :])
         nc.sync.dma_start(vp[1][:], vT[P : 2 * P, :])
+        nc.sync.dma_start(kp[3][:], kview[:, 3, :])
         nc.sync.dma_start(ks_sb[:], ks)
 
         identf = keep.tile([P, P], F32, name="identf")
@@ -73,20 +73,17 @@ def tile_attend_x_ks_append128_topk_kernel(tc, qT, kT, vT, new_kT, new_vT, ks, v
         kscale = keep.tile([P, N], U8, name="kscale", align_bytes=64)
         qscale = keep.tile([P, NQ], U8, name="qscale", align_bytes=64)
         kb = [keep.tile([P, T], BF16, name="kb%d" % t, tag="stage%d" % t, align_bytes=64) for t in range(2)]
-        vg = [keep.tile([P, N], BF16, name="vg%d" % b) for b in range(2)]
-        vps = psum.tile([P, 2, 2, P], F32, name="vps")
 
         def cast_values(b):
-            vb = keep.tile([P, T], BF16, name="vb%d" % b, tag="stage0", align_bytes=64)
+            vb = keep.tile([P, T], BF16, name="vb%d" % b, tag="stage%d" % b, align_bytes=64)
             nc.vector.tensor_copy(vp[b][:].indirect(place[:]), newv[:, b, :])
             nc.scalar.copy(vb[:], vp[b][:])
             return vb
 
         def gather_values(b, vb):
-            nc.scalar.activation(vg[b][:], vb[:].indirect(idx[:]), ACT.Copy)
-            words = vg[b][:].bitcast(F32)
-            for u in range(2):
-                nc.tensor.transpose(vps[:, b, u, :], words[:, u : N // 2 : 2], identf[:])
+            vg = keep.tile([P, N], BF16, name="vg%d" % b, tag="newv" if b == 0 else "vg1")
+            nc.scalar.activation(vg[:], vb[:].indirect(idx[:]), ACT.Copy)
+            return vg
 
         for t in range(2):
             nc.vector.tensor_copy(kp[t][:].indirect(place[:]), newk01[:, t, :])
@@ -98,16 +95,16 @@ def tile_attend_x_ks_append128_topk_kernel(tc, qT, kT, vT, new_kT, new_vT, ks, v
         nc.scalar.copy(vst[:], vsps[:, :, P - 1])
         nc.vector.tensor_copy(kp[2][:].indirect(place[:]), newk23[:, 0, :])
         nc.vector.tensor_copy(kgrp[:, :, 2], kp[2][:].indirect(idx[:]))
-        vb0 = cast_values(0)
-        qgrp = keep.tile([P, NQ, PACK], BF16, name="qgrp", tag="stage1", align_bytes=64)
-        nc.scalar.copy(qgrp[:], q_sb[:].rearrange("p t q -> p q t"))
-        gather_values(0, vb0)
+        qgrp = keep.tile([P, NQ, PACK], BF16, name="qgrp", align_bytes=64)
+        nc.gpsimd.tensor_scalar(qgrp[:], q_sb[:].rearrange("p t q -> p q t"), 1.0, 0.0, ALU.mult, ALU.add)
+        qcodes = keep.tile([P, NQ], U32, name="qcodes", align_bytes=64)
+        nc.vector.quantize_mx(out=qcodes[:].bitcast(FP8X4), scales=qscale[:], in_=qgrp[:].rearrange("p q t -> p (q t)"))
+        vbs = [cast_values(b) for b in range(2)]
+        vgs = [gather_values(b, vbs[b]) for b in range(2)]
         nc.vector.tensor_copy(kp[3][:].indirect(place[:]), newk23[:, 1, :])
         nc.vector.tensor_copy(kgrp[:, :, 3], kp[3][:].indirect(idx[:]))
-        qcodes = keep.tile([P, NQ], U32, name="qcodes", tag="newk23", align_bytes=64)
-        nc.vector.quantize_mx(out=qcodes[:].bitcast(FP8X4), scales=qscale[:], in_=qgrp[:].rearrange("p q t -> p (q t)"))
         nc.vector.quantize_mx(out=kcodes[:].bitcast(FP8X4), scales=kscale[:], in_=kgrp[:].rearrange("p n t -> p (n t)"))
-        scores = psum.tile([P, N], F32, name="scores")
+        scores = psum.tile([P, N], F32, name="scores", tag="scores")
         nc.tensor.matmul_mx(
             out=scores[:],
             lhsT=qcodes[:].bitcast(FP8X4),
@@ -117,8 +114,7 @@ def tile_attend_x_ks_append128_topk_kernel(tc, qT, kT, vT, new_kT, new_vT, ks, v
             start=True,
             stop=True,
         )
-        gather_values(1, cast_values(1))
-        ksg = keep.tile([P, N], F32, name="ksg", tag="grp", align_bytes=64)
+        ksg = keep.tile([P, N], F32, name="ksg", tag="ksg", align_bytes=64)
         nc.vector.tensor_copy(ksg[:], ks_sb[:].indirect(idx[:]))
 
         a = keep.tile([P, PACK, P], F32, name="a")
@@ -130,15 +126,23 @@ def tile_attend_x_ks_append128_topk_kernel(tc, qT, kT, vT, new_kT, new_vT, ks, v
             ALU.mult,
         )
         nc.vector.tensor_reduce(bias[:], a[:], AX.XY, ALU.max, negate=True)
-        p = keep.tile([P, PACK, P], F32, name="p", tag="stage0", align_bytes=64)
-        total = keep.tile([P, 1], F32, name="total")
-        nc.scalar.activation(p[:], a[:], ACT.Exp, bias=bias[:], scale=1.0, accum_out=total[:])
+        p = keep.tile([P, PACK, P], F32, name="p", tag="stage1", align_bytes=64)
+        sums = keep.tile([P, 2], F32, name="sums")
+        for h in range(2):
+            ts = slice(2 * h, 2 * h + 2)
+            nc.scalar.activation(p[:, ts, :], a[:, ts, :], ACT.Exp, bias=bias[:], scale=1.0, accum_out=sums[:, h : h + 1])
 
-        vgrp = keep.tile([P, DV * PACK], BF16, name="vgrp", tag="grp", align_bytes=64)
+        vps = psum.tile([P, 2, 2, P], F32, name="vps", tag="scores")
+        for b in range(2):
+            for u in range(2):
+                nc.tensor.transpose(vps[:, b, u, :], vgs[b][:].bitcast(F32)[:, u : N // 2 : 2], identf[:])
+        vgrp = keep.tile([P, DV * PACK], BF16, name="vgrp", tag="ksg", align_bytes=64)
         nc.vector.tensor_copy(vgrp[:].bitcast(F32).rearrange("s (b e u) -> s b e u", b=2, u=2), vps[:].rearrange("s b u e -> s b e u"))
         vcodes = keep.tile([P, DV], U32, name="vcodes", align_bytes=64)
         vscale = keep.tile([P, DV], U8, name="vscale", align_bytes=64)
         nc.vector.quantize_mx(out=vcodes[:].bitcast(FP8X4), scales=vscale[:], in_=vgrp[:])
+        total = keep.tile([P, 1], F32, name="total")
+        nc.vector.tensor_tensor(total[:], sums[:, 0:1], sums[:, 1:2], ALU.add)
         recip = keep.tile([P, 1], F32, name="recip")
         nc.vector.reciprocal(recip[:], total[:])
 

@@ -31,7 +31,7 @@ def tile_attend_x_ks_append128_topk_kernel(tc, qT, kT, vT, new_kT, new_vT, ks, v
 
         kview = kT.rearrange("(p t) n -> p t n", t=PACK)
         newkview = new_kT.rearrange("(p t) n -> p t n", t=PACK)
-        newk23 = keep.tile([P, 2, NEW], F32, name="newk23")
+        newk23 = keep.tile([P, 2, NEW], F32, name="newk23", tag="newk23", align_bytes=64)
         newk01 = keep.tile([P, 2, NEW], F32, name="newk01", tag="grp", align_bytes=64)
         newv = keep.tile([P, 2, NEW], F32, name="newv", tag="newv")
         place = keep.tile([P, NEW // 16], U16, name="place")
@@ -96,13 +96,13 @@ def tile_attend_x_ks_append128_topk_kernel(tc, qT, kT, vT, new_kT, new_vT, ks, v
         nc.vector.tensor_copy(kp[2][:].indirect(place[:]), newk23[:, 0, :])
         nc.vector.tensor_copy(kgrp[:, :, 2], kp[2][:].indirect(idx[:]))
         qgrp = keep.tile([P, NQ, PACK], BF16, name="qgrp", align_bytes=64)
-        nc.gpsimd.tensor_scalar(qgrp[:], q_sb[:].rearrange("p t q -> p q t"), 1.0, 0.0, ALU.mult, ALU.add)
-        qcodes = keep.tile([P, NQ], U32, name="qcodes", align_bytes=64)
-        nc.vector.quantize_mx(out=qcodes[:].bitcast(FP8X4), scales=qscale[:], in_=qgrp[:].rearrange("p q t -> p (q t)"))
+        nc.scalar.copy(qgrp[:], q_sb[:].rearrange("p t q -> p q t"))
         vbs = [cast_values(b) for b in range(2)]
         vgs = [gather_values(b, vbs[b]) for b in range(2)]
         nc.vector.tensor_copy(kp[3][:].indirect(place[:]), newk23[:, 1, :])
         nc.vector.tensor_copy(kgrp[:, :, 3], kp[3][:].indirect(idx[:]))
+        qcodes = keep.tile([P, NQ], U32, name="qcodes", tag="newk23", align_bytes=64)
+        nc.vector.quantize_mx(out=qcodes[:].bitcast(FP8X4), scales=qscale[:], in_=qgrp[:].rearrange("p q t -> p (q t)"))
         nc.vector.quantize_mx(out=kcodes[:].bitcast(FP8X4), scales=kscale[:], in_=kgrp[:].rearrange("p n t -> p (n t)"))
         scores = psum.tile([P, N], F32, name="scores", tag="scores")
         nc.tensor.matmul_mx(

@@ -20,6 +20,7 @@ N = 512
 NQ = 128
 DV = 256
 NEW = 128
+HALF = N // 2
 FLOPS = 2 * NQ * N * 512 + 2 * NQ * N * DV
 
 
@@ -33,13 +34,13 @@ def tile_attend_x_ks_append128_topk_kernel(tc, qT, kT, vT, new_kT, new_vT, ks, v
         newkview = new_kT.rearrange("(p t) n -> p t n", t=PACK)
         newk23 = keep.tile([P, 2, NEW], F32, name="newk23", tag="newk23", align_bytes=64)
         newk01 = keep.tile([P, 2, NEW], F32, name="newk01", tag="grp", align_bytes=64)
-        newv = keep.tile([P, 2, NEW], F32, name="newv", tag="newv")
+        newv = keep.tile([P, 2, NEW], F32, name="newv")
         place = keep.tile([P, NEW // 16], U16, name="place")
         idx = keep.tile([P, N // 16], U16, name="idx")
         kp = [keep.tile([P, T], F32, name="kpool%d" % t, tag="kpool%d" % t) for t in range(PACK)]
         vp = [keep.tile([P, T], F32, name="vpool%d" % b) for b in range(2)]
         q_sb = keep.tile([P, PACK, NQ], F32, name="q_sb")
-        ks_sb = keep.tile([P, T], F32, name="ks_sb")
+        ks_sb = keep.tile([P, T], F32, name="ks_sb", tag="ks", align_bytes=64)
         vs_sb = keep.tile([P, T], F32, name="vs_sb")
         nc.vector.memset(vs_sb[0 : P - 1, :], 0.0)
         nc.sync.dma_start(vs_sb[P - 1 : P, :], vs[0:1, :])
@@ -53,8 +54,8 @@ def tile_attend_x_ks_append128_topk_kernel(tc, qT, kT, vT, new_kT, new_vT, ks, v
         nc.sync.dma_start(q_sb[:], qT[0].rearrange("(p t) q -> p t q", t=PACK))
         nc.sync.dma_start(newv[:], new_vT.rearrange("(b p) n -> p b n", b=2))
         nc.sync.dma_start(vp[0][:], vT[0:P, :])
-        nc.sync.dma_start(vp[1][:], vT[P : 2 * P, :])
         nc.sync.dma_start(kp[3][:], kview[:, 3, :])
+        nc.sync.dma_start(vp[1][:], vT[P : 2 * P, :])
         nc.sync.dma_start(ks_sb[:], ks)
 
         identf = keep.tile([P, P], F32, name="identf")
@@ -69,7 +70,6 @@ def tile_attend_x_ks_append128_topk_kernel(tc, qT, kT, vT, new_kT, new_vT, ks, v
         for t in range(PACK):
             nc.tensor.transpose(vsps[:, t, :], vsg[:, t:N:PACK], identf[:])
 
-        kcodes = keep.tile([P, N], U32, name="kcodes", align_bytes=64)
         kscale = keep.tile([P, N], U8, name="kscale", align_bytes=64)
         qscale = keep.tile([P, NQ], U8, name="qscale", align_bytes=64)
         kb = [keep.tile([P, T], BF16, name="kb%d" % t, tag="stage%d" % t, align_bytes=64) for t in range(2)]
@@ -81,7 +81,7 @@ def tile_attend_x_ks_append128_topk_kernel(tc, qT, kT, vT, new_kT, new_vT, ks, v
             return vb
 
         def gather_values(b, vb):
-            vg = keep.tile([P, N], BF16, name="vg%d" % b, tag="newv" if b == 0 else "vg1")
+            vg = keep.tile([P, N], BF16, name="vg%d" % b)
             nc.scalar.activation(vg[:], vb[:].indirect(idx[:]), ACT.Copy)
             return vg
 
@@ -94,37 +94,44 @@ def tile_attend_x_ks_append128_topk_kernel(tc, qT, kT, vT, new_kT, new_vT, ks, v
         vst = keep.tile([P, PACK], F32, name="vst", tag="kpool1")
         nc.scalar.copy(vst[:], vsps[:, :, P - 1])
         nc.vector.tensor_copy(kp[2][:].indirect(place[:]), newk23[:, 0, :])
-        nc.vector.tensor_copy(kgrp[:, :, 2], kp[2][:].indirect(idx[:]))
+        kg23 = keep.tile([P, 2, N], BF16, name="kg23")
+        nc.vector.tensor_copy(kg23[:, 0, :], kp[2][:].indirect(idx[:]))
         qgrp = keep.tile([P, NQ, PACK], BF16, name="qgrp", align_bytes=64)
         nc.scalar.copy(qgrp[:], q_sb[:].rearrange("p t q -> p q t"))
-        vbs = [cast_values(b) for b in range(2)]
-        vgs = [gather_values(b, vbs[b]) for b in range(2)]
+        vgs = [gather_values(0, cast_values(0))]
         nc.vector.tensor_copy(kp[3][:].indirect(place[:]), newk23[:, 1, :])
-        nc.vector.tensor_copy(kgrp[:, :, 3], kp[3][:].indirect(idx[:]))
+        nc.vector.tensor_copy(kg23[:, 1, :], kp[3][:].indirect(idx[:]))
+        nc.gpsimd.tensor_scalar(kgrp[:, :, 2:4], kg23[:].rearrange("p t n -> p n t"), 1.0, 0.0, ALU.mult, ALU.add)
         qcodes = keep.tile([P, NQ], U32, name="qcodes", tag="newk23", align_bytes=64)
         nc.vector.quantize_mx(out=qcodes[:].bitcast(FP8X4), scales=qscale[:], in_=qgrp[:].rearrange("p q t -> p (q t)"))
-        nc.vector.quantize_mx(out=kcodes[:].bitcast(FP8X4), scales=kscale[:], in_=kgrp[:].rearrange("p n t -> p (n t)"))
-        scores = psum.tile([P, N], F32, name="scores", tag="scores")
-        nc.tensor.matmul_mx(
-            out=scores[:],
-            lhsT=qcodes[:].bitcast(FP8X4),
-            lhsT_scale=qscale[:],
-            rhs=kcodes[:].bitcast(FP8X4),
-            rhs_scale=kscale[:],
-            start=True,
-            stop=True,
-        )
+        vgs.append(gather_values(1, cast_values(1)))
         ksg = keep.tile([P, N], F32, name="ksg", tag="ksg", align_bytes=64)
         nc.vector.tensor_copy(ksg[:], ks_sb[:].indirect(idx[:]))
+        kcodes = keep.tile([P, N], U32, name="kcodes", tag="ks", align_bytes=64)
+        scores = []
+        for h in range(2):
+            cols = slice(h * HALF, (h + 1) * HALF)
+            scores.append(psum.tile([P, HALF], F32, name="scores%d" % h, tag="scores%d" % h))
+            nc.vector.quantize_mx(out=kcodes[:, cols].bitcast(FP8X4), scales=kscale[:, cols], in_=kgrp[:, cols, :].rearrange("p n t -> p (n t)"))
+            nc.tensor.matmul_mx(
+                out=scores[h][:],
+                lhsT=qcodes[:].bitcast(FP8X4),
+                lhsT_scale=qscale[:],
+                rhs=kcodes[:, cols].bitcast(FP8X4),
+                rhs_scale=kscale[:, cols],
+                start=True,
+                stop=True,
+            )
 
         a = keep.tile([P, PACK, P], F32, name="a")
         bias = keep.tile([P, 1], F32, name="bias")
-        nc.vector.tensor_tensor(
-            a[:].rearrange("q t s -> q s t"),
-            scores[:].rearrange("q (s t) -> q s t", t=PACK),
-            ksg[:].rearrange("q (s t) -> q s t", t=PACK),
-            ALU.mult,
-        )
+        for h in range(2):
+            nc.vector.tensor_tensor(
+                a[:, :, h * HALF // PACK : (h + 1) * HALF // PACK].rearrange("q t s -> q s t"),
+                scores[h][:].rearrange("q (s t) -> q s t", t=PACK),
+                ksg[:, h * HALF : (h + 1) * HALF].rearrange("q (s t) -> q s t", t=PACK),
+                ALU.mult,
+            )
         nc.vector.tensor_reduce(bias[:], a[:], AX.XY, ALU.max, negate=True)
         p = keep.tile([P, PACK, P], F32, name="p", tag="stage1", align_bytes=64)
         sums = keep.tile([P, 2], F32, name="sums")
@@ -132,7 +139,7 @@ def tile_attend_x_ks_append128_topk_kernel(tc, qT, kT, vT, new_kT, new_vT, ks, v
             ts = slice(2 * h, 2 * h + 2)
             nc.scalar.activation(p[:, ts, :], a[:, ts, :], ACT.Exp, bias=bias[:], scale=1.0, accum_out=sums[:, h : h + 1])
 
-        vps = psum.tile([P, 2, 2, P], F32, name="vps", tag="scores")
+        vps = psum.tile([P, 2, 2, P], F32, name="vps", tag="scores1")
         for b in range(2):
             for u in range(2):
                 nc.tensor.transpose(vps[:, b, u, :], vgs[b][:].bitcast(F32)[:, u : N // 2 : 2], identf[:])

@@ -51,11 +51,12 @@ def tile_attend_x_ks_append128_topk_kernel(tc, qT, kT, vT, new_kT, new_vT, ks, v
         nc.sync.dma_start(kp[1][:], kview[:, 1, :])
         nc.sync.dma_start(newk23[:], newkview[:, 2:4, :])
         nc.sync.dma_start(kp[2][:], kview[:, 2, :])
-        nc.sync.dma_start(q_sb[:], qT[0].rearrange("(p t) q -> p t q", t=PACK))
-        nc.sync.dma_start(newv[:], new_vT.rearrange("(b p) n -> p b n", b=2))
-        nc.sync.dma_start(vp[0][:], vT[0:P, :])
+        vview = vT.rearrange("(p b) n -> p b n", b=2)
+        nc.sync.dma_start(newv[:], new_vT.rearrange("(p b) n -> p b n", b=2))
+        nc.sync.dma_start(vp[0][:], vview[:, 0, :])
         nc.sync.dma_start(kp[3][:], kview[:, 3, :])
-        nc.sync.dma_start(vp[1][:], vT[P : 2 * P, :])
+        nc.sync.dma_start(q_sb[:], qT[0].rearrange("(p t) q -> p t q", t=PACK))
+        nc.sync.dma_start(vp[1][:], vview[:, 1, :])
         nc.sync.dma_start(ks_sb[:], ks)
 
         identf = keep.tile([P, P], F32, name="identf")
@@ -97,7 +98,7 @@ def tile_attend_x_ks_append128_topk_kernel(tc, qT, kT, vT, new_kT, new_vT, ks, v
         kg23 = keep.tile([P, 2, N], BF16, name="kg23")
         nc.vector.tensor_copy(kg23[:, 0, :], kp[2][:].indirect(idx[:]))
         qgrp = keep.tile([P, NQ, PACK], BF16, name="qgrp", align_bytes=64)
-        nc.scalar.copy(qgrp[:], q_sb[:].rearrange("p t q -> p q t"))
+        nc.gpsimd.tensor_scalar(qgrp[:], q_sb[:].rearrange("p t q -> p q t"), 1.0, 0.0, ALU.mult, ALU.add)
         vgs = [gather_values(0, cast_values(0))]
         nc.vector.tensor_copy(kp[3][:].indirect(place[:]), newk23[:, 1, :])
         nc.vector.tensor_copy(kg23[:, 1, :], kp[3][:].indirect(idx[:]))
@@ -139,38 +140,45 @@ def tile_attend_x_ks_append128_topk_kernel(tc, qT, kT, vT, new_kT, new_vT, ks, v
             ts = slice(2 * h, 2 * h + 2)
             nc.scalar.activation(p[:, ts, :], a[:, ts, :], ACT.Exp, bias=bias[:], scale=1.0, accum_out=sums[:, h : h + 1])
 
-        vps = psum.tile([P, 2, 2, P], F32, name="vps", tag="scores1")
+        vps = psum.tile([P, 2, 2, P], F32, name="vps", tag="scores0")
         for b in range(2):
             for u in range(2):
                 nc.tensor.transpose(vps[:, b, u, :], vgs[b][:].bitcast(F32)[:, u : N // 2 : 2], identf[:])
         vgrp = keep.tile([P, DV * PACK], BF16, name="vgrp", tag="ksg", align_bytes=64)
-        nc.vector.tensor_copy(vgrp[:].bitcast(F32).rearrange("s (b e u) -> s b e u", b=2, u=2), vps[:].rearrange("s b u e -> s b e u"))
+        nc.vector.tensor_copy(vgrp[:].bitcast(F32).rearrange("s (e b u) -> s e b u", b=2, u=2), vps[:].rearrange("s b u e -> s e b u"))
         vcodes = keep.tile([P, DV], U32, name="vcodes", align_bytes=64)
         vscale = keep.tile([P, DV], U8, name="vscale", align_bytes=64)
         nc.vector.quantize_mx(out=vcodes[:].bitcast(FP8X4), scales=vscale[:], in_=vgrp[:])
-        total = keep.tile([P, 1], F32, name="total")
-        nc.vector.tensor_tensor(total[:], sums[:, 0:1], sums[:, 1:2], ALU.add)
-        recip = keep.tile([P, 1], F32, name="recip")
-        nc.vector.reciprocal(recip[:], total[:])
 
-        pps = psum.tile([P, PACK, NQ], F32, name="pps")
-        for t in range(PACK):
-            nc.tensor.transpose(pps[:, t, :], p[:, t, :], identf[:])
         wgrp = keep.tile([P, NQ, PACK], BF16, name="wgrp", align_bytes=64)
-        nc.vector.tensor_tensor(wgrp[:], pps[:].rearrange("s t q -> s q t"), vst[:].unsqueeze(1).to_broadcast([P, NQ, PACK]), ALU.mult)
+        for h in range(2):
+            pps = psum.tile([P, 2, NQ], F32, name="pps%d" % h)
+            for j in range(2):
+                nc.tensor.transpose(pps[:, j, :], p[:, 2 * h + j, :], identf[:])
+            ts = slice(2 * h, 2 * h + 2)
+            nc.vector.tensor_tensor(wgrp[:, :, ts], pps[:].rearrange("s t q -> s q t"), vst[:, ts].unsqueeze(1).to_broadcast([P, NQ, 2]), ALU.mult)
         wcodes = keep.tile([P, NQ], U32, name="wcodes", align_bytes=64)
         wscale = keep.tile([P, NQ], U8, name="wscale", align_bytes=64)
         nc.vector.quantize_mx(out=wcodes[:].bitcast(FP8X4), scales=wscale[:], in_=wgrp[:].rearrange("p q t -> p (q t)"))
-        ps_out = psum.tile([P, DV], F32, name="ps_out")
-        nc.tensor.matmul_mx(
-            out=ps_out[:],
-            lhsT=wcodes[:].bitcast(FP8X4),
-            lhsT_scale=wscale[:],
-            rhs=vcodes[:].bitcast(FP8X4),
-            rhs_scale=vscale[:],
-            start=True,
-            stop=True,
-        )
+        total = keep.tile([P, 1], F32, name="total", tag="kpool1")
+        nc.vector.tensor_tensor(total[:], sums[:, 0:1], sums[:, 1:2], ALU.add)
+        recip = keep.tile([P, 1], F32, name="recip")
+        nc.vector.reciprocal(recip[:], total[:])
         o_sb = keep.tile([P, DV], F32, name="o_sb")
-        nc.vector.tensor_scalar(o_sb[:], ps_out[:], recip[:], None, ALU.mult)
+        for h in range(2):
+            cols = slice(h * P, (h + 1) * P)
+            ps_out = psum.tile([P, P], F32, name="ps_out%d" % h)
+            nc.tensor.matmul_mx(
+                out=ps_out[:],
+                lhsT=wcodes[:].bitcast(FP8X4),
+                lhsT_scale=wscale[:],
+                rhs=vcodes[:, cols].bitcast(FP8X4),
+                rhs_scale=vscale[:, cols],
+                start=True,
+                stop=True,
+            )
+            if h == 0:
+                nc.scalar.activation(o_sb[:, cols], ps_out[:], ACT.Copy, scale=recip[:])
+            else:
+                nc.vector.tensor_scalar(o_sb[:, cols], ps_out[:], recip[:], None, ALU.mult)
         nc.sync.dma_start(out[0], o_sb[:])

@@ -32,7 +32,7 @@ def tile_attend_x_ks_append128_topk_kernel(tc, qT, kT, vT, new_kT, new_vT, ks, v
 
         kview = kT.rearrange("(p t) n -> p t n", t=PACK)
         newkview = new_kT.rearrange("(p t) n -> p t n", t=PACK)
-        newk23 = keep.tile([P, 2, NEW], F32, name="newk23", tag="newk23", align_bytes=64)
+        newk23 = keep.tile([P, 2, NEW], F32, name="newk23")
         newk01 = keep.tile([P, 2, NEW], F32, name="newk01", tag="grp", align_bytes=64)
         newv = keep.tile([P, 2, NEW], F32, name="newv")
         place = keep.tile([P, NEW // 16], U16, name="place")
@@ -52,10 +52,10 @@ def tile_attend_x_ks_append128_topk_kernel(tc, qT, kT, vT, new_kT, new_vT, ks, v
         nc.sync.dma_start(newk23[:], newkview[:, 2:4, :])
         nc.sync.dma_start(kp[2][:], kview[:, 2, :])
         vview = vT.rearrange("(p b) n -> p b n", b=2)
+        nc.sync.dma_start(q_sb[:], qT[0].rearrange("(p t) q -> p t q", t=PACK))
         nc.sync.dma_start(newv[:], new_vT.rearrange("(p b) n -> p b n", b=2))
         nc.sync.dma_start(vp[0][:], vview[:, 0, :])
         nc.sync.dma_start(kp[3][:], kview[:, 3, :])
-        nc.sync.dma_start(q_sb[:], qT[0].rearrange("(p t) q -> p t q", t=PACK))
         nc.sync.dma_start(vp[1][:], vview[:, 1, :])
         nc.sync.dma_start(ks_sb[:], ks)
 
@@ -99,12 +99,14 @@ def tile_attend_x_ks_append128_topk_kernel(tc, qT, kT, vT, new_kT, new_vT, ks, v
         nc.vector.tensor_copy(kg23[:, 0, :], kp[2][:].indirect(idx[:]))
         qgrp = keep.tile([P, NQ, PACK], BF16, name="qgrp", align_bytes=64)
         nc.gpsimd.tensor_scalar(qgrp[:], q_sb[:].rearrange("p t q -> p q t"), 1.0, 0.0, ALU.mult, ALU.add)
+        qcodes = keep.tile([P, NQ], U32, name="qcodes", align_bytes=64)
+        nc.vector.quantize_mx(out=qcodes[:].bitcast(FP8X4), scales=qscale[:], in_=qgrp[:].rearrange("p q t -> p (q t)"))
         vgs = [gather_values(0, cast_values(0))]
         nc.vector.tensor_copy(kp[3][:].indirect(place[:]), newk23[:, 1, :])
-        nc.vector.tensor_copy(kg23[:, 1, :], kp[3][:].indirect(idx[:]))
-        nc.gpsimd.tensor_scalar(kgrp[:, :, 2:4], kg23[:].rearrange("p t n -> p n t"), 1.0, 0.0, ALU.mult, ALU.add)
-        qcodes = keep.tile([P, NQ], U32, name="qcodes", tag="newk23", align_bytes=64)
-        nc.vector.quantize_mx(out=qcodes[:].bitcast(FP8X4), scales=qscale[:], in_=qgrp[:].rearrange("p q t -> p (q t)"))
+        for h in range(2):
+            cols = slice(h * HALF, (h + 1) * HALF)
+            nc.vector.tensor_copy(kg23[:, 1, cols], kp[3][:].indirect(idx[:, h * HALF // 16 : (h + 1) * HALF // 16]))
+            nc.gpsimd.tensor_scalar(kgrp[:, cols, 2:4], kg23[:, :, cols].rearrange("p t n -> p n t"), 1.0, 0.0, ALU.mult, ALU.add)
         vgs.append(gather_values(1, cast_values(1)))
         ksg = keep.tile([P, N], F32, name="ksg", tag="ksg", align_bytes=64)
         nc.vector.tensor_copy(ksg[:], ks_sb[:].indirect(idx[:]))

@@ -38,9 +38,10 @@ def tile_attend_x_ks_append128_topk_kernel(tc, qT, kT, vT, new_kT, new_vT, ks, v
         place = keep.tile([P, NEW // 16], U16, name="place")
         idx = keep.tile([P, N // 16], U16, name="idx")
         kp = [keep.tile([P, T], F32, name="kpool%d" % t, tag="kpool%d" % t) for t in range(PACK)]
-        vp = [keep.tile([P, T], F32, name="vpool%d" % b) for b in range(2)]
+        vp0 = keep.tile([P, T], F32, name="vpool0")
+        vp1 = [keep.tile([P, T // 2], F32, name="vpool1%d" % h, tag="vpool1%d" % h, align_bytes=64) for h in range(2)]
         q_sb = keep.tile([P, PACK, NQ], F32, name="q_sb")
-        ks_sb = keep.tile([P, T], F32, name="ks_sb", tag="ks", align_bytes=64)
+        ks_sb = keep.tile([P, T], F32, name="ks_sb")
         vs_sb = keep.tile([P, T], F32, name="vs_sb")
         nc.vector.memset(vs_sb[0 : P - 1, :], 0.0)
         nc.sync.dma_start(vs_sb[P - 1 : P, :], vs[0:1, :])
@@ -51,19 +52,17 @@ def tile_attend_x_ks_append128_topk_kernel(tc, qT, kT, vT, new_kT, new_vT, ks, v
         nc.sync.dma_start(kp[1][:], kview[:, 1, :])
         nc.sync.dma_start(newk23[:], newkview[:, 2:4, :])
         nc.sync.dma_start(kp[2][:], kview[:, 2, :])
-        vview = vT.rearrange("(p b) n -> p b n", b=2)
+        vview = vT.rearrange("(b p) n -> p b n", b=2)
         nc.sync.dma_start(q_sb[:], qT[0].rearrange("(p t) q -> p t q", t=PACK))
-        nc.sync.dma_start(newv[:], new_vT.rearrange("(p b) n -> p b n", b=2))
-        nc.sync.dma_start(vp[0][:], vview[:, 0, :])
+        nc.sync.dma_start(newv[:], new_vT.rearrange("(b p) n -> p b n", b=2))
         nc.sync.dma_start(kp[3][:], kview[:, 3, :])
-        nc.sync.dma_start(vp[1][:], vview[:, 1, :])
+        nc.sync.dma_start(vp0[:], vview[:, 0, :])
+        for h in range(2):
+            nc.sync.dma_start(vp1[h][:], vview[:, 1, h * T // 2 : (h + 1) * T // 2])
         nc.sync.dma_start(ks_sb[:], ks)
 
         identf = keep.tile([P, P], F32, name="identf")
         make_identity(nc, identf[:])
-        dummy = keep.tile([P, 1], F32, name="dummy")
-        nc.vector.memset(dummy[:], 0.0)
-        nc.scalar.activation(dummy[:], dummy[:], ACT.Exp)
 
         vsg = keep.tile([P, N], F32, name="vsg")
         nc.vector.tensor_copy(vsg[:], vs_sb[:].indirect(idx[:]))
@@ -75,23 +74,16 @@ def tile_attend_x_ks_append128_topk_kernel(tc, qT, kT, vT, new_kT, new_vT, ks, v
         qscale = keep.tile([P, NQ], U8, name="qscale", align_bytes=64)
         kb = [keep.tile([P, T], BF16, name="kb%d" % t, tag="stage%d" % t, align_bytes=64) for t in range(2)]
 
-        def cast_values(b):
-            vb = keep.tile([P, T], BF16, name="vb%d" % b, tag="stage%d" % b, align_bytes=64)
-            nc.vector.tensor_copy(vp[b][:].indirect(place[:]), newv[:, b, :])
-            nc.scalar.copy(vb[:], vp[b][:])
-            return vb
-
-        def gather_values(b, vb):
-            vg = keep.tile([P, N], BF16, name="vg%d" % b)
-            nc.scalar.activation(vg[:], vb[:].indirect(idx[:]), ACT.Copy)
-            return vg
-
         for t in range(2):
             nc.vector.tensor_copy(kp[t][:].indirect(place[:]), newk01[:, t, :])
             nc.scalar.copy(kb[t][:], kp[t][:])
-        kgrp = keep.tile([P, N, PACK], BF16, name="kgrp", tag="grp", align_bytes=64)
-        for t in range(2):
-            nc.scalar.activation(kgrp[:, :, t], kb[t][:].indirect(idx[:]), ACT.Copy)
+        kgrp = keep.tile([P, N, PACK], BF16, name="kgrp", align_bytes=64)
+        kg01 = keep.tile([P, 2, N], BF16, name="kg01", tag="grp", align_bytes=64)
+        for h in range(2):
+            cols = slice(h * HALF, (h + 1) * HALF)
+            for t in range(2):
+                nc.scalar.activation(kg01[:, t, cols], kb[t][:].indirect(idx[:, h * HALF // 16 : (h + 1) * HALF // 16]), ACT.Copy)
+            nc.gpsimd.tensor_scalar(kgrp[:, cols, 0:2], kg01[:, :, cols].rearrange("p t n -> p n t"), 1.0, 0.0, ALU.mult, ALU.add)
         vst = keep.tile([P, PACK], F32, name="vst", tag="kpool1")
         nc.scalar.copy(vst[:], vsps[:, :, P - 1])
         nc.vector.tensor_copy(kp[2][:].indirect(place[:]), newk23[:, 0, :])
@@ -101,38 +93,47 @@ def tile_attend_x_ks_append128_topk_kernel(tc, qT, kT, vT, new_kT, new_vT, ks, v
         nc.gpsimd.tensor_scalar(qgrp[:], q_sb[:].rearrange("p t q -> p q t"), 1.0, 0.0, ALU.mult, ALU.add)
         qcodes = keep.tile([P, NQ], U32, name="qcodes", align_bytes=64)
         nc.vector.quantize_mx(out=qcodes[:].bitcast(FP8X4), scales=qscale[:], in_=qgrp[:].rearrange("p q t -> p (q t)"))
-        vgs = [gather_values(0, cast_values(0))]
+        newvb = keep.tile([P, NEW], BF16, name="newvb", tag="newvb", align_bytes=64)
+        nc.gpsimd.tensor_scalar(newvb[:], newv[:, 1, :], 1.0, 0.0, ALU.mult, ALU.add)
         nc.vector.tensor_copy(kp[3][:].indirect(place[:]), newk23[:, 1, :])
         for h in range(2):
             cols = slice(h * HALF, (h + 1) * HALF)
             nc.vector.tensor_copy(kg23[:, 1, cols], kp[3][:].indirect(idx[:, h * HALF // 16 : (h + 1) * HALF // 16]))
             nc.gpsimd.tensor_scalar(kgrp[:, cols, 2:4], kg23[:, :, cols].rearrange("p t n -> p n t"), 1.0, 0.0, ALU.mult, ALU.add)
-        vgs.append(gather_values(1, cast_values(1)))
-        ksg = keep.tile([P, N], F32, name="ksg", tag="ksg", align_bytes=64)
-        nc.vector.tensor_copy(ksg[:], ks_sb[:].indirect(idx[:]))
-        kcodes = keep.tile([P, N], U32, name="kcodes", tag="ks", align_bytes=64)
-        scores = []
+        vgs = [keep.tile([P, N], BF16, name="vg%d" % b) for b in range(2)]
+        nc.vector.tensor_copy(vp0[:].indirect(place[:]), newv[:, 0, :])
+        vb1 = keep.tile([P, T], BF16, name="vb1", tag="stage1", align_bytes=64)
         for h in range(2):
-            cols = slice(h * HALF, (h + 1) * HALF)
-            scores.append(psum.tile([P, HALF], F32, name="scores%d" % h, tag="scores%d" % h))
-            nc.vector.quantize_mx(out=kcodes[:, cols].bitcast(FP8X4), scales=kscale[:, cols], in_=kgrp[:, cols, :].rearrange("p n t -> p (n t)"))
-            nc.tensor.matmul_mx(
-                out=scores[h][:],
-                lhsT=qcodes[:].bitcast(FP8X4),
-                lhsT_scale=qscale[:],
-                rhs=kcodes[:, cols].bitcast(FP8X4),
-                rhs_scale=kscale[:, cols],
-                start=True,
-                stop=True,
-            )
+            nc.scalar.copy(vb1[:, h * T // 2 : (h + 1) * T // 2], vp1[h][:])
+        nc.vector.tensor_copy(vb1[:].indirect(place[:]), newvb[:])
+        vb0 = keep.tile([P, T], BF16, name="vb0", tag="vpool10", align_bytes=64)
+        nc.scalar.copy(vb0[:], vp0[:])
+        nc.scalar.activation(vgs[0][:], vb0[:].indirect(idx[:]), ACT.Copy)
+        nc.scalar.activation(vgs[1][:], vb1[:].indirect(idx[:]), ACT.Copy)
+        kcodes = keep.tile([P, N], U32, name="kcodes", tag="vpool11", align_bytes=64)
+        nc.vector.quantize_mx(out=kcodes[:].bitcast(FP8X4), scales=kscale[:], in_=kgrp[:].rearrange("p n t -> p (n t)"))
+        scores = psum.tile([P, N], F32, name="scores")
+        nc.tensor.matmul_mx(
+            out=scores[:],
+            lhsT=qcodes[:].bitcast(FP8X4),
+            lhsT_scale=qscale[:],
+            rhs=kcodes[:].bitcast(FP8X4),
+            rhs_scale=kscale[:],
+            start=True,
+            stop=True,
+        )
+        ksg = keep.tile([P, N], F32, name="ksg", tag="newvb", align_bytes=64)
+        for h in range(2):
+            nc.vector.tensor_copy(ksg[:, h * HALF : (h + 1) * HALF], ks_sb[:].indirect(idx[:, h * HALF // 16 : (h + 1) * HALF // 16]))
 
         a = keep.tile([P, PACK, P], F32, name="a")
         bias = keep.tile([P, 1], F32, name="bias")
         for h in range(2):
+            cols = slice(h * HALF, (h + 1) * HALF)
             nc.vector.tensor_tensor(
                 a[:, :, h * HALF // PACK : (h + 1) * HALF // PACK].rearrange("q t s -> q s t"),
-                scores[h][:].rearrange("q (s t) -> q s t", t=PACK),
-                ksg[:, h * HALF : (h + 1) * HALF].rearrange("q (s t) -> q s t", t=PACK),
+                scores[:, cols].rearrange("q (s t) -> q s t", t=PACK),
+                ksg[:, cols].rearrange("q (s t) -> q s t", t=PACK),
                 ALU.mult,
             )
         nc.vector.tensor_reduce(bias[:], a[:], AX.XY, ALU.max, negate=True)
@@ -142,15 +143,20 @@ def tile_attend_x_ks_append128_topk_kernel(tc, qT, kT, vT, new_kT, new_vT, ks, v
             ts = slice(2 * h, 2 * h + 2)
             nc.scalar.activation(p[:, ts, :], a[:, ts, :], ACT.Exp, bias=bias[:], scale=1.0, accum_out=sums[:, h : h + 1])
 
-        vps = psum.tile([P, 2, 2, P], F32, name="vps", tag="scores0")
-        for b in range(2):
-            for u in range(2):
-                nc.tensor.transpose(vps[:, b, u, :], vgs[b][:].bitcast(F32)[:, u : N // 2 : 2], identf[:])
-        vgrp = keep.tile([P, DV * PACK], BF16, name="vgrp", tag="ksg", align_bytes=64)
-        nc.vector.tensor_copy(vgrp[:].bitcast(F32).rearrange("s (e b u) -> s e b u", b=2, u=2), vps[:].rearrange("s b u e -> s e b u"))
+        vgrp = keep.tile([P, DV * PACK], BF16, name="vgrp", tag="newvb", align_bytes=64)
         vcodes = keep.tile([P, DV], U32, name="vcodes", align_bytes=64)
         vscale = keep.tile([P, DV], U8, name="vscale", align_bytes=64)
-        nc.vector.quantize_mx(out=vcodes[:].bitcast(FP8X4), scales=vscale[:], in_=vgrp[:])
+        for b in range(2):
+            vps = psum.tile([P, 2, P], F32, name="vps%d" % b)
+            for u in range(2):
+                nc.tensor.transpose(vps[:, u, :], vgs[b][:].bitcast(F32)[:, u : N // 2 : 2], identf[:])
+            nc.vector.tensor_copy(
+                vgrp[:, b * P * PACK : (b + 1) * P * PACK].bitcast(F32).rearrange("s (e u) -> s e u", u=2),
+                vps[:].rearrange("s u e -> s e u"),
+            )
+        for b in range(2):
+            cols = slice(b * P, (b + 1) * P)
+            nc.vector.quantize_mx(out=vcodes[:, cols].bitcast(FP8X4), scales=vscale[:, cols], in_=vgrp[:, b * P * PACK : (b + 1) * P * PACK])
 
         wgrp = keep.tile([P, NQ, PACK], BF16, name="wgrp", align_bytes=64)
         for h in range(2):

@@ -78,12 +78,12 @@ def tile_attend_x_ks_append128_topk_kernel(tc, qT, kT, vT, new_kT, new_vT, ks, v
             nc.vector.tensor_copy(kp[t][:].indirect(place[:]), newk01[:, t, :])
             nc.scalar.copy(kb[t][:], kp[t][:])
         kgrp = keep.tile([P, N, PACK], BF16, name="kgrp", align_bytes=64)
-        kg01 = keep.tile([P, 2, N], BF16, name="kg01", tag="grp", align_bytes=64)
-        for h in range(2):
-            cols = slice(h * HALF, (h + 1) * HALF)
-            for t in range(2):
-                nc.scalar.activation(kg01[:, t, cols], kb[t][:].indirect(idx[:, h * HALF // 16 : (h + 1) * HALF // 16]), ACT.Copy)
-            nc.gpsimd.tensor_scalar(kgrp[:, cols, 0:2], kg01[:, :, cols].rearrange("p t n -> p n t"), 1.0, 0.0, ALU.mult, ALU.add)
+        kg01 = keep.tile([P, 2, HALF], BF16, name="kg01", tag="grp", align_bytes=64)
+        for t in range(2):
+            nc.scalar.activation(kg01[:, t, :], kb[t][:].indirect(idx[:, 0 : HALF // 16]), ACT.Copy)
+        nc.gpsimd.tensor_scalar(kgrp[:, 0:HALF, 0:2], kg01[:].rearrange("p t n -> p n t"), 1.0, 0.0, ALU.mult, ALU.add)
+        for t in range(2):
+            nc.scalar.activation(kgrp[:, HALF:N, t], kb[t][:].indirect(idx[:, HALF // 16 : N // 16]), ACT.Copy)
         vst = keep.tile([P, PACK], F32, name="vst", tag="kpool1")
         nc.scalar.copy(vst[:], vsps[:, :, P - 1])
         nc.vector.tensor_copy(kp[2][:].indirect(place[:]), newk23[:, 0, :])

@@ -21,6 +21,7 @@ NQ = 128
 DV = 256
 NEW = 128
 HALF = N // 2
+QUARTER = N // 4
 FLOPS = 2 * NQ * N * 512 + 2 * NQ * N * DV
 
 
@@ -30,88 +31,100 @@ def tile_attend_x_ks_append128_topk_kernel(tc, qT, kT, vT, new_kT, new_vT, ks, v
         keep = ctx.enter_context(tc.tile_pool(name="keep", bufs=1))
         psum = ctx.enter_context(tc.psum_pool(name="psum", bufs=1))
 
+        late = ctx.enter_context(tc.tile_pool(name="late", bufs=1))
+
         kview = kT.rearrange("(p t) n -> p t n", t=PACK)
         newkview = new_kT.rearrange("(p t) n -> p t n", t=PACK)
-        newk23 = keep.tile([P, 2, NEW], F32, name="newk23")
-        newk01 = keep.tile([P, 2, NEW], F32, name="newk01", tag="grp", align_bytes=64)
-        newv = keep.tile([P, 2, NEW], F32, name="newv")
+        vview = vT.rearrange("(b p) n -> p b n", b=2)
         place = keep.tile([P, NEW // 16], U16, name="place")
         idx = keep.tile([P, N // 16], U16, name="idx")
-        kp = [keep.tile([P, T], F32, name="kpool%d" % t, tag="kpool%d" % t) for t in range(PACK)]
-        vp0 = keep.tile([P, T], F32, name="vpool0")
-        vp1 = [keep.tile([P, T // 2], F32, name="vpool1%d" % h, tag="vpool1%d" % h, align_bytes=64) for h in range(2)]
+        newk01 = keep.tile([P, 2, NEW], F32, name="newk01")
+        newk23 = keep.tile([P, 2, NEW], F32, name="newk23")
+        newv = keep.tile([P, 2, NEW], F32, name="newv", tag="newv", align_bytes=64)
+        kp = [keep.tile([P, T], F32, name="kpool%d" % t, tag="kpool%d" % t, align_bytes=64) for t in range(PACK)]
+        vp0 = keep.tile([P, T], F32, name="vpool0", tag="vpool0", align_bytes=64)
+        vp1 = late.tile([P, T], F32, name="vpool1", offset=0)
         q_sb = keep.tile([P, PACK, NQ], F32, name="q_sb")
         ks_sb = keep.tile([P, T], F32, name="ks_sb")
         vs_sb = keep.tile([P, T], F32, name="vs_sb")
-        nc.vector.memset(vs_sb[0 : P - 1, :], 0.0)
-        nc.sync.dma_start(vs_sb[P - 1 : P, :], vs[0:1, :])
+        nc.gpsimd.memset(vs_sb[0 : P - 1, :], 0.0)
+        nc.vector.memset(ks_sb[0 : P - 1, :], 0.0)
+        nc.sync.dma_start(ks_sb[P - 1 : P, :], ks[0:1, :])
         nc.sync.dma_start(idx[:], offs)
+        nc.sync.dma_start(vs_sb[P - 1 : P, :], vs[0:1, :])
         nc.sync.dma_start(kp[0][:], kview[:, 0, :])
         nc.sync.dma_start(place[:], slots)
         nc.sync.dma_start(newk01[:], newkview[:, 0:2, :])
         nc.sync.dma_start(kp[1][:], kview[:, 1, :])
         nc.sync.dma_start(newk23[:], newkview[:, 2:4, :])
         nc.sync.dma_start(kp[2][:], kview[:, 2, :])
-        vview = vT.rearrange("(b p) n -> p b n", b=2)
-        nc.sync.dma_start(q_sb[:], qT[0].rearrange("(p t) q -> p t q", t=PACK))
-        nc.sync.dma_start(newv[:], new_vT.rearrange("(b p) n -> p b n", b=2))
         nc.sync.dma_start(kp[3][:], kview[:, 3, :])
+        nc.sync.dma_start(newv[:], new_vT.rearrange("(b p) n -> p b n", b=2))
+        nc.sync.dma_start(q_sb[:], qT[0].rearrange("(p t) q -> p t q", t=PACK))
         nc.sync.dma_start(vp0[:], vview[:, 0, :])
-        for h in range(2):
-            nc.sync.dma_start(vp1[h][:], vview[:, 1, h * T // 2 : (h + 1) * T // 2])
-        nc.sync.dma_start(ks_sb[:], ks)
+        nc.sync.dma_start(vp1[:], vview[:, 1, :])
 
         identf = keep.tile([P, P], F32, name="identf")
         make_identity(nc, identf[:])
 
+        ksg = keep.tile([P, N], F32, name="ksg")
+        nc.vector.tensor_copy(ksg[:], ks_sb[:].indirect(idx[:]))
         vsg = keep.tile([P, N], F32, name="vsg")
         nc.vector.tensor_copy(vsg[:], vs_sb[:].indirect(idx[:]))
-        vsps = psum.tile([P, PACK, P], F32, name="vsps")
+        ksps = psum.tile([P, PACK, P], F32, name="ksps", tag="bank0")
+        for c in range(PACK):
+            nc.tensor.transpose(ksps[:, c, :], ksg[:, c * P : (c + 1) * P], identf[:])
+        vsps = psum.tile([P, PACK, P], F32, name="vsps", tag="bank1")
         for t in range(PACK):
             nc.tensor.transpose(vsps[:, t, :], vsg[:, t:N:PACK], identf[:])
 
         kscale = keep.tile([P, N], U8, name="kscale", align_bytes=64)
         qscale = keep.tile([P, NQ], U8, name="qscale", align_bytes=64)
         kb = [keep.tile([P, T], BF16, name="kb%d" % t, tag="stage%d" % t, align_bytes=64) for t in range(2)]
+        newkb = keep.tile([P, 2, NEW], BF16, name="newkb")
+        nc.gpsimd.tensor_scalar(newkb[:], newk01[:], 1.0, 0.0, ALU.mult, ALU.add)
+        for t in range(2):
+            nc.scalar.copy(kb[t][:], kp[t][:])
+            nc.vector.tensor_copy(kb[t][:].indirect(place[:]), newkb[:, t, :])
+        kgrp = keep.tile([P, N, PACK], BF16, name="kgrp", tag="kpool1", align_bytes=64)
+        for t in range(2):
+            nc.scalar.activation(kgrp[:, :, t], kb[t][:].indirect(idx[:]), ACT.Copy)
+        cols4 = keep.tile([P, 2 * PACK], F32, name="cols4", tag="stage0", align_bytes=64)
+        kst = cols4[:, 0:PACK]
+        vst = cols4[:, PACK : 2 * PACK]
+        nc.scalar.copy(kst, ksps[:, :, P - 1])
+        nc.scalar.copy(vst, vsps[:, :, P - 1])
+        ksrow = psum.tile([P, N], F32, name="ksrow")
+        for c in range(PACK):
+            nc.tensor.transpose(ksrow[:, c * P : (c + 1) * P], kst[:, c : c + 1].to_broadcast([P, P]), identf[:])
 
         for t in range(2):
-            nc.vector.tensor_copy(kp[t][:].indirect(place[:]), newk01[:, t, :])
-            nc.scalar.copy(kb[t][:], kp[t][:])
-        kgrp = keep.tile([P, N, PACK], BF16, name="kgrp", align_bytes=64)
-        kg01 = keep.tile([P, 2, HALF], BF16, name="kg01", tag="grp", align_bytes=64)
-        for t in range(2):
-            nc.scalar.activation(kg01[:, t, :], kb[t][:].indirect(idx[:, 0 : HALF // 16]), ACT.Copy)
-        nc.gpsimd.tensor_scalar(kgrp[:, 0:HALF, 0:2], kg01[:].rearrange("p t n -> p n t"), 1.0, 0.0, ALU.mult, ALU.add)
-        for t in range(2):
-            nc.scalar.activation(kgrp[:, HALF:N, t], kb[t][:].indirect(idx[:, HALF // 16 : N // 16]), ACT.Copy)
-        vst = keep.tile([P, PACK], F32, name="vst", tag="kpool1")
-        nc.scalar.copy(vst[:], vsps[:, :, P - 1])
-        nc.vector.tensor_copy(kp[2][:].indirect(place[:]), newk23[:, 0, :])
-        kg23 = keep.tile([P, 2, N], BF16, name="kg23")
-        nc.vector.tensor_copy(kg23[:, 0, :], kp[2][:].indirect(idx[:]))
+            nc.vector.tensor_copy(kp[2 + t][:].indirect(place[:]), newk23[:, t, :])
+        newvb = keep.tile([P, 2, NEW], BF16, name="newvb")
+        nc.gpsimd.tensor_scalar(newvb[:], newv[:], 1.0, 0.0, ALU.mult, ALU.add)
+        kg23 = keep.tile([P, 2, N], BF16, name="kg23", tag="newv", align_bytes=64)
         qgrp = keep.tile([P, NQ, PACK], BF16, name="qgrp", align_bytes=64)
         nc.gpsimd.tensor_scalar(qgrp[:], q_sb[:].rearrange("p t q -> p q t"), 1.0, 0.0, ALU.mult, ALU.add)
         qcodes = keep.tile([P, NQ], U32, name="qcodes", align_bytes=64)
         nc.vector.quantize_mx(out=qcodes[:].bitcast(FP8X4), scales=qscale[:], in_=qgrp[:].rearrange("p q t -> p (q t)"))
-        newvb = keep.tile([P, NEW], BF16, name="newvb", tag="newvb", align_bytes=64)
-        nc.gpsimd.tensor_scalar(newvb[:], newv[:, 1, :], 1.0, 0.0, ALU.mult, ALU.add)
-        nc.vector.tensor_copy(kp[3][:].indirect(place[:]), newk23[:, 1, :])
-        for h in range(2):
-            cols = slice(h * HALF, (h + 1) * HALF)
-            nc.vector.tensor_copy(kg23[:, 1, cols], kp[3][:].indirect(idx[:, h * HALF // 16 : (h + 1) * HALF // 16]))
+        for lo, hi in ((0, HALF), (HALF, HALF + QUARTER), (HALF + QUARTER, N)):
+            cols = slice(lo, hi)
+            for t in range(2):
+                nc.vector.tensor_copy(kg23[:, t, cols], kp[2 + t][:].indirect(idx[:, lo // 16 : hi // 16]))
             nc.gpsimd.tensor_scalar(kgrp[:, cols, 2:4], kg23[:, :, cols].rearrange("p t n -> p n t"), 1.0, 0.0, ALU.mult, ALU.add)
-        vgs = [keep.tile([P, N], BF16, name="vg%d" % b) for b in range(2)]
-        nc.vector.tensor_copy(vp0[:].indirect(place[:]), newv[:, 0, :])
+        vb0 = keep.tile([P, T], BF16, name="vb0", align_bytes=64)
         vb1 = keep.tile([P, T], BF16, name="vb1", tag="stage1", align_bytes=64)
-        for h in range(2):
-            nc.scalar.copy(vb1[:, h * T // 2 : (h + 1) * T // 2], vp1[h][:])
-        nc.vector.tensor_copy(vb1[:].indirect(place[:]), newvb[:])
-        vb0 = keep.tile([P, T], BF16, name="vb0", tag="vpool10", align_bytes=64)
         nc.scalar.copy(vb0[:], vp0[:])
+        nc.scalar.copy(vb1[:], vp1[:])
+        ksb = late.tile([P, N], F32, name="ksb", tag="ksb", align_bytes=64, offset=1024)
+        nc.scalar.copy(ksb[:], ksrow[:])
+        nc.vector.tensor_copy(vb0[:].indirect(place[:]), newvb[:, 0, :])
+        kcodes = keep.tile([P, N], U32, name="kcodes", tag="vpool0", align_bytes=64)
+        nc.vector.quantize_mx(out=kcodes[:].bitcast(FP8X4), scales=kscale[:], in_=kgrp[:].rearrange("p n t -> p (n t)"))
+        nc.vector.tensor_copy(vb1[:].indirect(place[:]), newvb[:, 1, :])
+        vgs = [late.tile([P, N], BF16, name="vg0", offset=0), keep.tile([P, N], BF16, name="vg1")]
         nc.scalar.activation(vgs[0][:], vb0[:].indirect(idx[:]), ACT.Copy)
         nc.scalar.activation(vgs[1][:], vb1[:].indirect(idx[:]), ACT.Copy)
-        kcodes = keep.tile([P, N], U32, name="kcodes", tag="vpool11", align_bytes=64)
-        nc.vector.quantize_mx(out=kcodes[:].bitcast(FP8X4), scales=kscale[:], in_=kgrp[:].rearrange("p n t -> p (n t)"))
         scores = psum.tile([P, N], F32, name="scores")
         nc.tensor.matmul_mx(
             out=scores[:],
@@ -122,9 +135,6 @@ def tile_attend_x_ks_append128_topk_kernel(tc, qT, kT, vT, new_kT, new_vT, ks, v
             start=True,
             stop=True,
         )
-        ksg = keep.tile([P, N], F32, name="ksg", tag="newvb", align_bytes=64)
-        for h in range(2):
-            nc.vector.tensor_copy(ksg[:, h * HALF : (h + 1) * HALF], ks_sb[:].indirect(idx[:, h * HALF // 16 : (h + 1) * HALF // 16]))
 
         a = keep.tile([P, PACK, P], F32, name="a")
         bias = keep.tile([P, 1], F32, name="bias")
@@ -133,7 +143,7 @@ def tile_attend_x_ks_append128_topk_kernel(tc, qT, kT, vT, new_kT, new_vT, ks, v
             nc.vector.tensor_tensor(
                 a[:, :, h * HALF // PACK : (h + 1) * HALF // PACK].rearrange("q t s -> q s t"),
                 scores[:, cols].rearrange("q (s t) -> q s t", t=PACK),
-                ksg[:, cols].rearrange("q (s t) -> q s t", t=PACK),
+                ksb[:, cols].rearrange("q (s t) -> q s t", t=PACK),
                 ALU.mult,
             )
         nc.vector.tensor_reduce(bias[:], a[:], AX.XY, ALU.max, negate=True)
@@ -143,7 +153,7 @@ def tile_attend_x_ks_append128_topk_kernel(tc, qT, kT, vT, new_kT, new_vT, ks, v
             ts = slice(2 * h, 2 * h + 2)
             nc.scalar.activation(p[:, ts, :], a[:, ts, :], ACT.Exp, bias=bias[:], scale=1.0, accum_out=sums[:, h : h + 1])
 
-        vgrp = keep.tile([P, DV * PACK], BF16, name="vgrp", tag="newvb", align_bytes=64)
+        vgrp = late.tile([P, DV * PACK], BF16, name="vgrp", tag="ksb", align_bytes=64, offset=1024)
         vcodes = keep.tile([P, DV], U32, name="vcodes", align_bytes=64)
         vscale = keep.tile([P, DV], U8, name="vscale", align_bytes=64)
         for b in range(2):
@@ -168,14 +178,14 @@ def tile_attend_x_ks_append128_topk_kernel(tc, qT, kT, vT, new_kT, new_vT, ks, v
         wcodes = keep.tile([P, NQ], U32, name="wcodes", align_bytes=64)
         wscale = keep.tile([P, NQ], U8, name="wscale", align_bytes=64)
         nc.vector.quantize_mx(out=wcodes[:].bitcast(FP8X4), scales=wscale[:], in_=wgrp[:].rearrange("p q t -> p (q t)"))
-        total = keep.tile([P, 1], F32, name="total", tag="kpool1")
+        total = keep.tile([P, 1], F32, name="total", tag="stage0", align_bytes=64)
         nc.vector.tensor_tensor(total[:], sums[:, 0:1], sums[:, 1:2], ALU.add)
         recip = keep.tile([P, 1], F32, name="recip")
         nc.vector.reciprocal(recip[:], total[:])
         o_sb = keep.tile([P, DV], F32, name="o_sb")
         for h in range(2):
             cols = slice(h * P, (h + 1) * P)
-            ps_out = psum.tile([P, P], F32, name="ps_out%d" % h)
+            ps_out = psum.tile([P, P], F32, name="ps_out%d" % h, tag="bank%d" % h)
             nc.tensor.matmul_mx(
                 out=ps_out[:],
                 lhsT=wcodes[:].bitcast(FP8X4),

@@ -36,14 +36,17 @@ def tile_attend_x_ks_append128_topk_kernel(tc, qT, kT, vT, new_kT, new_vT, ks, v
         kview = kT.rearrange("(p t) n -> p t n", t=PACK)
         newkview = new_kT.rearrange("(p t) n -> p t n", t=PACK)
         vview = vT.rearrange("(b p) n -> p b n", b=2)
+        newvview = new_vT.rearrange("(b p) n -> p b n", b=2)
         place = keep.tile([P, NEW // 16], U16, name="place")
         idx = keep.tile([P, N // 16], U16, name="idx")
         newk01 = keep.tile([P, 2, NEW], F32, name="newk01")
-        newk23 = keep.tile([P, 2, NEW], F32, name="newk23")
-        newv = keep.tile([P, 2, NEW], F32, name="newv", tag="newv", align_bytes=64)
-        kp = [keep.tile([P, T], F32, name="kpool%d" % t, tag="kpool%d" % t, align_bytes=64) for t in range(PACK)]
-        vp0 = keep.tile([P, T], F32, name="vpool0", tag="vpool0", align_bytes=64)
-        vp1 = late.tile([P, T], F32, name="vpool1", offset=0)
+        newk23 = late.tile([P, 2, NEW], F32, name="newk23", offset=8192)
+        newv = [keep.tile([P, NEW], F32, name="newv%d" % b, tag="newv%d" % b, align_bytes=64) for b in range(2)]
+        khalf = [[keep.tile([P, T // 2], F32, name="khalf%d%d" % (t, h)) for h in range(2)] for t in range(1)]
+        khalf.append([keep.tile([P, T // 2], F32, name="khalf10"), late.tile([P, T // 2], F32, name="khalf11", offset=4096)])
+        kp2 = keep.tile([P, T], F32, name="kp2")
+        kp3 = keep.tile([P, T], F32, name="kp3")
+        vp = [keep.tile([P, T], F32, name="vpool%d" % b) for b in range(2)]
         q_sb = keep.tile([P, PACK, NQ], F32, name="q_sb")
         ks_sb = keep.tile([P, T], F32, name="ks_sb")
         vs_sb = keep.tile([P, T], F32, name="vs_sb")
@@ -52,17 +55,19 @@ def tile_attend_x_ks_append128_topk_kernel(tc, qT, kT, vT, new_kT, new_vT, ks, v
         nc.sync.dma_start(ks_sb[P - 1 : P, :], ks[0:1, :])
         nc.sync.dma_start(idx[:], offs)
         nc.sync.dma_start(vs_sb[P - 1 : P, :], vs[0:1, :])
-        nc.sync.dma_start(kp[0][:], kview[:, 0, :])
-        nc.sync.dma_start(place[:], slots)
+        for h in range(2):
+            nc.sync.dma_start(khalf[0][h][:], kview[:, 0, h * T // 2 : (h + 1) * T // 2])
         nc.sync.dma_start(newk01[:], newkview[:, 0:2, :])
-        nc.sync.dma_start(kp[1][:], kview[:, 1, :])
+        nc.sync.dma_start(place[:], slots)
+        for h in range(2):
+            nc.sync.dma_start(khalf[1][h][:], kview[:, 1, h * T // 2 : (h + 1) * T // 2])
         nc.sync.dma_start(newk23[:], newkview[:, 2:4, :])
-        nc.sync.dma_start(kp[2][:], kview[:, 2, :])
-        nc.sync.dma_start(kp[3][:], kview[:, 3, :])
-        nc.sync.dma_start(newv[:], new_vT.rearrange("(b p) n -> p b n", b=2))
+        nc.sync.dma_start(kp2[:], kview[:, 2, :])
+        nc.sync.dma_start(kp3[:], kview[:, 3, :])
         nc.sync.dma_start(q_sb[:], qT[0].rearrange("(p t) q -> p t q", t=PACK))
-        nc.sync.dma_start(vp0[:], vview[:, 0, :])
-        nc.sync.dma_start(vp1[:], vview[:, 1, :])
+        for b in range(2):
+            nc.sync.dma_start(newv[b][:], newvview[:, b, :])
+            nc.sync.dma_start(vp[b][:], vview[:, b, :])
 
         identf = keep.tile([P, P], F32, name="identf")
         make_identity(nc, identf[:])
@@ -80,51 +85,57 @@ def tile_attend_x_ks_append128_topk_kernel(tc, qT, kT, vT, new_kT, new_vT, ks, v
 
         kscale = keep.tile([P, N], U8, name="kscale", align_bytes=64)
         qscale = keep.tile([P, NQ], U8, name="qscale", align_bytes=64)
-        kb = [keep.tile([P, T], BF16, name="kb%d" % t, tag="stage%d" % t, align_bytes=64) for t in range(2)]
+        kb = [keep.tile([P, T], BF16, name="kb%d" % t) for t in range(2)]
         newkb = keep.tile([P, 2, NEW], BF16, name="newkb")
         nc.gpsimd.tensor_scalar(newkb[:], newk01[:], 1.0, 0.0, ALU.mult, ALU.add)
         for t in range(2):
-            nc.scalar.copy(kb[t][:], kp[t][:])
+            for h in range(2):
+                nc.scalar.copy(kb[t][:, h * T // 2 : (h + 1) * T // 2], khalf[t][h][:])
             nc.vector.tensor_copy(kb[t][:].indirect(place[:]), newkb[:, t, :])
-        kgrp = keep.tile([P, N, PACK], BF16, name="kgrp", tag="kpool1", align_bytes=64)
-        for t in range(2):
-            nc.scalar.activation(kgrp[:, :, t], kb[t][:].indirect(idx[:]), ACT.Copy)
-        cols4 = keep.tile([P, 2 * PACK], F32, name="cols4", tag="stage0", align_bytes=64)
-        kst = cols4[:, 0:PACK]
-        vst = cols4[:, PACK : 2 * PACK]
-        nc.scalar.copy(kst, ksps[:, :, P - 1])
-        nc.scalar.copy(vst, vsps[:, :, P - 1])
+        kst = late.tile([P, PACK], F32, name="kst", offset=4096)
+        nc.scalar.copy(kst[:], ksps[:, :, P - 1])
         ksrow = psum.tile([P, N], F32, name="ksrow")
         for c in range(PACK):
             nc.tensor.transpose(ksrow[:, c * P : (c + 1) * P], kst[:, c : c + 1].to_broadcast([P, P]), identf[:])
-
+        kg01 = late.tile([P, 2, HALF], BF16, name="kg01", offset=4160)
+        kgrp = [keep.tile([P, HALF, PACK], BF16, name="kgrp0", align_bytes=64), late.tile([P, HALF, PACK], BF16, name="kgrp1", align_bytes=64, offset=8192 + 512)]
         for t in range(2):
-            nc.vector.tensor_copy(kp[2 + t][:].indirect(place[:]), newk23[:, t, :])
-        newvb = keep.tile([P, 2, NEW], BF16, name="newvb")
-        nc.gpsimd.tensor_scalar(newvb[:], newv[:], 1.0, 0.0, ALU.mult, ALU.add)
-        kg23 = keep.tile([P, 2, N], BF16, name="kg23", tag="newv", align_bytes=64)
+            nc.scalar.activation(kg01[:, t, :], kb[t][:].indirect(idx[:, 0 : HALF // 16]), ACT.Copy)
+        nc.vector.tensor_copy(kp2[:].indirect(place[:]), newk23[:, 0, :])
+        nc.vector.tensor_copy(kp3[:].indirect(place[:]), newk23[:, 1, :])
+        kb2 = late.tile([P, T], BF16, name="kb2", offset=0)
+        nc.scalar.copy(kb2[:], kp2[:])
+        kg23 = late.tile([P, PACK, 2, QUARTER], BF16, name="kg23", offset=8192 + 512 - 2048)
         qgrp = keep.tile([P, NQ, PACK], BF16, name="qgrp", align_bytes=64)
         nc.gpsimd.tensor_scalar(qgrp[:], q_sb[:].rearrange("p t q -> p q t"), 1.0, 0.0, ALU.mult, ALU.add)
+        nc.gpsimd.tensor_scalar(kgrp[0][:, :, 0:2], kg01[:].rearrange("p t n -> p n t"), 1.0, 0.0, ALU.mult, ALU.add)
+        nc.scalar.activation(kgrp[1][:, :, 0], kb[0][:].indirect(idx[:, HALF // 16 : N // 16]), ACT.Copy)
+        for c in range(PACK):
+            cols = slice(c % 2 * QUARTER, (c % 2 + 1) * QUARTER)
+            part = idx[:, c * QUARTER // 16 : (c + 1) * QUARTER // 16]
+            if c < 2:
+                nc.vector.tensor_copy(kg23[:, c, 0, :], kp2[:].indirect(part))
+            else:
+                nc.scalar.activation(kg23[:, c, 0, :], kb2[:].indirect(part), ACT.Copy)
+            nc.vector.tensor_copy(kg23[:, c, 1, :], kp3[:].indirect(part))
+            nc.gpsimd.tensor_scalar(kgrp[c // 2][:, cols, 2:4], kg23[:, c, :, :].rearrange("p t n -> p n t"), 1.0, 0.0, ALU.mult, ALU.add)
+        nc.scalar.activation(kgrp[1][:, :, 1], kb[1][:].indirect(idx[:, HALF // 16 : N // 16]), ACT.Copy)
         qcodes = keep.tile([P, NQ], U32, name="qcodes", align_bytes=64)
         nc.vector.quantize_mx(out=qcodes[:].bitcast(FP8X4), scales=qscale[:], in_=qgrp[:].rearrange("p q t -> p (q t)"))
-        for lo, hi in ((0, HALF), (HALF, HALF + QUARTER), (HALF + QUARTER, N)):
-            cols = slice(lo, hi)
-            for t in range(2):
-                nc.vector.tensor_copy(kg23[:, t, cols], kp[2 + t][:].indirect(idx[:, lo // 16 : hi // 16]))
-            nc.gpsimd.tensor_scalar(kgrp[:, cols, 2:4], kg23[:, :, cols].rearrange("p t n -> p n t"), 1.0, 0.0, ALU.mult, ALU.add)
-        vb0 = keep.tile([P, T], BF16, name="vb0", align_bytes=64)
-        vb1 = keep.tile([P, T], BF16, name="vb1", tag="stage1", align_bytes=64)
-        nc.scalar.copy(vb0[:], vp0[:])
-        nc.scalar.copy(vb1[:], vp1[:])
-        ksb = late.tile([P, N], F32, name="ksb", tag="ksb", align_bytes=64, offset=1024)
+        nc.vector.tensor_copy(vp[0][:].indirect(place[:]), newv[0][:])
+        kcodes = keep.tile([P, N], U32, name="kcodes", tag="newv0", align_bytes=64)
+        for h in range(2):
+            cols = slice(h * HALF, (h + 1) * HALF)
+            nc.vector.quantize_mx(out=kcodes[:, cols].bitcast(FP8X4), scales=kscale[:, cols], in_=kgrp[h][:].rearrange("p n t -> p (n t)"))
+        nc.vector.tensor_copy(vp[1][:].indirect(place[:]), newv[1][:])
+        vst = late.tile([P, PACK], F32, name="vst", tag="vst", offset=0)
+        ksb = late.tile([P, N], F32, name="ksb", tag="ksb", offset=1024)
         nc.scalar.copy(ksb[:], ksrow[:])
-        nc.vector.tensor_copy(vb0[:].indirect(place[:]), newvb[:, 0, :])
-        kcodes = keep.tile([P, N], U32, name="kcodes", tag="vpool0", align_bytes=64)
-        nc.vector.quantize_mx(out=kcodes[:].bitcast(FP8X4), scales=kscale[:], in_=kgrp[:].rearrange("p n t -> p (n t)"))
-        nc.vector.tensor_copy(vb1[:].indirect(place[:]), newvb[:, 1, :])
-        vgs = [late.tile([P, N], BF16, name="vg0", offset=0), keep.tile([P, N], BF16, name="vg1")]
+        nc.scalar.copy(vst[:], vsps[:, :, P - 1])
+        vb0 = keep.tile([P, T], BF16, name="vb0", tag="vb0")
+        nc.scalar.copy(vb0[:], vp[0][:])
+        vgs = [keep.tile([P, N], BF16, name="vg0"), late.tile([P, N], BF16, name="vg1", tag="ksb", offset=1024)]
         nc.scalar.activation(vgs[0][:], vb0[:].indirect(idx[:]), ACT.Copy)
-        nc.scalar.activation(vgs[1][:], vb1[:].indirect(idx[:]), ACT.Copy)
         scores = psum.tile([P, N], F32, name="scores")
         nc.tensor.matmul_mx(
             out=scores[:],
@@ -136,7 +147,7 @@ def tile_attend_x_ks_append128_topk_kernel(tc, qT, kT, vT, new_kT, new_vT, ks, v
             stop=True,
         )
 
-        a = keep.tile([P, PACK, P], F32, name="a")
+        a = keep.tile([P, PACK, P], F32, name="a", tag="newv1", align_bytes=64)
         bias = keep.tile([P, 1], F32, name="bias")
         for h in range(2):
             cols = slice(h * HALF, (h + 1) * HALF)
@@ -147,26 +158,12 @@ def tile_attend_x_ks_append128_topk_kernel(tc, qT, kT, vT, new_kT, new_vT, ks, v
                 ALU.mult,
             )
         nc.vector.tensor_reduce(bias[:], a[:], AX.XY, ALU.max, negate=True)
-        p = keep.tile([P, PACK, P], F32, name="p", tag="stage1", align_bytes=64)
+        nc.vector.tensor_copy(vgs[1][:], vp[1][:].indirect(idx[:]))
+        p = keep.tile([P, PACK, P], F32, name="p", tag="vb0")
         sums = keep.tile([P, 2], F32, name="sums")
         for h in range(2):
             ts = slice(2 * h, 2 * h + 2)
             nc.scalar.activation(p[:, ts, :], a[:, ts, :], ACT.Exp, bias=bias[:], scale=1.0, accum_out=sums[:, h : h + 1])
-
-        vgrp = late.tile([P, DV * PACK], BF16, name="vgrp", tag="ksb", align_bytes=64, offset=1024)
-        vcodes = keep.tile([P, DV], U32, name="vcodes", align_bytes=64)
-        vscale = keep.tile([P, DV], U8, name="vscale", align_bytes=64)
-        for b in range(2):
-            vps = psum.tile([P, 2, P], F32, name="vps%d" % b)
-            for u in range(2):
-                nc.tensor.transpose(vps[:, u, :], vgs[b][:].bitcast(F32)[:, u : N // 2 : 2], identf[:])
-            nc.vector.tensor_copy(
-                vgrp[:, b * P * PACK : (b + 1) * P * PACK].bitcast(F32).rearrange("s (e u) -> s e u", u=2),
-                vps[:].rearrange("s u e -> s e u"),
-            )
-        for b in range(2):
-            cols = slice(b * P, (b + 1) * P)
-            nc.vector.quantize_mx(out=vcodes[:, cols].bitcast(FP8X4), scales=vscale[:, cols], in_=vgrp[:, b * P * PACK : (b + 1) * P * PACK])
 
         wgrp = keep.tile([P, NQ, PACK], BF16, name="wgrp", align_bytes=64)
         for h in range(2):
@@ -175,13 +172,30 @@ def tile_attend_x_ks_append128_topk_kernel(tc, qT, kT, vT, new_kT, new_vT, ks, v
                 nc.tensor.transpose(pps[:, j, :], p[:, 2 * h + j, :], identf[:])
             ts = slice(2 * h, 2 * h + 2)
             nc.vector.tensor_tensor(wgrp[:, :, ts], pps[:].rearrange("s t q -> s q t"), vst[:, ts].unsqueeze(1).to_broadcast([P, NQ, 2]), ALU.mult)
+
+        vgrp = keep.tile([P, DV * PACK], BF16, name="vgrp", tag="newv1", align_bytes=64)
+        vcodes = keep.tile([P, DV], U32, name="vcodes", align_bytes=64)
+        vscale = keep.tile([P, DV], U8, name="vscale", align_bytes=64)
         wcodes = keep.tile([P, NQ], U32, name="wcodes", align_bytes=64)
         wscale = keep.tile([P, NQ], U8, name="wscale", align_bytes=64)
-        nc.vector.quantize_mx(out=wcodes[:].bitcast(FP8X4), scales=wscale[:], in_=wgrp[:].rearrange("p q t -> p (q t)"))
-        total = keep.tile([P, 1], F32, name="total", tag="stage0", align_bytes=64)
-        nc.vector.tensor_tensor(total[:], sums[:, 0:1], sums[:, 1:2], ALU.add)
+        for b in range(2):
+            vps = psum.tile([P, 2, P], F32, name="vps", tag="vps")
+            for u in range(2):
+                nc.tensor.transpose(vps[:, u, :], vgs[b][:].bitcast(F32)[:, u : N // 2 : 2], identf[:])
+            nc.scalar.copy(
+                vgrp[:, b * P * PACK : (b + 1) * P * PACK].bitcast(F32).rearrange("s (e u) -> s e u", u=2),
+                vps[:].rearrange("s u e -> s e u"),
+            )
+            if b == 1:
+                nc.vector.quantize_mx(out=wcodes[:].bitcast(FP8X4), scales=wscale[:], in_=wgrp[:].rearrange("p q t -> p (q t)"))
+            cols = slice(b * P, (b + 1) * P)
+            nc.vector.quantize_mx(out=vcodes[:, cols].bitcast(FP8X4), scales=vscale[:, cols], in_=vgrp[:, b * P * PACK : (b + 1) * P * PACK])
+        total = keep.tile([P, 1], F32, name="total")
+        nc.gpsimd.tensor_tensor(total[:], sums[:, 0:1], sums[:, 1:2], ALU.add)
+        minus_one = keep.tile([P, 1], F32, name="minus_one")
+        nc.gpsimd.memset(minus_one[:], -1.0)
         recip = keep.tile([P, 1], F32, name="recip")
-        nc.vector.reciprocal(recip[:], total[:])
+        nc.gpsimd.tensor_tensor(recip[:], total[:], minus_one[:], ALU.pow)
         o_sb = keep.tile([P, DV], F32, name="o_sb")
         for h in range(2):
             cols = slice(h * P, (h + 1) * P)

@@ -41,7 +41,7 @@ def tile_attend_x_ks_append128_topk_kernel(tc, qT, kT, vT, new_kT, new_vT, ks, v
         idx = keep.tile([P, N // 16], U16, name="idx")
         newk01 = keep.tile([P, 2, NEW], F32, name="newk01")
         newk23 = late.tile([P, 2, NEW], F32, name="newk23", offset=8192)
-        newv = [keep.tile([P, NEW], F32, name="newv%d" % b, tag="newv%d" % b, align_bytes=64) for b in range(2)]
+        newv = [keep.tile([P, NEW], F32, name="newv0", tag="newv0", align_bytes=64), late.tile([P, NEW], F32, name="newv1", offset=12800)]
         khalf = [[keep.tile([P, T // 2], F32, name="khalf%d%d" % (t, h)) for h in range(2)] for t in range(1)]
         khalf.append([keep.tile([P, T // 2], F32, name="khalf10"), late.tile([P, T // 2], F32, name="khalf11", offset=4096)])
         kp2 = keep.tile([P, T], F32, name="kp2")
@@ -128,15 +128,13 @@ def tile_attend_x_ks_append128_topk_kernel(tc, qT, kT, vT, new_kT, new_vT, ks, v
             cols = slice(h * HALF, (h + 1) * HALF)
             nc.vector.quantize_mx(out=kcodes[:, cols].bitcast(FP8X4), scales=kscale[:, cols], in_=kgrp[h][:].rearrange("p n t -> p (n t)"))
         nc.vector.tensor_copy(vp[1][:].indirect(place[:]), newv[1][:])
-        vst = late.tile([P, PACK], F32, name="vst", tag="vst", offset=0)
         ksb = late.tile([P, N], F32, name="ksb", tag="ksb", offset=1024)
         nc.scalar.copy(ksb[:], ksrow[:])
-        nc.scalar.copy(vst[:], vsps[:, :, P - 1])
         vb0 = keep.tile([P, T], BF16, name="vb0", tag="vb0")
         nc.scalar.copy(vb0[:], vp[0][:])
         vgs = [keep.tile([P, N], BF16, name="vg0"), late.tile([P, N], BF16, name="vg1", tag="ksb", offset=1024)]
         nc.scalar.activation(vgs[0][:], vb0[:].indirect(idx[:]), ACT.Copy)
-        scores = psum.tile([P, N], F32, name="scores")
+        scores = psum.tile([P, N], F32, name="scores", tag="scores")
         nc.tensor.matmul_mx(
             out=scores[:],
             lhsT=qcodes[:].bitcast(FP8X4),
@@ -147,7 +145,7 @@ def tile_attend_x_ks_append128_topk_kernel(tc, qT, kT, vT, new_kT, new_vT, ks, v
             stop=True,
         )
 
-        a = keep.tile([P, PACK, P], F32, name="a", tag="newv1", align_bytes=64)
+        a = late.tile([P, PACK, P], F32, name="a", offset=12800)
         bias = keep.tile([P, 1], F32, name="bias")
         for h in range(2):
             cols = slice(h * HALF, (h + 1) * HALF)
@@ -165,6 +163,8 @@ def tile_attend_x_ks_append128_topk_kernel(tc, qT, kT, vT, new_kT, new_vT, ks, v
             ts = slice(2 * h, 2 * h + 2)
             nc.scalar.activation(p[:, ts, :], a[:, ts, :], ACT.Exp, bias=bias[:], scale=1.0, accum_out=sums[:, h : h + 1])
 
+        vst = late.tile([P, PACK], F32, name="vst", offset=12800)
+        nc.scalar.copy(vst[:], vsps[:, :, P - 1])
         wgrp = keep.tile([P, NQ, PACK], BF16, name="wgrp", align_bytes=64)
         for h in range(2):
             pps = psum.tile([P, 2, NQ], F32, name="pps%d" % h)
@@ -173,13 +173,13 @@ def tile_attend_x_ks_append128_topk_kernel(tc, qT, kT, vT, new_kT, new_vT, ks, v
             ts = slice(2 * h, 2 * h + 2)
             nc.vector.tensor_tensor(wgrp[:, :, ts], pps[:].rearrange("s t q -> s q t"), vst[:, ts].unsqueeze(1).to_broadcast([P, NQ, 2]), ALU.mult)
 
-        vgrp = keep.tile([P, DV * PACK], BF16, name="vgrp", tag="newv1", align_bytes=64)
+        vgrp = late.tile([P, DV * PACK], BF16, name="vgrp", align_bytes=64, offset=12800 + 64)
         vcodes = keep.tile([P, DV], U32, name="vcodes", align_bytes=64)
         vscale = keep.tile([P, DV], U8, name="vscale", align_bytes=64)
         wcodes = keep.tile([P, NQ], U32, name="wcodes", align_bytes=64)
         wscale = keep.tile([P, NQ], U8, name="wscale", align_bytes=64)
         for b in range(2):
-            vps = psum.tile([P, 2, P], F32, name="vps", tag="vps")
+            vps = psum.tile([P, 2, P], F32, name="vps%d" % b, tag=("vps", "bank1")[b])
             for u in range(2):
                 nc.tensor.transpose(vps[:, u, :], vgs[b][:].bitcast(F32)[:, u : N // 2 : 2], identf[:])
             nc.scalar.copy(
@@ -192,14 +192,12 @@ def tile_attend_x_ks_append128_topk_kernel(tc, qT, kT, vT, new_kT, new_vT, ks, v
             nc.vector.quantize_mx(out=vcodes[:, cols].bitcast(FP8X4), scales=vscale[:, cols], in_=vgrp[:, b * P * PACK : (b + 1) * P * PACK])
         total = keep.tile([P, 1], F32, name="total")
         nc.gpsimd.tensor_tensor(total[:], sums[:, 0:1], sums[:, 1:2], ALU.add)
-        minus_one = keep.tile([P, 1], F32, name="minus_one")
-        nc.gpsimd.memset(minus_one[:], -1.0)
         recip = keep.tile([P, 1], F32, name="recip")
-        nc.gpsimd.tensor_tensor(recip[:], total[:], minus_one[:], ALU.pow)
+        nc.vector.reciprocal(recip[:], total[:])
         o_sb = keep.tile([P, DV], F32, name="o_sb")
         for h in range(2):
             cols = slice(h * P, (h + 1) * P)
-            ps_out = psum.tile([P, P], F32, name="ps_out%d" % h, tag="bank%d" % h)
+            ps_out = psum.tile([P, P], F32, name="ps_out%d" % h, tag=("bank0", "scores")[h])
             nc.tensor.matmul_mx(
                 out=ps_out[:],
                 lhsT=wcodes[:].bitcast(FP8X4),

@@ -113,7 +113,11 @@ def tile_attend_x_ks_append128_topk_kernel(tc, qT, kT, vT, new_kT, new_vT, ks, v
         for c in range(PACK):
             cols = slice(c % 2 * QUARTER, (c % 2 + 1) * QUARTER)
             part = idx[:, c * QUARTER // 16 : (c + 1) * QUARTER // 16]
-            if c < 2:
+            if c == PACK - 1:
+                nc.vector.tensor_copy(kgrp[1][:, cols, 2], kp2[:].indirect(part))
+                nc.vector.tensor_copy(kgrp[1][:, cols, 3], kp3[:].indirect(part))
+                continue
+            if c == 0:
                 nc.vector.tensor_copy(kg23[:, c, 0, :], kp2[:].indirect(part))
             else:
                 nc.scalar.activation(kg23[:, c, 0, :], kb2[:].indirect(part), ACT.Copy)

@@ -151,14 +151,12 @@ def tile_attend_x_ks_append128_topk_kernel(tc, qT, kT, vT, new_kT, new_vT, ks, v
 
         a = late.tile([P, PACK, P], F32, name="a", offset=12800)
         bias = keep.tile([P, 1], F32, name="bias")
-        for h in range(2):
-            cols = slice(h * HALF, (h + 1) * HALF)
-            nc.vector.tensor_tensor(
-                a[:, :, h * HALF // PACK : (h + 1) * HALF // PACK].rearrange("q t s -> q s t"),
-                scores[:, cols].rearrange("q (s t) -> q s t", t=PACK),
-                ksb[:, cols].rearrange("q (s t) -> q s t", t=PACK),
-                ALU.mult,
-            )
+        nc.vector.tensor_tensor(
+            a[:].rearrange("q t s -> q s t"),
+            scores[:].rearrange("q (s t) -> q s t", t=PACK),
+            ksb[:].rearrange("q (s t) -> q s t", t=PACK),
+            ALU.mult,
+        )
         nc.vector.tensor_reduce(bias[:], a[:], AX.XY, ALU.max, negate=True)
         nc.vector.tensor_copy(vgs[1][:], vp[1][:].indirect(idx[:]))
         p = keep.tile([P, PACK, P], F32, name="p", tag="vb0")
@@ -170,12 +168,10 @@ def tile_attend_x_ks_append128_topk_kernel(tc, qT, kT, vT, new_kT, new_vT, ks, v
         vst = late.tile([P, PACK], F32, name="vst", offset=12800)
         nc.scalar.copy(vst[:], vsps[:, :, P - 1])
         wgrp = keep.tile([P, NQ, PACK], BF16, name="wgrp", align_bytes=64)
-        for h in range(2):
-            pps = psum.tile([P, 2, NQ], F32, name="pps%d" % h)
-            for j in range(2):
-                nc.tensor.transpose(pps[:, j, :], p[:, 2 * h + j, :], identf[:])
-            ts = slice(2 * h, 2 * h + 2)
-            nc.vector.tensor_tensor(wgrp[:, :, ts], pps[:].rearrange("s t q -> s q t"), vst[:, ts].unsqueeze(1).to_broadcast([P, NQ, 2]), ALU.mult)
+        pps = psum.tile([P, PACK, NQ], F32, name="pps")
+        for t in range(PACK):
+            nc.tensor.transpose(pps[:, t, :], p[:, t, :], identf[:])
+        nc.vector.tensor_tensor(wgrp[:], pps[:].rearrange("s t q -> s q t"), vst[:].unsqueeze(1).to_broadcast([P, NQ, PACK]), ALU.mult)
 
         vgrp = late.tile([P, DV * PACK], BF16, name="vgrp", align_bytes=64, offset=12800 + 64)
         vcodes = keep.tile([P, DV], U32, name="vcodes", align_bytes=64)

@@ -30,7 +30,6 @@ def tile_attend_x_ks_append128_topk_kernel(tc, qT, kT, vT, new_kT, new_vT, ks, v
     with ExitStack() as ctx:
         keep = ctx.enter_context(tc.tile_pool(name="keep", bufs=1))
         psum = ctx.enter_context(tc.psum_pool(name="psum", bufs=1))
-
         late = ctx.enter_context(tc.tile_pool(name="late", bufs=1))
 
         kview = kT.rearrange("(p t) n -> p t n", t=PACK)
@@ -39,14 +38,13 @@ def tile_attend_x_ks_append128_topk_kernel(tc, qT, kT, vT, new_kT, new_vT, ks, v
         newvview = new_vT.rearrange("(b p) n -> p b n", b=2)
         place = keep.tile([P, NEW // 16], U16, name="place")
         idx = keep.tile([P, N // 16], U16, name="idx")
-        newk01 = keep.tile([P, 2, NEW], F32, name="newk01")
-        newk23 = late.tile([P, 2, NEW], F32, name="newk23", offset=8192)
-        newv = [keep.tile([P, NEW], F32, name="newv0", tag="newv0", align_bytes=64), late.tile([P, NEW], F32, name="newv1", offset=12800)]
-        khalf = [[keep.tile([P, T // 2], F32, name="khalf%d%d" % (t, h)) for h in range(2)] for t in range(1)]
-        khalf.append([keep.tile([P, T // 2], F32, name="khalf10"), late.tile([P, T // 2], F32, name="khalf11", offset=4096)])
-        kp2 = keep.tile([P, T], F32, name="kp2")
+        newk012 = keep.tile([P, 3, NEW], F32, name="newk012")
+        newk3 = keep.tile([P, NEW], F32, name="newk3")
+        newv = [keep.tile([P, NEW], F32, name="newv0"), late.tile([P, NEW], F32, name="newv1", offset=16384)]
+        khalf = [[keep.tile([P, T // 2], F32, name="khalf%d%d" % (t, h)) for h in range(2)] for t in range(2)]
+        khalf.append([keep.tile([P, T // 2], F32, name="khalf20"), late.tile([P, T // 2], F32, name="khalf21", offset=0)])
         kp3 = keep.tile([P, T], F32, name="kp3")
-        vp = [keep.tile([P, T], F32, name="vpool%d" % b) for b in range(2)]
+        vp = [late.tile([P, T], F32, name="vpool0", offset=10240), keep.tile([P, T], F32, name="vpool1")]
         q_sb = keep.tile([P, PACK, NQ], F32, name="q_sb")
         ks_sb = keep.tile([P, T], F32, name="ks_sb")
         vs_sb = keep.tile([P, T], F32, name="vs_sb")
@@ -57,17 +55,18 @@ def tile_attend_x_ks_append128_topk_kernel(tc, qT, kT, vT, new_kT, new_vT, ks, v
         nc.sync.dma_start(vs_sb[P - 1 : P, :], vs[0:1, :])
         for h in range(2):
             nc.sync.dma_start(khalf[0][h][:], kview[:, 0, h * T // 2 : (h + 1) * T // 2])
-        nc.sync.dma_start(newk01[:], newkview[:, 0:2, :])
+        nc.sync.dma_start(newk012[:], newkview[:, 0:3, :])
         nc.sync.dma_start(place[:], slots)
-        for h in range(2):
-            nc.sync.dma_start(khalf[1][h][:], kview[:, 1, h * T // 2 : (h + 1) * T // 2])
-        nc.sync.dma_start(newk23[:], newkview[:, 2:4, :])
-        nc.sync.dma_start(kp2[:], kview[:, 2, :])
-        nc.sync.dma_start(kp3[:], kview[:, 3, :])
+        for t in range(1, 3):
+            for h in range(2):
+                nc.sync.dma_start(khalf[t][h][:], kview[:, t, h * T // 2 : (h + 1) * T // 2])
         nc.sync.dma_start(q_sb[:], qT[0].rearrange("(p t) q -> p t q", t=PACK))
-        for b in range(2):
-            nc.sync.dma_start(newv[b][:], newvview[:, b, :])
-            nc.sync.dma_start(vp[b][:], vview[:, b, :])
+        nc.sync.dma_start(newv[0][:], newvview[:, 0, :])
+        nc.sync.dma_start(newk3[:], newkview[:, 3, :])
+        nc.sync.dma_start(kp3[:], kview[:, 3, :])
+        nc.sync.dma_start(newv[1][:], newvview[:, 1, :])
+        nc.sync.dma_start(vp[1][:], vview[:, 1, :])
+        nc.sync.dma_start(vp[0][:], vview[:, 0, :])
 
         identf = keep.tile([P, P], F32, name="identf")
         make_identity(nc, identf[:])
@@ -83,113 +82,102 @@ def tile_attend_x_ks_append128_topk_kernel(tc, qT, kT, vT, new_kT, new_vT, ks, v
         for t in range(PACK):
             nc.tensor.transpose(vsps[:, t, :], vsg[:, t:N:PACK], identf[:])
 
-        kscale = keep.tile([P, N], U8, name="kscale", align_bytes=64)
-        qscale = keep.tile([P, NQ], U8, name="qscale", align_bytes=64)
-        kb = [keep.tile([P, T], BF16, name="kb%d" % t) for t in range(2)]
-        newkb = keep.tile([P, 2, NEW], BF16, name="newkb")
-        nc.gpsimd.tensor_scalar(newkb[:], newk01[:], 1.0, 0.0, ALU.mult, ALU.add)
-        for t in range(2):
+        kb = [late.tile([P, T], BF16, name="kb0", offset=6144), keep.tile([P, T], BF16, name="kb1"), keep.tile([P, T], BF16, name="kb2")]
+        newkb = late.tile([P, 3, NEW], BF16, name="newkb", offset=4096)
+        nc.gpsimd.tensor_scalar(newkb[:], newk012[:], 1.0, 0.0, ALU.mult, ALU.add)
+        for t in range(3):
             for h in range(2):
                 nc.scalar.copy(kb[t][:, h * T // 2 : (h + 1) * T // 2], khalf[t][h][:])
             nc.vector.tensor_copy(kb[t][:].indirect(place[:]), newkb[:, t, :])
-        kst = late.tile([P, PACK], F32, name="kst", offset=4096)
+        kst = late.tile([P, PACK], F32, name="kst", offset=0)
         nc.scalar.copy(kst[:], ksps[:, :, P - 1])
-        ksrow = psum.tile([P, N], F32, name="ksrow")
-        for c in range(PACK):
-            nc.tensor.transpose(ksrow[:, c * P : (c + 1) * P], kst[:, c : c + 1].to_broadcast([P, P]), identf[:])
-        kg01 = late.tile([P, 2, HALF], BF16, name="kg01", offset=4160)
-        kgrp = [keep.tile([P, HALF, PACK], BF16, name="kgrp0", align_bytes=64), late.tile([P, HALF, PACK], BF16, name="kgrp1", align_bytes=64, offset=8192 + 512)]
-        for t in range(2):
-            nc.scalar.activation(kg01[:, t, :], kb[t][:].indirect(idx[:, 0 : HALF // 16]), ACT.Copy)
-        nc.vector.tensor_copy(kp2[:].indirect(place[:]), newk23[:, 0, :])
-        nc.vector.tensor_copy(kp3[:].indirect(place[:]), newk23[:, 1, :])
-        kb2 = late.tile([P, T], BF16, name="kb2", offset=0)
-        nc.scalar.copy(kb2[:], kp2[:])
-        kg23 = late.tile([P, PACK, 2, QUARTER], BF16, name="kg23", offset=8192 + 512 - 2048)
+        kg = [late.tile([P, PACK, HALF], BF16, name="kg%d" % h, offset=(64, 4096)[h]) for h in range(2)]
+        for h in range(2):
+            for t in range(3):
+                nc.scalar.activation(kg[h][:, t, :], kb[t][:].indirect(idx[:, h * HALF // 16 : (h + 1) * HALF // 16]), ACT.Copy)
         qgrp = keep.tile([P, NQ, PACK], BF16, name="qgrp", align_bytes=64)
         nc.gpsimd.tensor_scalar(qgrp[:], q_sb[:].rearrange("p t q -> p q t"), 1.0, 0.0, ALU.mult, ALU.add)
-        nc.gpsimd.tensor_scalar(kgrp[0][:, :, 0:2], kg01[:].rearrange("p t n -> p n t"), 1.0, 0.0, ALU.mult, ALU.add)
-        nc.scalar.activation(kgrp[1][:, :, 0], kb[0][:].indirect(idx[:, HALF // 16 : N // 16]), ACT.Copy)
-        for c in range(PACK):
-            cols = slice(c % 2 * QUARTER, (c % 2 + 1) * QUARTER)
-            part = idx[:, c * QUARTER // 16 : (c + 1) * QUARTER // 16]
-            if c == PACK - 1:
-                nc.vector.tensor_copy(kgrp[1][:, cols, 2], kp2[:].indirect(part))
-                nc.vector.tensor_copy(kgrp[1][:, cols, 3], kp3[:].indirect(part))
-                continue
-            if c == 0:
-                nc.vector.tensor_copy(kg23[:, c, 0, :], kp2[:].indirect(part))
-            else:
-                nc.scalar.activation(kg23[:, c, 0, :], kb2[:].indirect(part), ACT.Copy)
-            nc.vector.tensor_copy(kg23[:, c, 1, :], kp3[:].indirect(part))
-            nc.gpsimd.tensor_scalar(kgrp[c // 2][:, cols, 2:4], kg23[:, c, :, :].rearrange("p t n -> p n t"), 1.0, 0.0, ALU.mult, ALU.add)
-        nc.scalar.activation(kgrp[1][:, :, 1], kb[1][:].indirect(idx[:, HALF // 16 : N // 16]), ACT.Copy)
+        newvb = keep.tile([P, NEW], BF16, name="newvb")
+        nc.gpsimd.tensor_scalar(newvb[:], newv[0][:], 1.0, 0.0, ALU.mult, ALU.add)
+        kgrp = [keep.tile([P, HALF, PACK], BF16, name="kgrp0", align_bytes=64), late.tile([P, HALF, PACK], BF16, name="kgrp1", align_bytes=64, offset=16384 + 256)]
+        nc.gpsimd.tensor_scalar(kgrp[0][:, :, 0:2], kg[0][:, 0:2, :].rearrange("p t n -> p n t"), 1.0, 0.0, ALU.mult, ALU.add)
+        vst = late.tile([P, PACK], F32, name="vst", offset=6144)
+        nc.scalar.copy(vst[:], vsps[:, :, P - 1])
         qcodes = keep.tile([P, NQ], U32, name="qcodes", align_bytes=64)
+        qscale = keep.tile([P, NQ], U8, name="qscale", align_bytes=64)
         nc.vector.quantize_mx(out=qcodes[:].bitcast(FP8X4), scales=qscale[:], in_=qgrp[:].rearrange("p q t -> p (q t)"))
-        nc.vector.tensor_copy(vp[0][:].indirect(place[:]), newv[0][:])
-        kcodes = keep.tile([P, N], U32, name="kcodes", tag="newv0", align_bytes=64)
-        for h in range(2):
-            cols = slice(h * HALF, (h + 1) * HALF)
-            nc.vector.quantize_mx(out=kcodes[:, cols].bitcast(FP8X4), scales=kscale[:, cols], in_=kgrp[h][:].rearrange("p n t -> p (n t)"))
-        nc.vector.tensor_copy(vp[1][:].indirect(place[:]), newv[1][:])
-        ksb = late.tile([P, N], F32, name="ksb", tag="ksb", offset=1024)
-        nc.scalar.copy(ksb[:], ksrow[:])
-        vb0 = keep.tile([P, T], BF16, name="vb0", tag="vb0")
-        nc.scalar.copy(vb0[:], vp[0][:])
-        vgs = [keep.tile([P, N], BF16, name="vg0"), late.tile([P, N], BF16, name="vg1", tag="ksb", offset=1024)]
-        nc.scalar.activation(vgs[0][:], vb0[:].indirect(idx[:]), ACT.Copy)
-        scores = psum.tile([P, N], F32, name="scores", tag="scores")
-        nc.tensor.matmul_mx(
-            out=scores[:],
-            lhsT=qcodes[:].bitcast(FP8X4),
-            lhsT_scale=qscale[:],
-            rhs=kcodes[:].bitcast(FP8X4),
-            rhs_scale=kscale[:],
-            start=True,
-            stop=True,
-        )
 
-        a = late.tile([P, PACK, P], F32, name="a", offset=12800)
-        bias = keep.tile([P, 1], F32, name="bias")
-        nc.vector.tensor_tensor(
-            a[:].rearrange("q t s -> q s t"),
-            scores[:].rearrange("q (s t) -> q s t", t=PACK),
-            ksb[:].rearrange("q (s t) -> q s t", t=PACK),
-            ALU.mult,
-        )
-        nc.vector.tensor_reduce(bias[:], a[:], AX.XY, ALU.max, negate=True)
-        nc.vector.tensor_copy(vgs[1][:], vp[1][:].indirect(idx[:]))
-        p = keep.tile([P, PACK, P], F32, name="p", tag="vb0")
+        nc.vector.tensor_copy(kp3[:].indirect(place[:]), newk3[:])
+        for h in range(2):
+            nc.vector.tensor_copy(kg[h][:, 3, :], kp3[:].indirect(idx[:, h * HALF // 16 : (h + 1) * HALF // 16]))
+        for u in range(2):
+            cols = slice(u * QUARTER, (u + 1) * QUARTER)
+            nc.gpsimd.tensor_scalar(kgrp[0][:, cols, 2:4], kg[0][:, 2:4, cols].rearrange("p t n -> p n t"), 1.0, 0.0, ALU.mult, ALU.add)
+        nc.vector.tensor_copy(vp[1][:].indirect(place[:]), newv[1][:])
+        vb0 = keep.tile([P, T], BF16, name="vb0")
+        nc.scalar.copy(vb0[:], vp[0][:])
+
+        kcodes = late.tile([P, N], U32, name="kcodes", align_bytes=64, offset=16384 + 256 - 2048)
+        kscale = keep.tile([P, N], U8, name="kscale", align_bytes=64)
+        turn = late.tile([P, (PACK + 1) * NQ], F32, name="turn", offset=10240)
+        a = psum.tile([P, N], F32, name="a", tag="bank4")
+        for c in range(PACK):
+            cols = slice(c * QUARTER, (c + 1) * QUARTER)
+            part = slice(c % 2 * QUARTER, (c % 2 + 1) * QUARTER)
+            nc.vector.quantize_mx(out=kcodes[:, cols].bitcast(FP8X4), scales=kscale[:, cols], in_=kgrp[c // 2][:, part, :].rearrange("p n t -> p (n t)"))
+            if c == 0:
+                for u in range(2):
+                    run = slice(u * QUARTER, (u + 1) * QUARTER)
+                    nc.vector.tensor_copy(kgrp[1][:, run, :], kg[1][:, :, run].rearrange("p t n -> p n t"))
+            scores = psum.tile([P, NQ], F32, name="scores%d" % c, tag="bank%d" % c)
+            nc.tensor.matmul_mx(
+                out=scores[:],
+                lhsT=kcodes[:, cols].bitcast(FP8X4),
+                lhsT_scale=kscale[:, cols],
+                rhs=qcodes[:].bitcast(FP8X4),
+                rhs_scale=qscale[:],
+                start=True,
+                stop=True,
+            )
+            aT = turn[:, (PACK - c) * NQ : (PACK - c + 1) * NQ]
+            nc.scalar.activation(aT, scores[:], ACT.Copy, scale=kst[:, c : c + 1])
+            nc.tensor.transpose(a[:, cols], aT, identf[:])
+
+        nc.vector.tensor_copy(vb0[:].indirect(place[:]), newvb[:])
+        vg0 = keep.tile([P, N], BF16, name="vg0")
+        nc.scalar.activation(vg0[:], vb0[:].indirect(idx[:]), ACT.Copy)
+        vwords = [vg0[:].bitcast(F32), turn[:, 0 : N // 2]]
+        nc.vector.tensor_copy(turn[:, 0:NQ].bitcast(BF16), vp[1][:].indirect(idx[:, 0 : HALF // 16]))
+
+        bias = late.tile([P, 1], F32, name="bias", offset=20480)
+        nc.vector.tensor_reduce(bias[:], a[:], AX.X, ALU.max, negate=True)
+        nc.vector.tensor_copy(turn[:, NQ : 2 * NQ].bitcast(BF16), vp[1][:].indirect(idx[:, HALF // 16 : N // 16]))
+        p = late.tile([P, PACK, P], F32, name="p", offset=22528)
         sums = keep.tile([P, 2], F32, name="sums")
         for h in range(2):
             ts = slice(2 * h, 2 * h + 2)
-            nc.scalar.activation(p[:, ts, :], a[:, ts, :], ACT.Exp, bias=bias[:], scale=1.0, accum_out=sums[:, h : h + 1])
+            nc.scalar.activation(p[:, ts, :], a[:].rearrange("q (s t) -> q t s", t=PACK)[:, ts, :], ACT.Exp, bias=bias[:], scale=1.0, accum_out=sums[:, h : h + 1])
 
-        vst = late.tile([P, PACK], F32, name="vst", offset=12800)
-        nc.scalar.copy(vst[:], vsps[:, :, P - 1])
         wgrp = keep.tile([P, NQ, PACK], BF16, name="wgrp", align_bytes=64)
-        pps = psum.tile([P, PACK, NQ], F32, name="pps")
+        pps = psum.tile([P, PACK, NQ], F32, name="pps", tag="bank5")
         for t in range(PACK):
             nc.tensor.transpose(pps[:, t, :], p[:, t, :], identf[:])
         nc.vector.tensor_tensor(wgrp[:], pps[:].rearrange("s t q -> s q t"), vst[:].unsqueeze(1).to_broadcast([P, NQ, PACK]), ALU.mult)
 
-        vgrp = late.tile([P, DV * PACK], BF16, name="vgrp", align_bytes=64, offset=12800 + 64)
-        vcodes = keep.tile([P, DV], U32, name="vcodes", align_bytes=64)
+        vgrp = [late.tile([P, P * PACK], BF16, name="vgrp0", align_bytes=64, offset=20480), keep.tile([P, P * PACK], BF16, name="vgrp1", align_bytes=64)]
+        vcodes = late.tile([P, DV], U32, name="vcodes", align_bytes=64, offset=22528)
         vscale = keep.tile([P, DV], U8, name="vscale", align_bytes=64)
         wcodes = keep.tile([P, NQ], U32, name="wcodes", align_bytes=64)
         wscale = keep.tile([P, NQ], U8, name="wscale", align_bytes=64)
         for b in range(2):
-            vps = psum.tile([P, 2, P], F32, name="vps%d" % b, tag=("vps", "bank1")[b])
+            vps = psum.tile([P, 2, P], F32, name="vps%d" % b, tag=("bank6", "bank4")[b])
             for u in range(2):
-                nc.tensor.transpose(vps[:, u, :], vgs[b][:].bitcast(F32)[:, u : N // 2 : 2], identf[:])
-            nc.scalar.copy(
-                vgrp[:, b * P * PACK : (b + 1) * P * PACK].bitcast(F32).rearrange("s (e u) -> s e u", u=2),
-                vps[:].rearrange("s u e -> s e u"),
-            )
+                nc.tensor.transpose(vps[:, u, :], vwords[b][:, u : N // 2 : 2], identf[:])
+            nc.scalar.copy(vgrp[b][:].bitcast(F32).rearrange("s (e u) -> s e u", u=2), vps[:].rearrange("s u e -> s e u"))
             if b == 1:
                 nc.vector.quantize_mx(out=wcodes[:].bitcast(FP8X4), scales=wscale[:], in_=wgrp[:].rearrange("p q t -> p (q t)"))
             cols = slice(b * P, (b + 1) * P)
-            nc.vector.quantize_mx(out=vcodes[:, cols].bitcast(FP8X4), scales=vscale[:, cols], in_=vgrp[:, b * P * PACK : (b + 1) * P * PACK])
+            nc.vector.quantize_mx(out=vcodes[:, cols].bitcast(FP8X4), scales=vscale[:, cols], in_=vgrp[b][:])
         total = keep.tile([P, 1], F32, name="total")
         nc.gpsimd.tensor_tensor(total[:], sums[:, 0:1], sums[:, 1:2], ALU.add)
         recip = keep.tile([P, 1], F32, name="recip")
@@ -197,7 +185,7 @@ def tile_attend_x_ks_append128_topk_kernel(tc, qT, kT, vT, new_kT, new_vT, ks, v
         o_sb = keep.tile([P, DV], F32, name="o_sb")
         for h in range(2):
             cols = slice(h * P, (h + 1) * P)
-            ps_out = psum.tile([P, P], F32, name="ps_out%d" % h, tag=("bank0", "scores")[h])
+            ps_out = psum.tile([P, P], F32, name="ps_out%d" % h, tag="bank%d" % h)
             nc.tensor.matmul_mx(
                 out=ps_out[:],
                 lhsT=wcodes[:].bitcast(FP8X4),

@@ -38,14 +38,15 @@ def tile_attend_x_ks_append128_topk_kernel(tc, qT, kT, vT, new_kT, new_vT, ks, v
         newvview = new_vT.rearrange("(b p) n -> p b n", b=2)
         place = keep.tile([P, NEW // 16], U16, name="place")
         idx = keep.tile([P, N // 16], U16, name="idx")
-        newk012 = keep.tile([P, 3, NEW], F32, name="newk012")
-        newk3 = keep.tile([P, NEW], F32, name="newk3")
-        newv = [keep.tile([P, NEW], F32, name="newv0"), late.tile([P, NEW], F32, name="newv1", offset=16384)]
-        khalf = [[keep.tile([P, T // 2], F32, name="khalf%d%d" % (t, h)) for h in range(2)] for t in range(2)]
-        khalf.append([keep.tile([P, T // 2], F32, name="khalf20"), late.tile([P, T // 2], F32, name="khalf21", offset=0)])
+        newk = [keep.tile([P, 2, NEW], F32, name="newk%d" % g) for g in range(2)]
+        newv = keep.tile([P, 2, NEW], F32, name="newv")
+        khalf = [[keep.tile([P, T // 2], F32, name="khalf0%d" % h) for h in range(2)]]
+        khalf.append([keep.tile([P, T // 2], F32, name="khalf10"), late.tile([P, T // 2], F32, name="khalf11", offset=0)])
+        khalf.append([keep.tile([P, T // 2], F32, name="khalf2%d" % h) for h in range(2)])
         kp3 = keep.tile([P, T], F32, name="kp3")
-        vp = [late.tile([P, T], F32, name="vpool0", offset=10240), keep.tile([P, T], F32, name="vpool1")]
-        q_sb = keep.tile([P, PACK, NQ], F32, name="q_sb")
+        vhalf = [keep.tile([P, T // 2], F32, name="vhalf0"), late.tile([P, T // 2], F32, name="vhalf1", offset=10240)]
+        vp1 = keep.tile([P, T], F32, name="vpool1")
+        q_sb = late.tile([P, PACK, NQ], F32, name="q_sb", offset=14336)
         ks_sb = keep.tile([P, T], F32, name="ks_sb")
         vs_sb = keep.tile([P, T], F32, name="vs_sb")
         nc.gpsimd.memset(vs_sb[0 : P - 1, :], 0.0)
@@ -53,20 +54,21 @@ def tile_attend_x_ks_append128_topk_kernel(tc, qT, kT, vT, new_kT, new_vT, ks, v
         nc.sync.dma_start(ks_sb[P - 1 : P, :], ks[0:1, :])
         nc.sync.dma_start(idx[:], offs)
         nc.sync.dma_start(vs_sb[P - 1 : P, :], vs[0:1, :])
+        nc.sync.dma_start(newk[0][:], newkview[:, 0:2, :])
         for h in range(2):
             nc.sync.dma_start(khalf[0][h][:], kview[:, 0, h * T // 2 : (h + 1) * T // 2])
-        nc.sync.dma_start(newk012[:], newkview[:, 0:3, :])
         nc.sync.dma_start(place[:], slots)
-        for t in range(1, 3):
-            for h in range(2):
-                nc.sync.dma_start(khalf[t][h][:], kview[:, t, h * T // 2 : (h + 1) * T // 2])
-        nc.sync.dma_start(q_sb[:], qT[0].rearrange("(p t) q -> p t q", t=PACK))
-        nc.sync.dma_start(newv[0][:], newvview[:, 0, :])
-        nc.sync.dma_start(newk3[:], newkview[:, 3, :])
+        for h in range(2):
+            nc.sync.dma_start(khalf[1][h][:], kview[:, 1, h * T // 2 : (h + 1) * T // 2])
+        nc.sync.dma_start(newk[1][:], newkview[:, 2:4, :])
+        for h in range(2):
+            nc.sync.dma_start(khalf[2][h][:], kview[:, 2, h * T // 2 : (h + 1) * T // 2])
         nc.sync.dma_start(kp3[:], kview[:, 3, :])
-        nc.sync.dma_start(newv[1][:], newvview[:, 1, :])
-        nc.sync.dma_start(vp[1][:], vview[:, 1, :])
-        nc.sync.dma_start(vp[0][:], vview[:, 0, :])
+        nc.sync.dma_start(q_sb[:], qT[0].rearrange("(p t) q -> p t q", t=PACK))
+        nc.sync.dma_start(newv[:], newvview)
+        for h in range(2):
+            nc.sync.dma_start(vhalf[h][:], vview[:, 0, h * T // 2 : (h + 1) * T // 2])
+        nc.sync.dma_start(vp1[:], vview[:, 1, :])
 
         identf = keep.tile([P, P], F32, name="identf")
         make_identity(nc, identf[:])
@@ -83,52 +85,61 @@ def tile_attend_x_ks_append128_topk_kernel(tc, qT, kT, vT, new_kT, new_vT, ks, v
             nc.tensor.transpose(vsps[:, t, :], vsg[:, t:N:PACK], identf[:])
 
         kb = [late.tile([P, T], BF16, name="kb0", offset=6144), keep.tile([P, T], BF16, name="kb1"), keep.tile([P, T], BF16, name="kb2")]
-        newkb = late.tile([P, 3, NEW], BF16, name="newkb", offset=4096)
-        nc.gpsimd.tensor_scalar(newkb[:], newk012[:], 1.0, 0.0, ALU.mult, ALU.add)
-        for t in range(3):
+        newkb01 = keep.tile([P, 2, NEW], BF16, name="newkb01")
+        nc.gpsimd.tensor_scalar(newkb01[:], newk[0][:], 1.0, 0.0, ALU.mult, ALU.add)
+        newkb2 = late.tile([P, NEW], BF16, name="newkb2", offset=4096)
+        nc.gpsimd.tensor_scalar(newkb2[:], newk[1][:, 0, :], 1.0, 0.0, ALU.mult, ALU.add)
+        for t in range(2):
             for h in range(2):
                 nc.scalar.copy(kb[t][:, h * T // 2 : (h + 1) * T // 2], khalf[t][h][:])
-            nc.vector.tensor_copy(kb[t][:].indirect(place[:]), newkb[:, t, :])
+            nc.vector.tensor_copy(kb[t][:].indirect(place[:]), newkb01[:, t, :])
+        nc.scalar.copy(kb[2][:, 0 : T // 2], khalf[2][0][:])
+        nc.vector.tensor_copy(kb[2][:, T // 2 : T], khalf[2][1][:])
+        nc.vector.tensor_copy(kb[2][:].indirect(place[:]), newkb2[:])
+        kg = [keep.tile([P, PACK, HALF], BF16, name="kg0"), late.tile([P, PACK, HALF], BF16, name="kg1", offset=4096)]
         kst = late.tile([P, PACK], F32, name="kst", offset=0)
-        nc.scalar.copy(kst[:], ksps[:, :, P - 1])
-        kg = [late.tile([P, PACK, HALF], BF16, name="kg%d" % h, offset=(64, 4096)[h]) for h in range(2)]
         for h in range(2):
             for t in range(3):
                 nc.scalar.activation(kg[h][:, t, :], kb[t][:].indirect(idx[:, h * HALF // 16 : (h + 1) * HALF // 16]), ACT.Copy)
+                if h == 0 and t == 0:
+                    nc.scalar.copy(kst[:], ksps[:, :, P - 1])
         qgrp = keep.tile([P, NQ, PACK], BF16, name="qgrp", align_bytes=64)
         nc.gpsimd.tensor_scalar(qgrp[:], q_sb[:].rearrange("p t q -> p q t"), 1.0, 0.0, ALU.mult, ALU.add)
         newvb = keep.tile([P, NEW], BF16, name="newvb")
-        nc.gpsimd.tensor_scalar(newvb[:], newv[0][:], 1.0, 0.0, ALU.mult, ALU.add)
-        kgrp = [keep.tile([P, HALF, PACK], BF16, name="kgrp0", align_bytes=64), late.tile([P, HALF, PACK], BF16, name="kgrp1", align_bytes=64, offset=16384 + 256)]
-        nc.gpsimd.tensor_scalar(kgrp[0][:, :, 0:2], kg[0][:, 0:2, :].rearrange("p t n -> p n t"), 1.0, 0.0, ALU.mult, ALU.add)
+        nc.gpsimd.tensor_scalar(newvb[:], newv[:, 0, :], 1.0, 0.0, ALU.mult, ALU.add)
         vst = late.tile([P, PACK], F32, name="vst", offset=6144)
         nc.scalar.copy(vst[:], vsps[:, :, P - 1])
-        qcodes = keep.tile([P, NQ], U32, name="qcodes", align_bytes=64)
-        qscale = keep.tile([P, NQ], U8, name="qscale", align_bytes=64)
-        nc.vector.quantize_mx(out=qcodes[:].bitcast(FP8X4), scales=qscale[:], in_=qgrp[:].rearrange("p q t -> p (q t)"))
 
-        nc.vector.tensor_copy(kp3[:].indirect(place[:]), newk3[:])
+        nc.vector.tensor_copy(kp3[:].indirect(place[:]), newk[1][:, 1, :])
         for h in range(2):
             nc.vector.tensor_copy(kg[h][:, 3, :], kp3[:].indirect(idx[:, h * HALF // 16 : (h + 1) * HALF // 16]))
-        for u in range(2):
-            cols = slice(u * QUARTER, (u + 1) * QUARTER)
-            nc.gpsimd.tensor_scalar(kgrp[0][:, cols, 2:4], kg[0][:, 2:4, cols].rearrange("p t n -> p n t"), 1.0, 0.0, ALU.mult, ALU.add)
-        nc.vector.tensor_copy(vp[1][:].indirect(place[:]), newv[1][:])
         vb0 = keep.tile([P, T], BF16, name="vb0")
-        nc.scalar.copy(vb0[:], vp[0][:])
+        for h in range(2):
+            nc.scalar.copy(vb0[:, h * T // 2 : (h + 1) * T // 2], vhalf[h][:])
 
-        kcodes = late.tile([P, N], U32, name="kcodes", align_bytes=64, offset=16384 + 256 - 2048)
+        kgrp = keep.tile([P, N, PACK], BF16, name="kgrp", align_bytes=64)
+
+        def weave(c):
+            run = slice(c % 2 * QUARTER, (c % 2 + 1) * QUARTER)
+            nc.vector.tensor_copy(
+                kgrp[:, c * QUARTER : (c + 1) * QUARTER, :].rearrange("p (g i) t -> p g t i", i=PACK),
+                kg[c // 2][:, :, run].rearrange("p t (g i) -> p g t i", i=PACK),
+            )
+
+        qcodes = keep.tile([P, NQ], U32, name="qcodes", align_bytes=64)
+        qscale = keep.tile([P, NQ], U8, name="qscale", align_bytes=64)
+        kcodes = late.tile([P, N], U32, name="kcodes", align_bytes=64, offset=14336)
         kscale = keep.tile([P, N], U8, name="kscale", align_bytes=64)
-        turn = late.tile([P, (PACK + 1) * NQ], F32, name="turn", offset=10240)
+        aT = late.tile([P, PACK, NQ], F32, name="aT", offset=10240)
         a = psum.tile([P, N], F32, name="a", tag="bank4")
+        weave(0)
+        weave(1)
+        nc.vector.quantize_mx(out=qcodes[:].bitcast(FP8X4), scales=qscale[:], in_=qgrp[:].rearrange("p q t -> p (q t)"))
         for c in range(PACK):
             cols = slice(c * QUARTER, (c + 1) * QUARTER)
-            part = slice(c % 2 * QUARTER, (c % 2 + 1) * QUARTER)
-            nc.vector.quantize_mx(out=kcodes[:, cols].bitcast(FP8X4), scales=kscale[:, cols], in_=kgrp[c // 2][:, part, :].rearrange("p n t -> p (n t)"))
-            if c == 0:
-                for u in range(2):
-                    run = slice(u * QUARTER, (u + 1) * QUARTER)
-                    nc.vector.tensor_copy(kgrp[1][:, run, :], kg[1][:, :, run].rearrange("p t n -> p n t"))
+            nc.vector.quantize_mx(out=kcodes[:, cols].bitcast(FP8X4), scales=kscale[:, cols], in_=kgrp[:, cols, :].rearrange("p n t -> p (n t)"))
+            if c < 2:
+                weave(c + 2)
             scores = psum.tile([P, NQ], F32, name="scores%d" % c, tag="bank%d" % c)
             nc.tensor.matmul_mx(
                 out=scores[:],
@@ -139,19 +150,19 @@ def tile_attend_x_ks_append128_topk_kernel(tc, qT, kT, vT, new_kT, new_vT, ks, v
                 start=True,
                 stop=True,
             )
-            aT = turn[:, (PACK - c) * NQ : (PACK - c + 1) * NQ]
-            nc.scalar.activation(aT, scores[:], ACT.Copy, scale=kst[:, c : c + 1])
-            nc.tensor.transpose(a[:, cols], aT, identf[:])
+            nc.scalar.activation(aT[:, c, :], scores[:], ACT.Copy, scale=kst[:, c : c + 1])
+            nc.tensor.transpose(a[:, cols], aT[:, c, :], identf[:])
 
         nc.vector.tensor_copy(vb0[:].indirect(place[:]), newvb[:])
+        nc.vector.tensor_copy(vp1[:].indirect(place[:]), newv[:, 1, :])
         vg0 = keep.tile([P, N], BF16, name="vg0")
         nc.scalar.activation(vg0[:], vb0[:].indirect(idx[:]), ACT.Copy)
-        vwords = [vg0[:].bitcast(F32), turn[:, 0 : N // 2]]
-        nc.vector.tensor_copy(turn[:, 0:NQ].bitcast(BF16), vp[1][:].indirect(idx[:, 0 : HALF // 16]))
+        vg1 = late.tile([P, N], BF16, name="vg1", offset=10240)
+        vwords = [vg0[:].bitcast(F32), vg1[:].bitcast(F32)]
 
         bias = late.tile([P, 1], F32, name="bias", offset=20480)
         nc.vector.tensor_reduce(bias[:], a[:], AX.X, ALU.max, negate=True)
-        nc.vector.tensor_copy(turn[:, NQ : 2 * NQ].bitcast(BF16), vp[1][:].indirect(idx[:, HALF // 16 : N // 16]))
+        nc.vector.tensor_copy(vg1[:], vp1[:].indirect(idx[:]))
         p = late.tile([P, PACK, P], F32, name="p", offset=22528)
         sums = keep.tile([P, 2], F32, name="sums")
         for h in range(2):

@@ -51,12 +51,12 @@ def tile_attend_x_ks_append128_topk_kernel(tc, qT, kT, vT, new_kT, new_vT, ks, v
         vs_sb = keep.tile([P, T], F32, name="vs_sb")
         nc.gpsimd.memset(vs_sb[0 : P - 1, :], 0.0)
         nc.vector.memset(ks_sb[0 : P - 1, :], 0.0)
-        nc.sync.dma_start(ks_sb[P - 1 : P, :], ks[0:1, :])
+        nc.scalar.dma_start(ks_sb[P - 1 : P, :], ks[0:1, :])
+        nc.scalar.dma_start(vs_sb[P - 1 : P, :], vs[0:1, :])
         nc.sync.dma_start(idx[:], offs)
-        nc.sync.dma_start(vs_sb[P - 1 : P, :], vs[0:1, :])
+        nc.sync.dma_start(khalf[0][0][:], kview[:, 0, 0 : T // 2])
         nc.sync.dma_start(newk[0][:], newkview[:, 0:2, :])
-        for h in range(2):
-            nc.sync.dma_start(khalf[0][h][:], kview[:, 0, h * T // 2 : (h + 1) * T // 2])
+        nc.sync.dma_start(khalf[0][1][:], kview[:, 0, T // 2 : T])
         nc.sync.dma_start(place[:], slots)
         for h in range(2):
             nc.sync.dma_start(khalf[1][h][:], kview[:, 1, h * T // 2 : (h + 1) * T // 2])

@@ -51,10 +51,10 @@ def tile_attend_x_ks_append128_topk_kernel(tc, qT, kT, vT, new_kT, new_vT, ks, v
         vs_sb = keep.tile([P, T], F32, name="vs_sb")
         nc.gpsimd.memset(vs_sb[0 : P - 1, :], 0.0)
         nc.vector.memset(ks_sb[0 : P - 1, :], 0.0)
-        nc.scalar.dma_start(ks_sb[P - 1 : P, :], ks[0:1, :])
-        nc.scalar.dma_start(vs_sb[P - 1 : P, :], vs[0:1, :])
+        nc.sync.dma_start(ks_sb[P - 1 : P, :], ks[0:1, :])
         nc.sync.dma_start(idx[:], offs)
         nc.sync.dma_start(khalf[0][0][:], kview[:, 0, 0 : T // 2])
+        nc.sync.dma_start(vs_sb[P - 1 : P, :], vs[0:1, :])
         nc.sync.dma_start(newk[0][:], newkview[:, 0:2, :])
         nc.sync.dma_start(khalf[0][1][:], kview[:, 0, T // 2 : T])
         nc.sync.dma_start(place[:], slots)
@@ -85,24 +85,27 @@ def tile_attend_x_ks_append128_topk_kernel(tc, qT, kT, vT, new_kT, new_vT, ks, v
             nc.tensor.transpose(vsps[:, t, :], vsg[:, t:N:PACK], identf[:])
 
         kb = [late.tile([P, T], BF16, name="kb0", offset=6144), keep.tile([P, T], BF16, name="kb1"), keep.tile([P, T], BF16, name="kb2")]
-        newkb01 = keep.tile([P, 2, NEW], BF16, name="newkb01")
+        newkb01 = late.tile([P, 2, NEW], BF16, name="newkb01", offset=4096)
         nc.gpsimd.tensor_scalar(newkb01[:], newk[0][:], 1.0, 0.0, ALU.mult, ALU.add)
-        newkb2 = late.tile([P, NEW], BF16, name="newkb2", offset=4096)
+        newkb2 = keep.tile([P, NEW], BF16, name="newkb2")
         nc.gpsimd.tensor_scalar(newkb2[:], newk[1][:, 0, :], 1.0, 0.0, ALU.mult, ALU.add)
         for t in range(2):
             for h in range(2):
                 nc.scalar.copy(kb[t][:, h * T // 2 : (h + 1) * T // 2], khalf[t][h][:])
             nc.vector.tensor_copy(kb[t][:].indirect(place[:]), newkb01[:, t, :])
+        kg = [late.tile([P, PACK, HALF], BF16, name="kg%d" % h, offset=(64, 4096)[h]) for h in range(2)]
+
+        def gather_keys(h, t):
+            nc.scalar.activation(kg[h][:, t, :], kb[t][:].indirect(idx[:, h * HALF // 16 : (h + 1) * HALF // 16]), ACT.Copy)
+
+        gather_keys(0, 0)
+        kst = late.tile([P, PACK], F32, name="kst", offset=0)
+        nc.scalar.copy(kst[:], ksps[:, :, P - 1])
         nc.scalar.copy(kb[2][:, 0 : T // 2], khalf[2][0][:])
         nc.vector.tensor_copy(kb[2][:, T // 2 : T], khalf[2][1][:])
         nc.vector.tensor_copy(kb[2][:].indirect(place[:]), newkb2[:])
-        kg = [keep.tile([P, PACK, HALF], BF16, name="kg0"), late.tile([P, PACK, HALF], BF16, name="kg1", offset=4096)]
-        kst = late.tile([P, PACK], F32, name="kst", offset=0)
-        for h in range(2):
-            for t in range(3):
-                nc.scalar.activation(kg[h][:, t, :], kb[t][:].indirect(idx[:, h * HALF // 16 : (h + 1) * HALF // 16]), ACT.Copy)
-                if h == 0 and t == 0:
-                    nc.scalar.copy(kst[:], ksps[:, :, P - 1])
+        for h, t in ((0, 1), (1, 0), (1, 1), (0, 2), (1, 2)):
+            gather_keys(h, t)
         qgrp = keep.tile([P, NQ, PACK], BF16, name="qgrp", align_bytes=64)
         nc.gpsimd.tensor_scalar(qgrp[:], q_sb[:].rearrange("p t q -> p q t"), 1.0, 0.0, ALU.mult, ALU.add)
         newvb = keep.tile([P, NEW], BF16, name="newvb")
@@ -113,15 +116,11 @@ def tile_attend_x_ks_append128_topk_kernel(tc, qT, kT, vT, new_kT, new_vT, ks, v
         nc.vector.tensor_copy(kp3[:].indirect(place[:]), newk[1][:, 1, :])
         for h in range(2):
             nc.vector.tensor_copy(kg[h][:, 3, :], kp3[:].indirect(idx[:, h * HALF // 16 : (h + 1) * HALF // 16]))
-        vb0 = keep.tile([P, T], BF16, name="vb0")
-        for h in range(2):
-            nc.scalar.copy(vb0[:, h * T // 2 : (h + 1) * T // 2], vhalf[h][:])
-
         kgrp = keep.tile([P, N, PACK], BF16, name="kgrp", align_bytes=64)
 
         def weave(c):
             run = slice(c % 2 * QUARTER, (c % 2 + 1) * QUARTER)
-            nc.vector.tensor_copy(
+            (nc.scalar.copy if c == 0 else nc.vector.tensor_copy)(
                 kgrp[:, c * QUARTER : (c + 1) * QUARTER, :].rearrange("p (g i) t -> p g t i", i=PACK),
                 kg[c // 2][:, :, run].rearrange("p t (g i) -> p g t i", i=PACK),
             )
@@ -133,6 +132,9 @@ def tile_attend_x_ks_append128_topk_kernel(tc, qT, kT, vT, new_kT, new_vT, ks, v
         aT = late.tile([P, PACK, NQ], F32, name="aT", offset=10240)
         a = psum.tile([P, N], F32, name="a", tag="bank4")
         weave(0)
+        vb0 = keep.tile([P, T], BF16, name="vb0")
+        for h in range(2):
+            nc.scalar.copy(vb0[:, h * T // 2 : (h + 1) * T // 2], vhalf[h][:])
         weave(1)
         nc.vector.quantize_mx(out=qcodes[:].bitcast(FP8X4), scales=qscale[:], in_=qgrp[:].rearrange("p q t -> p (q t)"))
         for c in range(PACK):
@@ -158,11 +160,11 @@ def tile_attend_x_ks_append128_topk_kernel(tc, qT, kT, vT, new_kT, new_vT, ks, v
         vg0 = keep.tile([P, N], BF16, name="vg0")
         nc.scalar.activation(vg0[:], vb0[:].indirect(idx[:]), ACT.Copy)
         vg1 = late.tile([P, N], BF16, name="vg1", offset=10240)
-        vwords = [vg0[:].bitcast(F32), vg1[:].bitcast(F32)]
+        vwords = [vg0[:].bitcast(F32)[:, 0 : N // 2 : 2], vg0[:].bitcast(F32)[:, 1 : N // 2 : 2], vg1[:].bitcast(F32)[:, 0:P], vg1[:].bitcast(F32)[:, P : 2 * P]]
 
         bias = late.tile([P, 1], F32, name="bias", offset=20480)
         nc.vector.tensor_reduce(bias[:], a[:], AX.X, ALU.max, negate=True)
-        nc.vector.tensor_copy(vg1[:], vp1[:].indirect(idx[:]))
+        nc.vector.tensor_copy(vg1[:].rearrange("p (u s e) -> p s u e", u=2, e=2), vp1[:].indirect(idx[:]))
         p = late.tile([P, PACK, P], F32, name="p", offset=22528)
         sums = keep.tile([P, 2], F32, name="sums")
         for h in range(2):
@@ -183,7 +185,7 @@ def tile_attend_x_ks_append128_topk_kernel(tc, qT, kT, vT, new_kT, new_vT, ks, v
         for b in range(2):
             vps = psum.tile([P, 2, P], F32, name="vps%d" % b, tag=("bank6", "bank4")[b])
             for u in range(2):
-                nc.tensor.transpose(vps[:, u, :], vwords[b][:, u : N // 2 : 2], identf[:])
+                nc.tensor.transpose(vps[:, u, :], vwords[2 * b + u], identf[:])
             nc.scalar.copy(vgrp[b][:].bitcast(F32).rearrange("s (e u) -> s e u", u=2), vps[:].rearrange("s u e -> s e u"))
             if b == 1:
                 nc.vector.quantize_mx(out=wcodes[:].bitcast(FP8X4), scales=wscale[:], in_=wgrp[:].rearrange("p q t -> p (q t)"))

@@ -212,4 +212,4 @@ def tile_attend_x_ks_append128_topk_kernel(tc, qT, kT, vT, new_kT, new_vT, ks, v
                 nc.scalar.activation(o_sb[:, cols], ps_out[:], ACT.Copy, scale=recip[:])
             else:
                 nc.vector.tensor_scalar(o_sb[:, cols], ps_out[:], recip[:], None, ALU.mult)
-        nc.sync.dma_start(out[0], o_sb[:])
+            nc.sync.dma_start(out[0][:, cols], o_sb[:, cols])

@@ -22,6 +22,7 @@ DV = 256
 NEW = 128
 HALF = N // 2
 QUARTER = N // 4
+SHARED = 3 * N // 8
 FLOPS = 2 * NQ * N * 512 + 2 * NQ * N * DV
 
 
@@ -106,6 +107,8 @@ def tile_attend_x_ks_append128_topk_kernel(tc, qT, kT, vT, new_kT, new_vT, ks, v
         nc.vector.tensor_copy(kb[2][:].indirect(place[:]), newkb2[:])
         for h, t in ((0, 1), (1, 0), (1, 1), (0, 2), (1, 2)):
             gather_keys(h, t)
+        kgrp = keep.tile([P, N, PACK], BF16, name="kgrp", align_bytes=64)
+        nc.gpsimd.tensor_scalar(kgrp[:, 0:SHARED, 0:2], kg[0][:, 0:2, 0:SHARED].rearrange("p t n -> p n t"), 1.0, 0.0, ALU.mult, ALU.add)
         qgrp = keep.tile([P, NQ, PACK], BF16, name="qgrp", align_bytes=64)
         nc.gpsimd.tensor_scalar(qgrp[:], q_sb[:].rearrange("p t q -> p q t"), 1.0, 0.0, ALU.mult, ALU.add)
         newvb = keep.tile([P, NEW], BF16, name="newvb")
@@ -116,13 +119,12 @@ def tile_attend_x_ks_append128_topk_kernel(tc, qT, kT, vT, new_kT, new_vT, ks, v
         nc.vector.tensor_copy(kp3[:].indirect(place[:]), newk[1][:, 1, :])
         for h in range(2):
             nc.vector.tensor_copy(kg[h][:, 3, :], kp3[:].indirect(idx[:, h * HALF // 16 : (h + 1) * HALF // 16]))
-        kgrp = keep.tile([P, N, PACK], BF16, name="kgrp", align_bytes=64)
 
-        def weave(c):
-            run = slice(c % 2 * QUARTER, (c % 2 + 1) * QUARTER)
-            (nc.scalar.copy if c == 0 else nc.vector.tensor_copy)(
-                kgrp[:, c * QUARTER : (c + 1) * QUARTER, :].rearrange("p (g i) t -> p g t i", i=PACK),
-                kg[c // 2][:, :, run].rearrange("p t (g i) -> p g t i", i=PACK),
+        def weave(copy, lo, hi, first):
+            h = lo // HALF
+            copy(
+                kgrp[:, lo:hi, first:PACK].rearrange("p (g i) t -> p g t i", i=PACK),
+                kg[h][:, first:PACK, lo - h * HALF : hi - h * HALF].rearrange("p t (g i) -> p g t i", i=PACK),
             )
 
         qcodes = keep.tile([P, NQ], U32, name="qcodes", align_bytes=64)
@@ -131,17 +133,17 @@ def tile_attend_x_ks_append128_topk_kernel(tc, qT, kT, vT, new_kT, new_vT, ks, v
         kscale = keep.tile([P, N], U8, name="kscale", align_bytes=64)
         aT = late.tile([P, PACK, NQ], F32, name="aT", offset=10240)
         a = psum.tile([P, N], F32, name="a", tag="bank4")
-        weave(0)
+        weave(nc.scalar.copy, 0, SHARED, 2)
         vb0 = keep.tile([P, T], BF16, name="vb0")
         for h in range(2):
             nc.scalar.copy(vb0[:, h * T // 2 : (h + 1) * T // 2], vhalf[h][:])
-        weave(1)
+        weave(nc.vector.tensor_copy, SHARED, HALF, 0)
         nc.vector.quantize_mx(out=qcodes[:].bitcast(FP8X4), scales=qscale[:], in_=qgrp[:].rearrange("p q t -> p (q t)"))
         for c in range(PACK):
             cols = slice(c * QUARTER, (c + 1) * QUARTER)
             nc.vector.quantize_mx(out=kcodes[:, cols].bitcast(FP8X4), scales=kscale[:, cols], in_=kgrp[:, cols, :].rearrange("p n t -> p (n t)"))
             if c < 2:
-                weave(c + 2)
+                weave(nc.vector.tensor_copy, HALF + c * QUARTER, HALF + (c + 1) * QUARTER, 0)
             scores = psum.tile([P, NQ], F32, name="scores%d" % c, tag="bank%d" % c)
             nc.tensor.matmul_mx(
                 out=scores[:],

@@ -22,7 +22,8 @@ DV = 256
 NEW = 128
 HALF = N // 2
 QUARTER = N // 4
-SHARED = 3 * N // 8
+SHARED = 5 * N // 16
+VCUT = 3 * T // 4
 FLOPS = 2 * NQ * N * 512 + 2 * NQ * N * DV
 
 
@@ -45,7 +46,7 @@ def tile_attend_x_ks_append128_topk_kernel(tc, qT, kT, vT, new_kT, new_vT, ks, v
         khalf.append([keep.tile([P, T // 2], F32, name="khalf10"), late.tile([P, T // 2], F32, name="khalf11", offset=0)])
         khalf.append([keep.tile([P, T // 2], F32, name="khalf2%d" % h) for h in range(2)])
         kp3 = keep.tile([P, T], F32, name="kp3")
-        vhalf = [keep.tile([P, T // 2], F32, name="vhalf0"), late.tile([P, T // 2], F32, name="vhalf1", offset=10240)]
+        vpart = [keep.tile([P, VCUT], F32, name="vpart0"), late.tile([P, T - VCUT], F32, name="vpart1", offset=10240)]
         vp1 = keep.tile([P, T], F32, name="vpool1")
         q_sb = late.tile([P, PACK, NQ], F32, name="q_sb", offset=14336)
         ks_sb = keep.tile([P, T], F32, name="ks_sb")
@@ -67,8 +68,8 @@ def tile_attend_x_ks_append128_topk_kernel(tc, qT, kT, vT, new_kT, new_vT, ks, v
         nc.sync.dma_start(kp3[:], kview[:, 3, :])
         nc.sync.dma_start(q_sb[:], qT[0].rearrange("(p t) q -> p t q", t=PACK))
         nc.sync.dma_start(newv[:], newvview)
-        for h in range(2):
-            nc.sync.dma_start(vhalf[h][:], vview[:, 0, h * T // 2 : (h + 1) * T // 2])
+        nc.sync.dma_start(vpart[0][:], vview[:, 0, 0:VCUT])
+        nc.sync.dma_start(vpart[1][:], vview[:, 0, VCUT:T])
         nc.sync.dma_start(vp1[:], vview[:, 1, :])
 
         identf = keep.tile([P, P], F32, name="identf")
@@ -135,8 +136,8 @@ def tile_attend_x_ks_append128_topk_kernel(tc, qT, kT, vT, new_kT, new_vT, ks, v
         a = psum.tile([P, N], F32, name="a", tag="bank4")
         weave(nc.scalar.copy, 0, SHARED, 2)
         vb0 = keep.tile([P, T], BF16, name="vb0")
-        for h in range(2):
-            nc.scalar.copy(vb0[:, h * T // 2 : (h + 1) * T // 2], vhalf[h][:])
+        nc.scalar.copy(vb0[:, 0:VCUT], vpart[0][:])
+        nc.scalar.copy(vb0[:, VCUT:T], vpart[1][:])
         weave(nc.vector.tensor_copy, SHARED, HALF, 0)
         nc.vector.quantize_mx(out=qcodes[:].bitcast(FP8X4), scales=qscale[:], in_=qgrp[:].rearrange("p q t -> p (q t)"))
         for c in range(PACK):

@@ -62,9 +62,9 @@ def tile_attend_x_ks_append128_topk_kernel(tc, qT, kT, vT, new_kT, new_vT, ks, v
         nc.sync.dma_start(place[:], slots)
         for h in range(2):
             nc.sync.dma_start(khalf[1][h][:], kview[:, 1, h * T // 2 : (h + 1) * T // 2])
+        nc.sync.dma_start(khalf[2][0][:], kview[:, 2, 0 : T // 2])
         nc.sync.dma_start(newk[1][:], newkview[:, 2:4, :])
-        for h in range(2):
-            nc.sync.dma_start(khalf[2][h][:], kview[:, 2, h * T // 2 : (h + 1) * T // 2])
+        nc.sync.dma_start(khalf[2][1][:], kview[:, 2, T // 2 : T])
         nc.sync.dma_start(kp3[:], kview[:, 3, :])
         nc.sync.dma_start(q_sb[:], qT[0].rearrange("(p t) q -> p t q", t=PACK))
         nc.sync.dma_start(newv[:], newvview)

@@ -22,7 +22,7 @@ DV = 256
 NEW = 128
 HALF = N // 2
 QUARTER = N // 4
-SHARED = 5 * N // 16
+SHARED = N // 4
 VCUT = 3 * T // 4
 FLOPS = 2 * NQ * N * 512 + 2 * NQ * N * DV
 
@@ -79,12 +79,11 @@ def tile_attend_x_ks_append128_topk_kernel(tc, qT, kT, vT, new_kT, new_vT, ks, v
         nc.vector.tensor_copy(ksg[:], ks_sb[:].indirect(idx[:]))
         vsg = keep.tile([P, N], F32, name="vsg")
         nc.vector.tensor_copy(vsg[:], vs_sb[:].indirect(idx[:]))
-        ksps = psum.tile([P, PACK, P], F32, name="ksps", tag="bank0")
-        for c in range(PACK):
-            nc.tensor.transpose(ksps[:, c, :], ksg[:, c * P : (c + 1) * P], identf[:])
-        vsps = psum.tile([P, PACK, P], F32, name="vsps", tag="bank1")
-        for t in range(PACK):
-            nc.tensor.transpose(vsps[:, t, :], vsg[:, t:N:PACK], identf[:])
+        turned = psum.tile([P, N], F32, name="turned", tag="bank0")
+        for c in reversed(range(PACK)):
+            nc.tensor.transpose(turned[:, 2 * (PACK + c) : 2 * (PACK + c) + P], ksg[:, c * P : (c + 1) * P], identf[:])
+        for t in reversed(range(PACK)):
+            nc.tensor.transpose(turned[:, 2 * t : 2 * t + P], vsg[:, t:N:PACK], identf[:])
 
         kb = [late.tile([P, T], BF16, name="kb0", offset=6144), keep.tile([P, T], BF16, name="kb1"), keep.tile([P, T], BF16, name="kb2")]
         newkb01 = late.tile([P, 2, NEW], BF16, name="newkb01", offset=4096)
@@ -95,63 +94,61 @@ def tile_attend_x_ks_append128_topk_kernel(tc, qT, kT, vT, new_kT, new_vT, ks, v
             for h in range(2):
                 nc.scalar.copy(kb[t][:, h * T // 2 : (h + 1) * T // 2], khalf[t][h][:])
             nc.vector.tensor_copy(kb[t][:].indirect(place[:]), newkb01[:, t, :])
-        kg = [late.tile([P, PACK, HALF], BF16, name="kg%d" % h, offset=(64, 4096)[h]) for h in range(2)]
+        kg0 = late.tile([P, PACK, HALF], BF16, name="kg0", offset=4096)
+        kg1 = late.tile([P, 3, HALF], BF16, name="kg1", offset=64)
+        runs = [[kg0[:, t, :] for t in range(PACK)], [kg1[:, r, :] for r in (1, 2, 0, 1)]]
 
         def gather_keys(h, t):
-            nc.scalar.activation(kg[h][:, t, :], kb[t][:].indirect(idx[:, h * HALF // 16 : (h + 1) * HALF // 16]), ACT.Copy)
+            nc.scalar.activation(runs[h][t], kb[t][:].indirect(idx[:, h * HALF // 16 : (h + 1) * HALF // 16]), ACT.Copy)
 
-        gather_keys(0, 0)
-        kst = late.tile([P, PACK], F32, name="kst", offset=0)
-        nc.scalar.copy(kst[:], ksps[:, :, P - 1])
+        gather_keys(1, 0)
         nc.scalar.copy(kb[2][:, 0 : T // 2], khalf[2][0][:])
         nc.vector.tensor_copy(kb[2][:, T // 2 : T], khalf[2][1][:])
         nc.vector.tensor_copy(kb[2][:].indirect(place[:]), newkb2[:])
-        for h, t in ((0, 1), (1, 0), (1, 1), (0, 2), (1, 2)):
+        for h, t in ((1, 1), (0, 0), (0, 1), (0, 2), (1, 2)):
             gather_keys(h, t)
-        kgrp = keep.tile([P, N, PACK], BF16, name="kgrp", align_bytes=64)
-        nc.gpsimd.tensor_scalar(kgrp[:, 0:SHARED, 0:2], kg[0][:, 0:2, 0:SHARED].rearrange("p t n -> p n t"), 1.0, 0.0, ALU.mult, ALU.add)
-        qgrp = keep.tile([P, NQ, PACK], BF16, name="qgrp", align_bytes=64)
-        nc.gpsimd.tensor_scalar(qgrp[:], q_sb[:].rearrange("p t q -> p q t"), 1.0, 0.0, ALU.mult, ALU.add)
+        qkgrp = keep.tile([P, NQ + SHARED, PACK], BF16, name="qkgrp", align_bytes=64)
+        krest = keep.tile([P, N - SHARED, PACK], BF16, name="krest", align_bytes=64)
+        khigh = krest[:, HALF - SHARED : N - SHARED, :]
+        nc.gpsimd.tensor_scalar(khigh[:, :, 0:2], kg1[:, 1:3, :].rearrange("p t n -> p n t"), 1.0, 0.0, ALU.mult, ALU.add)
+        nc.gpsimd.tensor_scalar(qkgrp[:, 0:NQ, :], q_sb[:].rearrange("p t q -> p q t"), 1.0, 0.0, ALU.mult, ALU.add)
+        nc.gpsimd.tensor_scalar(qkgrp[:, NQ : NQ + SHARED, 0:2], kg0[:, 0:2, 0:SHARED].rearrange("p t n -> p n t"), 1.0, 0.0, ALU.mult, ALU.add)
         newvb = keep.tile([P, NEW], BF16, name="newvb")
         nc.gpsimd.tensor_scalar(newvb[:], newv[:, 0, :], 1.0, 0.0, ALU.mult, ALU.add)
-        vst = late.tile([P, PACK], F32, name="vst", offset=6144)
-        nc.scalar.copy(vst[:], vsps[:, :, P - 1])
+        scales = late.tile([P, 2 * PACK], F32, name="scales", offset=6144)
+        nc.scalar.copy(scales[:], turned[:, P - 1 : P - 1 + 4 * PACK : 2])
+        vst = scales[:, 0:PACK]
+        kst = scales[:, PACK : 2 * PACK]
 
         nc.vector.tensor_copy(kp3[:].indirect(place[:]), newk[1][:, 1, :])
         for h in range(2):
-            nc.vector.tensor_copy(kg[h][:, 3, :], kp3[:].indirect(idx[:, h * HALF // 16 : (h + 1) * HALF // 16]))
+            nc.vector.tensor_copy(runs[h][3], kp3[:].indirect(idx[:, h * HALF // 16 : (h + 1) * HALF // 16]))
 
-        def weave(copy, lo, hi, first):
-            h = lo // HALF
-            copy(
-                kgrp[:, lo:hi, first:PACK].rearrange("p (g i) t -> p g t i", i=PACK),
-                kg[h][:, first:PACK, lo - h * HALF : hi - h * HALF].rearrange("p t (g i) -> p g t i", i=PACK),
-            )
+        def weave(copy, grouped, planes):
+            copy(grouped.rearrange("p (g i) t -> p g t i", i=PACK), planes.rearrange("p t (g i) -> p g t i", i=PACK))
 
-        qcodes = keep.tile([P, NQ], U32, name="qcodes", align_bytes=64)
-        qscale = keep.tile([P, NQ], U8, name="qscale", align_bytes=64)
-        kcodes = late.tile([P, N], U32, name="kcodes", align_bytes=64, offset=14336)
-        kscale = keep.tile([P, N], U8, name="kscale", align_bytes=64)
+        qkcodes = late.tile([P, NQ + N], U32, name="qkcodes", align_bytes=64, offset=14336)
+        qkscale = keep.tile([P, NQ + N], U8, name="qkscale", align_bytes=64)
         aT = late.tile([P, PACK, NQ], F32, name="aT", offset=10240)
         a = psum.tile([P, N], F32, name="a", tag="bank4")
-        weave(nc.scalar.copy, 0, SHARED, 2)
+        weave(nc.scalar.copy, qkgrp[:, NQ : NQ + SHARED, 2:PACK], kg0[:, 2:PACK, 0:SHARED])
         vb0 = keep.tile([P, T], BF16, name="vb0")
         nc.scalar.copy(vb0[:, 0:VCUT], vpart[0][:])
         nc.scalar.copy(vb0[:, VCUT:T], vpart[1][:])
-        weave(nc.vector.tensor_copy, SHARED, HALF, 0)
-        nc.vector.quantize_mx(out=qcodes[:].bitcast(FP8X4), scales=qscale[:], in_=qgrp[:].rearrange("p q t -> p (q t)"))
+        weave(nc.vector.tensor_copy, krest[:, 0 : HALF - SHARED, :], kg0[:, :, SHARED:HALF])
+        weave(nc.vector.tensor_copy, khigh[:, :, 2:PACK], kg1[:, 0:2, :])
         for c in range(PACK):
             cols = slice(c * QUARTER, (c + 1) * QUARTER)
-            nc.vector.quantize_mx(out=kcodes[:, cols].bitcast(FP8X4), scales=kscale[:, cols], in_=kgrp[:, cols, :].rearrange("p n t -> p (n t)"))
-            if c < 2:
-                weave(nc.vector.tensor_copy, HALF + c * QUARTER, HALF + (c + 1) * QUARTER, 0)
+            keys = slice(NQ + c * QUARTER, NQ + (c + 1) * QUARTER)
+            made = slice(0 if c == 0 else keys.start, keys.stop)
+            nc.vector.quantize_mx(out=qkcodes[:, made].bitcast(FP8X4), scales=qkscale[:, made], in_=(qkgrp[:] if c == 0 else krest[:, (c - 1) * QUARTER : c * QUARTER, :]).rearrange("p n t -> p (n t)"))
             scores = psum.tile([P, NQ], F32, name="scores%d" % c, tag="bank%d" % c)
             nc.tensor.matmul_mx(
                 out=scores[:],
-                lhsT=kcodes[:, cols].bitcast(FP8X4),
-                lhsT_scale=kscale[:, cols],
-                rhs=qcodes[:].bitcast(FP8X4),
-                rhs_scale=qscale[:],
+                lhsT=qkcodes[:, keys].bitcast(FP8X4),
+                lhsT_scale=qkscale[:, keys],
+                rhs=qkcodes[:, 0:NQ].bitcast(FP8X4),
+                rhs_scale=qkscale[:, 0:NQ],
                 start=True,
                 stop=True,
             )
@@ -178,7 +175,7 @@ def tile_attend_x_ks_append128_topk_kernel(tc, qT, kT, vT, new_kT, new_vT, ks, v
         pps = psum.tile([P, PACK, NQ], F32, name="pps", tag="bank5")
         for t in range(PACK):
             nc.tensor.transpose(pps[:, t, :], p[:, t, :], identf[:])
-        nc.vector.tensor_tensor(wgrp[:], pps[:].rearrange("s t q -> s q t"), vst[:].unsqueeze(1).to_broadcast([P, NQ, PACK]), ALU.mult)
+        nc.vector.tensor_tensor(wgrp[:], pps[:].rearrange("s t q -> s q t"), vst.unsqueeze(1).to_broadcast([P, NQ, PACK]), ALU.mult)
 
         vgrp = [late.tile([P, P * PACK], BF16, name="vgrp0", align_bytes=64, offset=20480), keep.tile([P, P * PACK], BF16, name="vgrp1", align_bytes=64)]
         vcodes = late.tile([P, DV], U32, name="vcodes", align_bytes=64, offset=22528)

@@ -114,7 +114,6 @@ def tile_attend_x_ks_append128_topk_kernel(tc, qT, kT, vT, new_kT, new_vT, ks, v
         nc.gpsimd.tensor_scalar(qkgrp[:, 0:NQ, :], q_sb[:].rearrange("p t q -> p q t"), 1.0, 0.0, ALU.mult, ALU.add)
         nc.gpsimd.tensor_scalar(qkgrp[:, NQ : NQ + SHARED, 0:2], kg0[:, 0:2, 0:SHARED].rearrange("p t n -> p n t"), 1.0, 0.0, ALU.mult, ALU.add)
         newvb = keep.tile([P, NEW], BF16, name="newvb")
-        nc.gpsimd.tensor_scalar(newvb[:], newv[:, 0, :], 1.0, 0.0, ALU.mult, ALU.add)
         scales = late.tile([P, 2 * PACK], F32, name="scales", offset=6144)
         nc.scalar.copy(scales[:], turned[:, P - 1 : P - 1 + 4 * PACK : 2])
         vst = scales[:, 0:PACK]
@@ -133,6 +132,7 @@ def tile_attend_x_ks_append128_topk_kernel(tc, qT, kT, vT, new_kT, new_vT, ks, v
         a = psum.tile([P, N], F32, name="a", tag="bank4")
         weave(nc.scalar.copy, qkgrp[:, NQ : NQ + SHARED, 2:PACK], kg0[:, 2:PACK, 0:SHARED])
         vb0 = keep.tile([P, T], BF16, name="vb0")
+        nc.scalar.copy(newvb[:], newv[:, 0, :])
         nc.scalar.copy(vb0[:, 0:VCUT], vpart[0][:])
         nc.scalar.copy(vb0[:, VCUT:T], vpart[1][:])
         weave(nc.vector.tensor_copy, krest[:, 0 : HALF - SHARED, :], kg0[:, :, SHARED:HALF])

from contextlib import ExitStack

import concourse.mybir as mybir
from concourse.masks import make_identity

F32 = mybir.dt.float32
BF16 = mybir.dt.bfloat16
U32 = mybir.dt.uint32
U16 = mybir.dt.uint16
U8 = mybir.dt.uint8
FP8X4 = mybir.dt.float8_e4m3fn_x4
ACT = mybir.ActivationFunctionType
ALU = mybir.AluOpType
AX = mybir.AxisListType

P = 128
PACK = 4
T = 1024
N = 512
NQ = 128
DV = 256
NEW = 128
HALF = N // 2
QUARTER = N // 4
SHARED = N // 4
VCUT = 3 * T // 4
FLOPS = 2 * NQ * N * 512 + 2 * NQ * N * DV


def tile_attend_x_ks_append128_topk_kernel(tc, qT, kT, vT, new_kT, new_vT, ks, vs, offs, slots, out):
    nc = tc.nc
    with ExitStack() as ctx:
        keep = ctx.enter_context(tc.tile_pool(name="keep", bufs=1))
        psum = ctx.enter_context(tc.psum_pool(name="psum", bufs=1))
        late = ctx.enter_context(tc.tile_pool(name="late", bufs=1))

        kview = kT.rearrange("(p t) n -> p t n", t=PACK)
        newkview = new_kT.rearrange("(p t) n -> p t n", t=PACK)
        vview = vT.rearrange("(b p) n -> p b n", b=2)
        newvview = new_vT.rearrange("(b p) n -> p b n", b=2)
        place = keep.tile([P, NEW // 16], U16, name="place")
        idx = keep.tile([P, N // 16], U16, name="idx")
        newk = [keep.tile([P, 2, NEW], F32, name="newk%d" % g) for g in range(2)]
        newv = keep.tile([P, 2, NEW], F32, name="newv")
        khalf = [[keep.tile([P, T // 2], F32, name="khalf0%d" % h) for h in range(2)]]
        khalf.append([keep.tile([P, T // 2], F32, name="khalf10"), late.tile([P, T // 2], F32, name="khalf11", offset=0)])
        khalf.append([keep.tile([P, T // 2], F32, name="khalf2%d" % h) for h in range(2)])
        kp3 = keep.tile([P, T], F32, name="kp3")
        vpart = [keep.tile([P, VCUT], F32, name="vpart0"), late.tile([P, T - VCUT], F32, name="vpart1", offset=10240)]
        vp1 = keep.tile([P, T], F32, name="vpool1")
        q_sb = late.tile([P, PACK, NQ], F32, name="q_sb", offset=14336)
        ks_sb = keep.tile([P, T], F32, name="ks_sb")
        vs_sb = keep.tile([P, T], F32, name="vs_sb")
        nc.gpsimd.memset(vs_sb[0 : P - 1, :], 0.0)
        nc.vector.memset(ks_sb[0 : P - 1, :], 0.0)
        nc.sync.dma_start(ks_sb[P - 1 : P, :], ks[0:1, :])
        nc.sync.dma_start(idx[:], offs)
        nc.sync.dma_start(khalf[0][0][:], kview[:, 0, 0 : T // 2])
        nc.sync.dma_start(vs_sb[P - 1 : P, :], vs[0:1, :])
        nc.sync.dma_start(newk[0][:], newkview[:, 0:2, :])
        nc.sync.dma_start(khalf[0][1][:], kview[:, 0, T // 2 : T])
        nc.sync.dma_start(place[:], slots)
        for h in range(2):
            nc.sync.dma_start(khalf[1][h][:], kview[:, 1, h * T // 2 : (h + 1) * T // 2])
        nc.sync.dma_start(khalf[2][0][:], kview[:, 2, 0 : T // 2])
        nc.sync.dma_start(newk[1][:], newkview[:, 2:4, :])
        nc.sync.dma_start(khalf[2][1][:], kview[:, 2, T // 2 : T])
        nc.sync.dma_start(kp3[:], kview[:, 3, :])
        nc.sync.dma_start(q_sb[:], qT[0].rearrange("(p t) q -> p t q", t=PACK))
        nc.sync.dma_start(newv[:], newvview)
        nc.sync.dma_start(vpart[0][:], vview[:, 0, 0:VCUT])
        nc.sync.dma_start(vpart[1][:], vview[:, 0, VCUT:T])
        nc.sync.dma_start(vp1[:], vview[:, 1, :])

        identf = keep.tile([P, P], F32, name="identf")
        make_identity(nc, identf[:])

        ksg = keep.tile([P, N], F32, name="ksg")
        nc.vector.tensor_copy(ksg[:], ks_sb[:].indirect(idx[:]))
        vsg = keep.tile([P, N], F32, name="vsg")
        nc.vector.tensor_copy(vsg[:], vs_sb[:].indirect(idx[:]))
        turned = psum.tile([P, N], F32, name="turned", tag="bank0")
        for c in reversed(range(PACK)):
            nc.tensor.transpose(turned[:, 2 * (PACK + c) : 2 * (PACK + c) + P], ksg[:, c * P : (c + 1) * P], identf[:])
        for t in reversed(range(PACK)):
            nc.tensor.transpose(turned[:, 2 * t : 2 * t + P], vsg[:, t:N:PACK], identf[:])

        kb = [late.tile([P, T], BF16, name="kb0", offset=6144), keep.tile([P, T], BF16, name="kb1"), keep.tile([P, T], BF16, name="kb2")]
        newkb01 = late.tile([P, 2, NEW], BF16, name="newkb01", offset=4096)
        nc.gpsimd.tensor_scalar(newkb01[:], newk[0][:], 1.0, 0.0, ALU.mult, ALU.add)
        newkb2 = keep.tile([P, NEW], BF16, name="newkb2")
        nc.gpsimd.tensor_scalar(newkb2[:], newk[1][:, 0, :], 1.0, 0.0, ALU.mult, ALU.add)
        for t in range(2):
            for h in range(2):
                nc.scalar.copy(kb[t][:, h * T // 2 : (h + 1) * T // 2], khalf[t][h][:])
            nc.vector.tensor_copy(kb[t][:].indirect(place[:]), newkb01[:, t, :])
        kg0 = late.tile([P, PACK, HALF], BF16, name="kg0", offset=4096)
        kg1 = late.tile([P, 3, HALF], BF16, name="kg1", offset=64)
        runs = [[kg0[:, t, :] for t in range(PACK)], [kg1[:, r, :] for r in (1, 2, 0, 1)]]

        def gather_keys(h, t):
            nc.scalar.activation(runs[h][t], kb[t][:].indirect(idx[:, h * HALF // 16 : (h + 1) * HALF // 16]), ACT.Copy)

        gather_keys(1, 0)
        nc.scalar.copy(kb[2][:, 0 : T // 2], khalf[2][0][:])
        nc.vector.tensor_copy(kb[2][:, T // 2 : T], khalf[2][1][:])
        nc.vector.tensor_copy(kb[2][:].indirect(place[:]), newkb2[:])
        for h, t in ((1, 1), (0, 0), (0, 1), (0, 2), (1, 2)):
            gather_keys(h, t)
        qkgrp = keep.tile([P, NQ + SHARED, PACK], BF16, name="qkgrp", align_bytes=64)
        krest = keep.tile([P, N - SHARED, PACK], BF16, name="krest", align_bytes=64)
        khigh = krest[:, HALF - SHARED : N - SHARED, :]
        nc.gpsimd.tensor_scalar(khigh[:, :, 0:2], kg1[:, 1:3, :].rearrange("p t n -> p n t"), 1.0, 0.0, ALU.mult, ALU.add)
        nc.gpsimd.tensor_scalar(qkgrp[:, 0:NQ, :], q_sb[:].rearrange("p t q -> p q t"), 1.0, 0.0, ALU.mult, ALU.add)
        nc.gpsimd.tensor_scalar(qkgrp[:, NQ : NQ + SHARED, 0:2], kg0[:, 0:2, 0:SHARED].rearrange("p t n -> p n t"), 1.0, 0.0, ALU.mult, ALU.add)
        newvb = keep.tile([P, NEW], BF16, name="newvb")
        scales = late.tile([P, 2 * PACK], F32, name="scales", offset=6144)
        nc.scalar.copy(scales[:], turned[:, P - 1 : P - 1 + 4 * PACK : 2])
        vst = scales[:, 0:PACK]
        kst = scales[:, PACK : 2 * PACK]

        nc.vector.tensor_copy(kp3[:].indirect(place[:]), newk[1][:, 1, :])
        for h in range(2):
            nc.vector.tensor_copy(runs[h][3], kp3[:].indirect(idx[:, h * HALF // 16 : (h + 1) * HALF // 16]))

        def weave(copy, grouped, planes):
            copy(grouped.rearrange("p (g i) t -> p g t i", i=PACK), planes.rearrange("p t (g i) -> p g t i", i=PACK))

        qkcodes = late.tile([P, NQ + N], U32, name="qkcodes", align_bytes=64, offset=14336)
        qkscale = keep.tile([P, NQ + N], U8, name="qkscale", align_bytes=64)
        aT = late.tile([P, PACK, NQ], F32, name="aT", offset=10240)
        a = psum.tile([P, N], F32, name="a", tag="bank4")
        weave(nc.scalar.copy, qkgrp[:, NQ : NQ + SHARED, 2:PACK], kg0[:, 2:PACK, 0:SHARED])
        vb0 = keep.tile([P, T], BF16, name="vb0")
        nc.scalar.copy(newvb[:], newv[:, 0, :])
        nc.scalar.copy(vb0[:, 0:VCUT], vpart[0][:])
        nc.scalar.copy(vb0[:, VCUT:T], vpart[1][:])
        weave(nc.vector.tensor_copy, krest[:, 0 : HALF - SHARED, :], kg0[:, :, SHARED:HALF])
        weave(nc.vector.tensor_copy, khigh[:, :, 2:PACK], kg1[:, 0:2, :])
        for c in range(PACK):
            cols = slice(c * QUARTER, (c + 1) * QUARTER)
            keys = slice(NQ + c * QUARTER, NQ + (c + 1) * QUARTER)
            made = slice(0 if c == 0 else keys.start, keys.stop)
            nc.vector.quantize_mx(out=qkcodes[:, made].bitcast(FP8X4), scales=qkscale[:, made], in_=(qkgrp[:] if c == 0 else krest[:, (c - 1) * QUARTER : c * QUARTER, :]).rearrange("p n t -> p (n t)"))
            scores = psum.tile([P, NQ], F32, name="scores%d" % c, tag="bank%d" % c)
            nc.tensor.matmul_mx(
                out=scores[:],
                lhsT=qkcodes[:, keys].bitcast(FP8X4),
                lhsT_scale=qkscale[:, keys],
                rhs=qkcodes[:, 0:NQ].bitcast(FP8X4),
                rhs_scale=qkscale[:, 0:NQ],
                start=True,
                stop=True,
            )
            nc.scalar.activation(aT[:, c, :], scores[:], ACT.Copy, scale=kst[:, c : c + 1])
            nc.tensor.transpose(a[:, cols], aT[:, c, :], identf[:])

        nc.vector.tensor_copy(vb0[:].indirect(place[:]), newvb[:])
        nc.vector.tensor_copy(vp1[:].indirect(place[:]), newv[:, 1, :])
        vg0 = keep.tile([P, N], BF16, name="vg0")
        nc.scalar.activation(vg0[:], vb0[:].indirect(idx[:]), ACT.Copy)
        vg1 = late.tile([P, N], BF16, name="vg1", offset=10240)
        vwords = [vg0[:].bitcast(F32)[:, 0 : N // 2 : 2], vg0[:].bitcast(F32)[:, 1 : N // 2 : 2], vg1[:].bitcast(F32)[:, 0:P], vg1[:].bitcast(F32)[:, P : 2 * P]]

        bias = late.tile([P, 1], F32, name="bias", offset=20480)
        nc.vector.tensor_reduce(bias[:], a[:], AX.X, ALU.max, negate=True)
        nc.vector.tensor_copy(vg1[:].rearrange("p (u s e) -> p s u e", u=2, e=2), vp1[:].indirect(idx[:]))
        p = late.tile([P, PACK, P], F32, name="p", offset=22528)
        sums = keep.tile([P, 2], F32, name="sums")
        for h in range(2):
            ts = slice(2 * h, 2 * h + 2)
            nc.scalar.activation(p[:, ts, :], a[:].rearrange("q (s t) -> q t s", t=PACK)[:, ts, :], ACT.Exp, bias=bias[:], scale=1.0, accum_out=sums[:, h : h + 1])

        wgrp = keep.tile([P, NQ, PACK], BF16, name="wgrp", align_bytes=64)
        pps = psum.tile([P, PACK, NQ], F32, name="pps", tag="bank5")
        for t in range(PACK):
            nc.tensor.transpose(pps[:, t, :], p[:, t, :], identf[:])
        nc.vector.tensor_tensor(wgrp[:], pps[:].rearrange("s t q -> s q t"), vst.unsqueeze(1).to_broadcast([P, NQ, PACK]), ALU.mult)

        vgrp = [late.tile([P, P * PACK], BF16, name="vgrp0", align_bytes=64, offset=20480), keep.tile([P, P * PACK], BF16, name="vgrp1", align_bytes=64)]
        vcodes = late.tile([P, DV], U32, name="vcodes", align_bytes=64, offset=22528)
        vscale = keep.tile([P, DV], U8, name="vscale", align_bytes=64)
        wcodes = keep.tile([P, NQ], U32, name="wcodes", align_bytes=64)
        wscale = keep.tile([P, NQ], U8, name="wscale", align_bytes=64)
        for b in range(2):
            vps = psum.tile([P, 2, P], F32, name="vps%d" % b, tag=("bank6", "bank4")[b])
            for u in range(2):
                nc.tensor.transpose(vps[:, u, :], vwords[2 * b + u], identf[:])
            nc.scalar.copy(vgrp[b][:].bitcast(F32).rearrange("s (e u) -> s e u", u=2), vps[:].rearrange("s u e -> s e u"))
            if b == 1:
                nc.vector.quantize_mx(out=wcodes[:].bitcast(FP8X4), scales=wscale[:], in_=wgrp[:].rearrange("p q t -> p (q t)"))
            cols = slice(b * P, (b + 1) * P)
            nc.vector.quantize_mx(out=vcodes[:, cols].bitcast(FP8X4), scales=vscale[:, cols], in_=vgrp[b][:])
        total = keep.tile([P, 1], F32, name="total")
        nc.gpsimd.tensor_tensor(total[:], sums[:, 0:1], sums[:, 1:2], ALU.add)
        recip = keep.tile([P, 1], F32, name="recip")
        nc.vector.reciprocal(recip[:], total[:])
        o_sb = keep.tile([P, DV], F32, name="o_sb")
        for h in range(2):
            cols = slice(h * P, (h + 1) * P)
            ps_out = psum.tile([P, P], F32, name="ps_out%d" % h, tag="bank%d" % h)
            nc.tensor.matmul_mx(
                out=ps_out[:],
                lhsT=wcodes[:].bitcast(FP8X4),
                lhsT_scale=wscale[:],
                rhs=vcodes[:, cols].bitcast(FP8X4),
                rhs_scale=vscale[:, cols],
                start=True,
                stop=True,
            )
            if h == 0:
                nc.scalar.activation(o_sb[:, cols], ps_out[:], ACT.Copy, scale=recip[:])
            else:
                nc.vector.tensor_scalar(o_sb[:, cols], ps_out[:], recip[:], None, ALU.mult)
            nc.sync.dma_start(out[0][:, cols], o_sb[:, cols])
